import numpy as np, ml_dtypes
CORES = [10,34,74,98]
N = 4
BF = ml_dtypes.bfloat16
W, P, Q, C, R, EV = 4096, 15, 256, 64, 3, 2048
def spots(e, w):
    a = np.sum(w[..., 0:1] * e, axis=-2) & 4095; b = np.sum(w[..., 1:2] * e, axis=-2) & 4095; m = a * b
    return ((m >> 5) + b) & (W - 1), ((m >> 9) + a) & (W - 1), (m >> 7) & (EV - 1)
def lattice():
    i = np.stack(np.meshgrid(*[np.arange(17)] * 4, indexing="ij"), -1).reshape(-1, 4)
    i = i[np.all(i[:, 1:] >= i[:, :-1], axis=1)]; v = np.zeros((len(i), 17), np.int64)
    np.add.at(v, (np.arange(len(i))[:, None], i), 1)
    return np.concatenate([v[:, :16], (np.arange(5, 201)[:, None, None] * np.eye(16, dtype=np.int64)).reshape(-1, 16)])
LST = lattice()
def place(e, w):
    h1, h2, z = spots(e.T, w); odd = (z & 1) == 1; at = np.full(len(e), -1, np.int64); used = np.zeros(W, bool)
    for h in (np.where(odd, h2, h1), np.where(odd, h1, h2)):
        o = np.flatnonzero((at < 0) & ~used[h]); i = o[np.unique(h[o], return_index=True)[1]]
        at[i] = h[i]; used[h[i]] = True
    return at
def seat(rng, e):
    for i in range(50):
        w = rng.integers(1, 4096, (16, 2))
        if np.min(place(e, w)) >= 0: break
    return w
def tab(rng, a, n, act, far):
    e = LST[np.argsort(np.dot(LST, a))[:n]]; x = rng.integers(0, 201, (far, 16)); t = rng.permutation(far)
    x[:, 0] = rng.integers(100, 201, far); x[:, 1] = t % 200; x[:, 2] = t // 200; x[:, 3] = np.maximum(x[:, 3], 1)
    k = np.full(n + far, 2, np.int64); lo = n - max(act, n // 3); k[lo + rng.permutation(n - lo)[:act]] = 1
    k[n:] = 1 + (rng.random(far) < 0.5)
    sz = np.concatenate([rng.integers(64, 257, n), rng.integers(8, 33, far)])
    return np.concatenate([e, x]), k, (sz[:, None] * rng.random((n + far, 16))).astype(np.int64)
def plain(rng, r, a, young):
    a = a * (1 + 0.02 * rng.random(16))
    if young: return tab(rng, a, 17, 16, 2 * Q)
    return tab(rng, a, W // 3 - r * (W // 64) + int(rng.integers(0, W // 128)), W // 34, W // 10)
def pack(rng, w, items, nq, th, env=None, stray=0.0):
    ex = np.full((N, 8, 16, W), -1, np.int32); su = np.zeros((N, 8, 16, W), np.int32); st = np.zeros((N, 8, W), np.int32); qu = np.full((N, 8, Q), -1, np.int32)
    for r in range(N):
        for g in range(8):
            e, k, s, *out = items[r][g]; out = out[0] if out else rng.random(len(e)) < stray
            at = place(e, w[r, g]); i = np.flatnonzero(at >= 0); p = at[i]
            if np.any(out):
                h1, h2, z = spots(e.T, w[r, g]); free = rng.permutation(np.setdiff1d(np.arange(W), p))
                j = np.flatnonzero(out[i])[:len(free)]; to = free[:len(j)]
                away = (to != h1[i[j]]) & (to != h2[i[j]]); p[j[away]] = to[away]
            ex[r, g][:, p] = e[i].T; su[r, g][:, p] = s[i].T; st[r, g, p] = k[i]
            o = rng.permutation(p[k[i] == 1][:int(nq[r, g])]); qu[r, g, :len(o)] = o
    if env is None: env = rng.integers(0, 256, (N, 128, EV))
    return {"ex": ex.reshape(N, 128, W).astype(np.float32).astype(BF), "su": su.reshape(N, 128, W).astype(np.float32).astype(BF), "st": st, "qu": qu,
            "wt": np.ascontiguousarray(w.reshape(N, 128, 2)).astype(np.int32), "env": env.astype(np.float32).astype(BF), "th": np.ascontiguousarray(th.reshape(N, 8, 1)).astype(np.int32)}
def parts(rng):
    w = rng.integers(1, 4096, (N, 8, 16, 2)); a = 1 + 0.9 * rng.random((8, 16)); th = rng.integers(150, 700, (N, 8))
    y = (int(rng.integers(0, 8)) + 3 * np.arange(N)) % 8
    items = [[plain(rng, r, a[g], g == y[r]) for g in range(8)] for r in range(N)]
    nq = rng.integers(Q // 2, Q + 1, (N, 8))
    for r in range(N): nq[r, y[r]] = Q; nq[r, (y[r] + 4) % 8] = rng.integers(0, P)
    return w, a, th, items, nq
def setup_inputs(rng):
    w, a, th, items, nq = parts(rng)
    return pack(rng, w, items, nq, th)
def exact(rng, want):
    m = 1
    while m * m < want: m += 1
    x = m * m - want; o = rng.permutation(16); o[:m] = np.sort(o[:m]); one = np.eye(16, dtype=np.int64)[o]
    pairs = np.array([(i, j) for i in range(m) for j in range(i)], np.int64).reshape(-1, 2); pairs = pairs[rng.permutation(len(pairs))[:x // 2]]
    e = np.concatenate([np.zeros((1, 16), np.int64), one, one[pairs[:, 0]] + one[pairs[:, 1]], 2 * one[:x % 2]])
    k = np.full(len(e), 2, np.int64); k[1:17] = 1; s = np.zeros((len(e), 16), np.int64)
    s[0] = rng.integers(0, 256, 16); s[1:m] = rng.integers(129, 256, (m - 1, 16)); s[m] = 128
    return (e, k, s), seat(rng, e)
def setup_inputs_room(rng):
    w, a, th, items, nq = parts(rng); a = 1 + 0.01 * rng.random((8, 16))
    for r in range(N):
        for g in range(8):
            items[r][g] = plain(rng, r, a[g], r % 2 == 1 and g in (3, 6)); nq[r, g] = Q
            if r % 2 == 1 and g in (0, 1, 2, 4):
                items[r][g], w[r, g] = exact(rng, {0: C, 1: C + 1, 2: C - 1, 4: 1}[g]); th[r, g] = 1000
            if r % 2 == 1 and g in (3, 6): th[r, g] = 200
            if r % 2 == 0 and g == 6:
                e, k, s = items[r][g]; two = rng.permutation(np.flatnonzero(np.sum(e, axis=1) == 2))[:P + 4]
                k[two] = 1; s[two] = 255
    return pack(rng, w, items, nq, th)
def setup_inputs_ties(rng):
    w, a, th, items, nq = parts(rng); th = rng.choice(np.array([512, 512, 513, 1024]), (N, 8))
    for r in range(N):
        for g in range(8):
            e, k, s = items[r][g]; v = rng.choice(np.array([32, 64, 64]), (len(e), 1))
            items[r][g] = e, k, np.tile(v, (1, 16))
    e = np.concatenate([np.zeros((1, 16), np.int64), np.eye(16, dtype=np.int64)]); k = np.full(17, 1, np.int64); k[0] = 2
    items[0][0] = e, k, np.full((17, 16), 64, np.int64); w[0, 0] = seat(rng, e); nq[0, 0] = Q; th[0, 0] = 1024
    return pack(rng, w, items, nq, th, 128 * rng.integers(0, 2, (N, 128, EV)))
def forge(rng):
    b = np.concatenate([np.array([5, 5]), rng.integers(2, 121, 2), np.array([5]), rng.integers(2, 121, 3)])
    n = np.arange(8); u = 2 * n + (n > 3); v = 4 * n + 1 - u; one = np.eye(16, dtype=np.int64); es = []; ks = []
    for j in range(11):
        p = j if j < 8 else (0, 1, int(rng.integers(2, 8)))[j - 8]
        x = (2 * p + 2 + int(rng.integers(0, 14))) % 16; y = np.zeros(16, np.int64)
        y[u[p]] = rng.integers(2, 61); y[v[p]] = rng.integers(4, 61); y[x] = 10 * j + 5 + rng.integers(0, 4)
        near = y - one[np.array([u[p], v[p], x])]; more = b[p] * one[u[p]] - one[v[p]]
        if j < 8: near[2] = near[2] + more
        else: near = np.concatenate([near, (y + more)[None]])
        k = np.full(len(near), 2, np.int64); k[0] = 1; es.append(near); ks.append(k)
    return np.concatenate(es), np.concatenate(ks), b, u, v
def setup_inputs_clash(rng):
    w, a, th, items, nq = parts(rng); th = rng.integers(100, 300, (N, 8))
    for r in range(N):
        for g in range(8): items[r][g] = plain(rng, r, a[g], r % 2 == 1 and 1 <= g <= 4); nq[r, g] = Q
        if r % 2 == 1:
            w[r, 1, :, 0] = 0; w[r, 2, :, 1] = w[r, 2, :, 0]; w[r, 3, :, 1] = 0; w[r, 4, 1::2] = w[r, 4, ::2]
            few = rng.choice(np.array([0, 1, 2, 64, 2048, 4095]), (3, 16, 2)); w[r, 5:] = np.where(rng.random((3, 16, 2)) < 0.5, few, w[r, 5:])
    e, k, b, u, v = forge(rng)
    for r in range(N):
        w[r, 0, v] = (b[:, None] * w[r, 0, u]) & 4095; items[r][0] = e, k, rng.integers(100, 256, (len(e), 16))
    return pack(rng, w, items, nq, th)
def dense(rng, n):
    y = rng.integers(100, 201, (n, 16)); y[1::2] = rng.integers(1, 4, y[1::2].shape); y[:, 0] = 100 + 3 * rng.permutation(33)[:n]
    return y
def kin(rng, y, j):
    s = 80 + 8 * np.arange(16)[:, None] + rng.integers(0, 56, (16, 16))
    return y - np.eye(16, dtype=np.int64), np.full(16, 2, np.int64), s[::-1] if j % 2 == 0 else s, np.zeros(16, bool)
def nest(l, w):
    e, k, s, out = [np.concatenate(v) for v in zip(*l)]
    if np.any(e[0] != 0):
        h1, h2, z = spots(e.T, w); i = (h1 > 0) & (h2 > 0); e, k, s, out = e[i], k[i], s[i], out[i]
    return e, k, s, out
def setup_inputs_short(rng):
    w, a, th, items, nq = parts(rng); nq = rng.choice(np.array([0, 1, P - 1, P, P + 1, Q]), (N, 8))
    nq[0] = np.array([0, 1, P - 1, P, P + 1, 1, Q, Q]); nq[1, 0] = Q; nq[N - 1] = 0; nq[::2, 5] = 1; nq[:N - 1, 6] = Q; nq[:, 7] = Q
    th[:, 5] = 100; th[:, 6:] = rng.integers(50, 300, (N, 2))
    y = dense(rng, 6); b = dense(rng, 4 * N).reshape(N, 4, 16)
    for r in range(N):
        if r % 2 == 1: items[r][5] = tab(rng, a[5], 0, 0, 0)
        else: items[r][5] = np.zeros((1, 16), np.int64), np.ones(1, np.int64), rng.integers(64, 256, (1, 16))
        z = [(np.zeros((1, 16), np.int64), np.full(1, 2, np.int64), rng.integers(200, 256, (1, 16)), np.zeros(1, bool))] if r % 2 == 0 else []
        l = []
        for j in range(6):
            e, k, s, out = kin(rng, y[j], j); k[int(rng.integers(0, 16 if j < 4 else 7))] = 1
            i = np.flatnonzero(np.arange(16) != {4: 15, 5: 7}.get(j, 16)); l.append((e[i], k[i], s[i], out[i]))
        items[r][6] = nest(z + l, w[r, 6])
        l = [(b[r], np.ones(4, np.int64), rng.integers(150, 256, (4, 16)), np.arange(4) == 1)] + [kin(rng, b[r - 1, j], j) for j in range(4)]
        l.append((b[r - 1, 2:3], np.full(1, 2, np.int64), rng.integers(64, 256, (1, 16)), np.zeros(1, bool)))
        items[r][7] = nest(z + l, w[r, 7])
    return pack(rng, w, items, nq, th)
def setup_inputs_spread(rng):
    w, a, th, items, nq = parts(rng); w = rng.integers(0, 4096, (N, 8, 16, 2)); w[:, :, 3] = 4095
    a = np.exp2(-2 + 3 * rng.random((8, 16))); a[0, 0] = 0.001
    th = np.minimum(np.exp2(12 * rng.random((N, 8))).astype(np.int64), 4080)
    for r in range(N):
        for g in range(8):
            if r % 2 == 1 and g == 6: continue
            e, k, s = plain(rng, r, a[g], False); s = (np.exp2(3 + 5 * rng.random((len(e), 1))) * rng.random(s.shape) ** 0.5).astype(np.int64)
            i = (e[:, 0] == 200) & (np.sum(e, axis=1) == 200); k[i] = 1; s[i] = 255
            items[r][g] = e, k, s
    nq[:] = Q
    env = (np.exp2(8 * rng.random((N, 1, EV))) * rng.random((N, 128, EV))).astype(np.int64)
    return pack(rng, w, items, nq, th, env, 0.125)
def check_inputs(d):
    bad = []; x = d["ex"].astype(np.float32).reshape(N, 8, 16, W); s = d["su"].astype(np.float32).reshape(N, 8, 16, W); v = d["env"].astype(np.float32); t = d["st"]; q = d["qu"]; free = t == 0
    if np.min(t) < 0 or np.max(t) > 2: bad.append("range of st")
    if np.any(x != np.floor(x)) or np.max(x) > 200 or np.any(np.where(free[:, :, None], x != -1, x < 0)): bad.append("ex: whole numbers from 0 to 200, -1 in free places")
    if np.any(s != np.floor(s)) or np.min(s) < 0 or np.max(s) > 255 or np.any(free[:, :, None] & (s != 0)): bad.append("su: whole numbers from 0 to 255, 0 in free places")
    if np.any(v != np.floor(v)) or np.min(v) < 0 or np.max(v) > 255: bad.append("env: whole numbers from 0 to 255")
    if np.min(d["wt"]) < 0 or np.max(d["wt"]) > 4095: bad.append("range of wt")
    if np.min(d["th"]) < 1 or np.max(d["th"]) > 4080: bad.append("range of th")
    z = np.sort(q, axis=-1)
    if np.min(q) < -1 or np.max(q) >= W: bad.append("range of qu")
    if np.any((q[..., 1:] >= 0) & (q[..., :-1] < 0)): bad.append("qu: an entry behind -1")
    if np.any((q >= 0) & (np.take_along_axis(t, np.clip(q, 0, W - 1), 2) != 1)): bad.append("qu: a place that is not active")
    if np.any((z[..., 1:] == z[..., :-1]) & (z[..., 1:] >= 0)): bad.append("qu: a place twice")
    for a in range(N):
        for g in range(8):
            y = np.ascontiguousarray(x[a, g][:, ~free[a, g]].T)
            if len(y) and len(np.unique(y, axis=0)) < len(y): bad.append("ex: an index twice on rank " + str(a) + " in group " + str(g))
    return bad
def pick(t, h):
    return np.take_along_axis(t, h[:, None, :], 2)
def look(e, E, V, w):
    h1, h2, z = spots(e, w)
    f1 = np.all(pick(E, h1) == e, axis=1); f2 = np.all(pick(E, h2) == e, axis=1)
    return f1 | f2, np.where(f1[:, None], pick(V, h1), np.where(f2[:, None], pick(V, h2), 0))
def reference(ex, su, st, qu, wt, env, th):
    E = ex.astype(np.float32).astype(np.int32).reshape(N, 8, 16, W); S = su.astype(np.float32).astype(np.int32).reshape(N, 8, 16, W)
    T = st.astype(np.int32); q = qu.astype(np.int32); w = wt.astype(np.int32).reshape(N, 8, 16, 2)
    V = env.astype(np.float32).astype(np.int32).reshape(N, 8, 16, EV); t = th.astype(np.int32).reshape(N, 8, 1); one = np.eye(16, dtype=np.int32)
    for rnd in range(R):
        par = np.full((N, 8, 16, P), -1, np.int32); live = np.zeros((N, 8, P), bool)
        for a in range(N):
            s = np.where(q[a] >= 0, np.sum(pick(S[a], np.maximum(q[a], 0)), axis=1), -1)
            z = np.take_along_axis(q[a], np.argsort(-s, axis=1, kind="stable"), 1)
            live[a] = z[:, :P] >= 0; par[a] = np.where(live[a][:, None], pick(E[a], np.maximum(z[:, :P], 0)), -1)
            for g in range(8): T[a, g, z[g, :P][live[a, g]]] = 2
            q[a] = np.concatenate([z[:, P:], np.full((8, P), -1, np.int32)], axis=1)
        old = np.where(T[:, :, None, :] == 2, S, 0)
        for a in range(N):
            own = (par[a][:, :, :, None] + one[None, :, None, :]).reshape(8, 16, 16 * P)
            c = np.concatenate([own, par[a - 1] if a else np.full_like(par[0], -1)], axis=2)
            ok = np.concatenate([np.repeat(live[a], 16, axis=1), live[a - 1] if a else np.zeros_like(live[0])], axis=1)
            c = np.where(ok[:, None], c, 0)
            v = look((c[:, :, :, None] - one[None, :, None, :]).reshape(8, 16, -1), E[a], old[a], w[a])[1].reshape(8, 16, -1, 16)
            M = np.min(np.where((np.swapaxes(c, 1, 2) == 0)[:, None], 255, v), axis=3)
            good = ok & ~look(c, E[a], old[a], w[a])[0] & (np.sum(M, axis=1) >= t[a])
            good = good & (np.add.accumulate(good.astype(np.int32), axis=1) <= C)
            if a: M = np.minimum(M, look(c, E[a - 1], old[a - 1], w[a - 1])[1])
            h1, h2, z = spots(c, w[a])
            f1 = np.take_along_axis(T[a], h1, 1) == 0; f2 = np.take_along_axis(T[a], h2, 1) == 0
            to = np.where(f1, h1, np.where(f2, h2, -1)); good = good & (np.sum(M, axis=1) >= t[a]) & (to >= 0)
            new = np.abs(M - pick(V[a], z))
            for g in range(8):
                j = np.flatnonzero(good[g]); j = j[np.sort(np.unique(to[g, j], return_index=True)[1])]; p = to[g, j]
                E[a, g][:, p] = c[g][:, j]; S[a, g][:, p] = new[g][:, j]; T[a, g, p] = 1
                n = int(np.sum(q[a, g] >= 0)); m = min(len(j), Q - n); q[a, g, n:n + m] = p[:m]
    return {"ys": S.reshape(N, 128, W).astype(np.float32).astype(BF), "yst": T.astype(np.float32)}

@@ -1,0 +1,618 @@
+from concourse.bass import DstId, RemoteDMATransfer
+from concourse.mybir import AluOpType as Op, AxisListType, ActivationFunctionType as Fn
+
+W, EV, R = 4096, 2048, 3
+HC = [(0, 4), (4, 15)]
+SC = [(0, 4), (4, 8), (8, 12), (12, 15)]
+ON_A = {0: 32, 1: 32, 2: 48, 3: 24}
+XC = 480
+MUL, OFF, PEN = 32768.0, 9437184.0, 16384.0
+NEUTRAL, ZERO = 4176, 4177
+CY, GA, SCA, PE, HOP, FAR = 1.04, 1.56, 3.8, 0.6, 100.0, 3600.0
+B, F, I, U = "bfloat16", "float32", "int32", "uint16"
+_SB = {
+    "E": (4176, B), "S": (4432, B), "ENV": (EV, B), "PLC": (4192, F), "ST": (4176, F),
+    "qi": (16, I), "qo": (16, U), "wi": (2, I), "wf": (8, F), "wj": (4, I), "thi": (8, I), "thb": (8, I), "thf": (8, F), "thc": (2, F),
+    "ec": (256, B), "sti": (256, I), "f1": (256, F), "f2": (256, F), "fx": (256, B), "yc": (256, F),
+    "pi": (4, I), "pc": (16, F), "qg": (128, F), "qq": (256, F), "jm": (256, F), "ri": (32, I), "rj": (32, I), "wt16": (32, F),
+    "BO": (128, B), "ID": (128, B), "IDF": (128, F), "I8": (128, B), "In22": (128, B), "In1": (128, B), "BO1k": (128, B),
+    "BOz": (128, B), "BOh": (128, B), "LD": (128, B), "DG": (128, B), "WB": (512, B), "D16": (256, B), "LK": (2048, B),
+    "tg": (16, F), "ti": (48, I), "TGh": (256, B), "TGl": (256, B),
+    "EXi": (16, I), "EX": (16, U), "RM": (1536, B), "RZ": (256, B), "ONE": (256, B), "JT": (96, B), "JT1": (256, B), "K2": (256, B),
+    "OD": (32, B), "thr": (64, F), "qt": (64, F), "tr": (64, F), "mA": (64, F), "FX": (96, F), "G8": (8, F),
+    "X": (48 * R, B), "RP": (256 * R, B), "SV": (256 * R, B), "b8": (16, F), "C": (272, B), "CU": (256, B), "YE": (256, B), "NZ": (256, F),
+    "AB": (576, I), "MM": (288, I), "SS": (576, I), "HU": (576, U), "zi": (16, I), "zu": (16, U),
+    "FF": (7680, B), "FD": (1536, B), "mh": (288, F), "sl": (256, F), "SU": (256, U), "su2": (16, U), "G2": (4096, B), "MS": (4096, B),
+    "sq": (512, B), "sg": (512, B), "ta": (16, F), "tu": (16, U), "t256": (256, F), "tp": (272, F),
+    "EVg": (256, B), "M5": (256, B), "D": (272, B), "good": (256, B), "pre": (256, B), "junk": (1024, B), "acc": (4, F), "ix": (4, U),
+    "tB": (64, F), "tm": (64, F), "tA": (64, F), "eq": (256, B), "nd": (64, F), "so": (4, U), "Ce": (64, B),
+    "PS": (256, B), "PB": (256, F), "nb": (64, B), "qc": (64, F), "ov": (64, B), "rm": (4, F), "KB": (256, F), "KA": (256, F), "cm": (4096, B),
+    "pl": (4, F), "po": (2, U), "zs": (512, F), "vo": (2, U),
+}
+SCRATCH = {k: ("sbuf", [128, n], d) for k, (n, d) in _SB.items()}
+for _k in range(8):
+    SCRATCH["p%d" % _k] = ("psum", [128, 512], F)
+SEMAPHORES = ["V", "A", "P", "G"] + ["d%d" % k for k in range(24)] + [a + str(r) for a in ("lo", "up", "rp", "ls", "lr") for r in range(R)]
+
+
+def rank_program(g, core, T, topo):
+    rank = T.rank_of(core)
+    if rank is None:
+        return
+    below = T.cores[rank - 1] if rank > 0 else None
+    above = T.cores[rank + 1] if rank + 1 < len(T.cores) else None
+    Q = {"V": g.vector, "A": g.scalar, "P": g.tensor, "G": g, "Y": g.sync}
+    ops, hist, bank, lastq, soft, line = [], {}, {}, {}, [], {}
+
+    def c(name, lo=0, hi=None, step=1, rows=None):
+        where, shape, dt = SCRATCH[name]
+        hi = shape[1] if hi is None else hi
+        ps = slice(0, 128) if rows is None else rows
+        return (T[name][ps, lo:hi:step] if step != 1 else T[name][ps, lo:hi], [(name, lo, hi)], [], len(range(lo, hi, step)), dt in (B, U), where == "psum", False)
+
+    def ind(win, off):
+        return (win[0].indirect(off[0]), win[1], off[1], 16 * off[3], win[4], False, True)
+
+    def emit(eng, outs, ins, call, dur, sem=None, inc=1, chain=True, after=(), lat=0.0, size=0, skip=()):
+        k = len(ops)
+        wr = [x for o in outs for x in o[1]]
+        rd = [x for o in outs for x in o[2]] + [x for o in ins if isinstance(o, tuple) for x in o[1] + o[2]]
+        deps, order = set(), set(after)
+        for is_wr, acc in ((True, wr), (False, rd)):
+            for (n, lo, hi) in acc:
+                if SCRATCH[n][0] == "psum":
+                    st = bank.setdefault(n, [eng, [], []])
+                    if st[0] != eng:
+                        st[:] = [eng, [], st[1]]
+                    deps.update(st[2])
+                    if eng == "P":
+                        order.update(st[1][-1:])
+                    if k not in st[1]:
+                        st[1].append(k)
+                    if eng == "P":
+                        continue
+                for (a, b, w, j) in hist.get(n, []):
+                    if a < hi and lo < b and (w or is_wr) and j not in skip:
+                        deps.add(j)
+        for (n, lo, hi) in rd:
+            hist.setdefault(n, []).append((lo, hi, False, k))
+        for (n, lo, hi) in wr:
+            h = hist.setdefault(n, [])
+            h[:] = [x for x in h if x[3] in skip or not (lo <= x[0] and x[1] <= hi)] + [(lo, hi, True, k)]
+        deps.discard(k)
+        order.discard(k)
+        if size and eng in lastq:
+            order.add(lastq[eng])
+        if size:
+            lastq[eng] = k
+        ops.append(dict(eng=eng, deps=deps, order=order, call=call, dur=dur, sem=sem or eng, inc=inc, chain=chain, lat=lat, size=size))
+        return k
+
+    def issue():
+        n = len(ops)
+        succ, more = [[] for _ in ops], [[] for _ in ops]
+        for k, o in enumerate(ops):
+            for j in o["deps"] | o["order"]:
+                succ[j].append(k)
+        for a, b in soft:
+            more[a].append(b)
+        prio = [0.0] * n
+        for k in range(n - 1, -1, -1):
+            o = ops[k]
+            prio[k] = o["dur"] + o["lat"] + o["size"] / 200.0 + max([prio[j] + HOP for j in succ[k]] + [prio[j] for j in more[k]], default=0.0)
+        left = [len(o["deps"] | o["order"]) for o in ops]
+        start, done, free, seq, wire = [0.0] * n, [0.0] * n, {e: 0.0 for e in list(Q) + [None]}, {e: [] for e in Q}, [0.0]
+        ready = {k: 0.0 for k in range(n) if left[k] == 0}
+        while ready:
+            at = {k: max(t, free[ops[k]["eng"]]) for k, t in ready.items()}
+            e = ops[min(at, key=lambda k: (at[k], -prio[k]))]["eng"]
+            mine = [k for k in at if ops[k]["eng"] == e]
+            t0 = min(at[k] for k in mine)
+            k = max((j for j in mine if at[j] <= t0 + HOP), key=lambda j: (prio[j], -j))
+            o = ops[k]
+            del ready[k]
+            start[k] = at[k]
+            done[k] = at[k] + o["dur"] + o["lat"]
+            if o["size"]:
+                wire[0] = max(wire[0], at[k] + 1000.0) + o["size"] / 200.0
+                done[k] = wire[0] + 1000.0
+            if e is not None:
+                free[e] = at[k] + o["dur"]
+                seq[e].append(k)
+            for j in succ[k]:
+                left[j] -= 1
+                if left[j] == 0:
+                    ready[j] = max([done[i] + HOP for i in ops[j]["deps"]] + [done[i] if ops[j]["eng"] is None else start[i] for i in ops[j]["order"]])
+        top, val = {}, {}
+        for k in [k for e in Q for k in seq[e]] + [k for k in range(n) if ops[k]["eng"] is None]:
+            top[ops[k]["sem"]] = val[k] = top.get(ops[k]["sem"], 0) + ops[k]["inc"]
+        for e in Q:
+            seen = {}
+            for k in seq[e]:
+                want = {}
+                for j in ops[k]["deps"]:
+                    s = ops[j]["sem"]
+                    if seen.get(s, 0) < val[j] and not e == s == "P":
+                        want[s] = max(want.get(s, 0), val[j])
+                for s, v in sorted(want.items()):
+                    Q[e].wait_ge(T.sem[s], v)
+                    seen[s] = v
+                r = ops[k]["call"]()
+                if ops[k]["chain"]:
+                    r.then_inc(T.sem[ops[k]["sem"]], ops[k]["inc"])
+        for s, v in sorted(top.items()):
+            g.wait_ge(T.sem[s], v)
+
+    def follow(key):
+        if key in line:
+            soft.append((line[key], len(ops) - 1))
+        line[key] = len(ops) - 1
+
+    def ap(x):
+        return x[0] if isinstance(x, tuple) else x
+
+    def cost(o, i, per, fix=50.0):
+        if o[6] or i[6]:
+            return fix + CY * (o[3] * SCA if o[6] else i[3] * GA)
+        return CY * max(64.0, i[3] * per)
+
+    def half(*xs):
+        return 0.5 if all(x[4] for x in xs) else 1.0
+
+    def ts(o, i, s1, op0, s2=None, op1=None):
+        if op1 is None:
+            emit("V", [o], [i, s1], lambda: g.vector.tensor_scalar(o[0], i[0], ap(s1), None, op0), cost(o, i, half(o, i)))
+        else:
+            emit("V", [o], [i, s1, s2], lambda: g.vector.tensor_scalar(o[0], i[0], ap(s1), ap(s2), op0, op1), cost(o, i, half(o, i)))
+
+    def tt(o, a, b, op):
+        emit("V", [o], [a, b], lambda: g.vector.tensor_tensor(o[0], a[0], b[0], op), cost(o, a, 1.0 if a[5] or b[5] else 2.0))
+
+    def cp(o, i):
+        emit("V", [o], [i], lambda: g.vector.tensor_copy(o[0], i[0]), cost(o, i, half(o, i)))
+
+    def ms(o, v):
+        emit("V", [o], [], lambda: g.vector.memset(o[0], v), cost(o, o, half(o)))
+
+    def red(o, i, op, ab=False):
+        emit("V", [o], [i], lambda: g.vector.tensor_reduce(o[0], i[0], AxisListType.X, op, apply_absolute_value=ab), cost(o, i, 1.0))
+
+    def scan(o, d0, d1, init, op0, op1):
+        emit("V", [o], [d0, d1, init], lambda: g.vector.tensor_tensor_scan(o[0], d0[0], d1[0], ap(init), op0, op1), cost(o, d0, half(o, d0, d1)))
+
+    def act(o, i, fn, bias=0.0, scale=1.0, accum=None):
+        emit("A", [o] + ([accum] if accum else []), [i, bias, scale],
+             lambda: g.scalar.activation(o[0], i[0], fn, bias=ap(bias), scale=ap(scale), accum_out=ap(accum)), cost(o, i, 1.0, 65.0))
+
+    def mm(o, l, r, start, stop):
+        emit("P", [o], [l, r], lambda: g.tensor.matmul(o[0], l[0], r[0], start, stop), PE * max(64, r[3]) * (1 if r[4] else 4))
+
+    def mms(parts):
+        for k, (o, l, r) in enumerate(parts):
+            mm(o, l, r, k == 0, k == len(parts) - 1)
+
+    def iota(o, pat, base, cm):
+        if SCRATCH[o[1][0][0]][2] == I:
+            emit("G", [o], [], lambda: g.iota(o[0], pat, base, cm), 130 + 2 * CY * o[3])
+        else:
+            emit("G", [o], [], lambda: g.iota(o[0], pat, base, cm, allow_small_or_imprecise_dtypes=True), 130 + 2 * CY * o[3])
+
+    n_dma = [0]
+
+    def dma(eng, o, i, size, skip=()):
+        n_dma[0] += 1
+        return emit(eng, [o] if isinstance(o, tuple) else [], [i], lambda: Q[eng].dma_start(ap(o), ap(i)), 100.0,
+                    sem="d%d" % (n_dma[0] - 1), inc=16, size=size, skip=skip)
+
+    def mask_of(es):
+        return sum(1 << e for e in es)
+
+    def halves(src, dst, k):
+        es = topo.engines(src, dst)
+        return es[:len(es) // 2] if k == 0 else es[len(es) // 2:]
+
+    def landed(o, sem, n, after, lat):
+        emit(None, [o], [], None, 0.0, sem=sem, inc=n, after=[after], lat=lat)
+
+    def dst_id(dst):
+        rid, pid, _ = topo.addr(dst)
+        return DstId(rid=rid, pnc=pid)
+
+    row0 = slice(0, 128, 16)
+    dma("Y", c("qi"), T.qu[:], 8192)
+    dma("Y", c("S", 0, W), T.su[:], 1 << 20)
+    dma("A", c("wi"), T.wt[:], 1024)
+    dma("A", c("thi", rows=slice(0, 1)), T.th[:], 32)
+    dma("Y", c("ec"), T.ex[row0, :], 1 << 16)
+    dma("Y", c("sti"), T.st[:], 1 << 17)
+    parts_e = []
+    for k in range(8):
+        rows = slice(16 * k + 1, 16 * k + 16)
+        parts_e.append(dma("Y", c("E", 0, W, rows=rows), T.ex[rows, :], 15 << 13, skip=list(parts_e)))
+    iota(c("pi", 0, 1), [[0, 1]], 0, 1)
+    iota(c("qq"), [[1, 256]], 0, 0)
+    iota(c("jm"), [[0, 16], [1, 16]], 0, 0)
+    iota(c("qg"), [[1, 8], [0, 16]], 0, 0)
+    iota(c("JT1"), [[-2, 16], [-32, 16]], 0, 0)
+    iota(c("EXi"), [[1, 16]], 0, 0)
+    iota(c("ri", 0, 16), [[-1, 16]], 16, 1)
+    iota(c("ri", 16, 32), [[1, 16]], 128, -1)
+    act(c("PLC", 0, 256), c("qq"), Fn.Copy)
+    for k in (256, 512, 1024, 2048):
+        act(c("PLC", k, 2 * k), c("PLC", 0, k), Fn.Identity, bias=float(k))
+    act(c("PLC", W, 4192), c("PLC", 0, 96), Fn.Identity, bias=float(W))
+    ms(c("S", W, W + 16), -1.0)
+    ms(c("S", W + 16, ZERO), 255.0)
+    ms(c("S", ZERO, 4432), 0.0)
+    ms(c("E", W, 4176), 240.0)
+    ms(c("RZ"), 1.0)
+    ms(c("ONE"), 1.0)
+    ms(c("RZ", 0, 256, 16), 0.0)
+    ts(c("pi", 1, 2), c("pi", 0, 1), 15, Op.bitwise_and)
+    ts(c("pi", 2, 3), c("pi", 0, 1), 4, Op.arith_shift_right)
+    cp(c("pc", 0, 3), c("pi", 0, 3))
+    pcol, lcol, gcol = c("pc", 0, 1), c("pc", 1, 2), c("pc", 2, 3)
+    ts(c("BO1k"), c("qg"), gcol, Op.is_equal, 1024.0, Op.mult)
+    ts(c("ID"), c("qq", 0, 128), pcol, Op.is_equal)
+    ts(c("D16"), c("jm"), lcol, Op.is_equal)
+    ts(c("qi"), c("qi"), 8191, Op.bitwise_and)
+    ts(c("qo"), c("qi"), 4111.0, Op.min)
+    ts(c("K2"), c("D16"), OFF + 2.0 ** 24, Op.mult, -2.0 ** 24, Op.add)
+    ts(c("BOz"), c("BO1k"), MUL / 1024, Op.mult)
+    ts(c("BOh"), c("BO1k"), MUL / 2048, Op.mult)
+    ts(c("IDF"), c("qq", 0, 128), pcol, Op.is_equal)
+    ts(c("pc", 3, 4), lcol, 15.0, Op.is_equal, 305.0, Op.mult)
+    tt(c("pc", 3, 4), c("pc", 3, 4), lcol, Op.add)
+    ts(c("DG"), c("ID"), c("pc", 3, 4), Op.mult, -MUL, Op.mult)
+    ts(c("pc", 5, 6), lcol, 0.0, Op.is_equal, -2.0, Op.mult)
+    ts(c("pc", 4, 5), c("pc", 5, 6), 1.0, Op.add)
+    ts(c("pc", 6, 7), lcol, 4096.0, Op.add)
+    sgn, off = c("pc", 4, 5), c("pc", 5, 6)
+    ts(c("f1"), c("sti"), 1.0, Op.is_equal, -2.0, Op.mult)
+    ts(c("p3", 0, 256), c("ec"), 1.0, Op.add)
+    tt(c("p3", 0, 256), c("p3", 0, 256), c("f1"), Op.mult)
+    tt(c("fx"), c("p3", 0, 256), c("ec"), Op.add)
+    dma("Y", c("E", 0, W, rows=row0), c("fx"), 1 << 16, skip=parts_e)
+    dma("Y", c("ENV"), T.env[:], 1 << 19)
+    cp(c("EX"), c("EXi"))
+    ts(c("BO"), c("BO1k"), 1.0 / 1024, Op.mult)
+    ts(c("wj", 0, 2), c("wi"), 4032, Op.bitwise_and)
+    ts(c("wj", 2, 4), c("wi"), 63, Op.bitwise_and)
+    cp(c("wf", 0, 4), c("wj"))
+    cp(c("wf", 4, 6), c("wi"))
+    ts(c("wf", 6, 8), c("wi"), -1.0, Op.mult)
+    for k in range(4):
+        ts(c("WB", 128 * k, 128 * k + 128), c("BO"), c("wf", k, k + 1), Op.mult)
+    ts(c("ri"), c("ri"), 15, Op.bitwise_and)
+    ts(c("rj"), c("ri"), 3.0, Op.add)
+    ts(c("rj"), c("rj"), 2, Op.arith_shift_right)
+    tt(c("rj"), c("rj"), c("ri"), Op.add)
+    ts(c("wt16"), c("rj"), 1.0, Op.max, 235.0, Op.add)
+    ms(c("LK"), 0.0)
+    ts(c("G8"), c("qq", 0, 8), gcol, Op.is_equal)
+    for k in range(8):
+        ts(c("LK", 16 * k, 16 * k + 129 * 15 + 1, 129), c("wt16", 0, 16), c("G8", k, k + 1), Op.mult)
+    ts(c("tg"), c("wt16", 16, 32), 80.0, Op.mult, 3917.0 + 11328.0, Op.add)
+    ts(c("qt", 16, 32), c("D16", 0, 16), -30208.0, Op.mult)
+    tt(c("ti", 0, 16), c("tg"), c("qt", 16, 32), Op.add)
+    ts(c("ti", 16, 32), c("ti", 0, 16), 0xFF00, Op.bitwise_and)
+    ts(c("ti", 32, 48), c("ti", 0, 16), 0xFF, Op.bitwise_and)
+    for name, lo in (("TGh", 16), ("TGl", 32)):
+        ts(c(name, 0, 32, 2), c("ti", lo, lo + 16), -1.0, Op.mult)
+        ts(c(name, 1, 32, 2), c("ti", lo, lo + 16), -1.0, Op.mult)
+        for k in (32, 64, 128):
+            cp(c(name, k, 2 * k), c(name, 0, k))
+    ms(c("RM"), 0.0)
+    ms(c("RM", 0, 1536, 16), 255.0)
+    ts(c("OD"), c("D16", 0, 32), 2.0 ** 25, Op.mult, -2.0 ** 25, Op.add)
+    ms(c("FX"), 0.0)
+    for h, k in ((0, 1), (48, 0)):
+        ts(c("FX", h, h + 16), c("ONE", 0, 16), c("wf", 6 + k, 7 + k), Op.mult)
+        ts(c("FX", h + 16, h + 31), c("ONE", 0, 15), c("wf", 4 + k, 5 + k), Op.mult)
+        ts(c("FX", h + 32, h + 47), c("ONE", 0, 15), c("wf", 4 + k, 5 + k), Op.mult)
+    ts(c("I8"), c("ID"), 8192.0, Op.mult)
+    ts(c("In22"), c("ID"), -2.0 ** 22, Op.mult)
+    ts(c("In1"), c("ID"), -1.0, Op.mult)
+    ts(c("JT"), c("qq", 0, 96), -2.0, Op.mult)
+    ms(c("qt"), 0.25)
+    ms(c("nd"), 0.0)
+    scan(c("thr"), c("qt"), c("nd"), 2.0 ** 51, Op.mult, Op.add)
+    tt(c("qt", 0, 16), c("thr", 0, 16), c("D16", 0, 16), Op.mult)
+    red(c("pc", 13, 14), c("qt", 0, 16), Op.add)
+    ts(c("LD"), c("BO"), c("pc", 13, 14), Op.mult)
+    ts(c("tr"), c("qq", 0, 64), 4112.0, Op.add)
+    ts(c("mA"), c("qq", 0, 64), 4113.0, Op.add)
+    tt(c("mA"), c("mA"), c("D16", 0, 64), Op.mult)
+    ts(c("mA"), c("mA"), -1.0, Op.add)
+    tt(c("pc", 7, 8), c("pc", 3, 4), lcol, Op.subtract)
+    ts(c("pc", 8, 9), c("pc", 7, 8), -31.0, Op.add, MUL, Op.mult)
+    ts(c("pc", 7, 8), c("pc", 7, 8), -15.0, Op.add, MUL, Op.mult)
+    ts(c("pc", 9, 13), c("qq", 0, 64, 16), lcol, Op.add)
+    ts(c("pc", 9, 11), c("pc", 9, 11), -1.0, Op.mult, -0.5, Op.add)
+    emit("G", [c("thb")], [c("thi")], lambda: g.partition_broadcast(T.thb[:], T.thi[0:1, :], 128), 180.0)
+    tt(c("thf"), c("thb"), c("G8"), Op.mult)
+    red(c("thc", 0, 1), c("thf"), Op.add)
+    ts(c("thc", 1, 2), c("thc", 0, 1), 16384.0, Op.add)
+    ms(c("C", 256, 272), 0.0)
+    ms(c("D", 256, 272), 0.0)
+    ms(c("tp", 256, 272), 8000.0)
+    if above is None:
+        ms(c("FD"), 1.0)
+    for r in range(R):
+        if below is None:
+            ms(c("X", 48 * r, 48 * r + 16), 240.0)
+        if above is None:
+            ms(c("X", 48 * r + 32, 48 * r + 48), 240.0)
+
+    Ew, Sw, Pw = c("E"), c("S"), c("PLC")
+
+    def keys(r, lo, hi):
+        for bk in ("p7", "p6"):
+            parts = [(c(bk, lo, hi), c("ID"), c("JT1" if r == 0 else "JT", lo, hi))]
+            if bk == "p7":
+                parts.append((c(bk, lo, hi), c("ID"), c("K2", lo, hi)))
+            parts.append((c(bk, lo, hi), c("BO1k"), c("PS", lo, hi)))
+            if r:
+                parts += [(c(bk, 32, 96), c("In22"), c("nb")), (c(bk, 32, 96), c("In22"), c("ov"))]
+            mms(parts)
+
+    def ranks(r, lo, hi, on_v):
+        n = hi - lo
+        scan(c("KA", lo, hi), c("RZ", 0, n), c("p7", lo, hi), 0.0, Op.mult, Op.max)
+        act(c("KB", lo, hi), c("p6", lo, hi), Fn.Identity, bias=OFF + 1)
+        z = c("p4", lo, hi)
+        mm(z, c("DG"), c("ONE", 0, n), True, False)
+        mm(z, c("IDF"), c("PB", lo, hi), False, False)
+        if r:
+            mm(c("p4", 32, 96), c("I8"), c("ov"), False, False)
+        ks = list(range(n // 16))
+        kv, ka = ks[:on_v], ks[on_v:]
+        order = []
+        for j in range(max(len(kv), len(ka))):
+            order += kv[j:j + 1] + ka[j:j + 1]
+        for k in order:
+            o, key = c("cm", n * k, n * k + n), c("KA", lo + 16 * k + 15, lo + 16 * k + 16)
+            if k in kv:
+                ts(o, c("KB", lo, hi), key, Op.is_lt, len(ka) / 2 if k == 0 else 0.0, Op.add)
+            else:
+                act(o, c("KB", lo, hi), Fn.Sign, bias=key, scale=-1.0)
+            mm(z, c("BOz" if k in kv else "BOh"), o, False, k == order[-1])
+        red(c("pl", 0, 1), z, Op.min, True)
+        ts(c("po", 0, 1), c("pl", 0, 1), c("pc", 6, 7), Op.min)
+
+    def stayers(r, lo, hi):
+        m = 2 - r
+        for k in range(m):
+            act(c("zs", 256 * k + lo, 256 * k + hi), c("p4", lo, hi), Fn.Abs, bias=c("pc", 7 + k, 8 + k))
+            red(c("pl", 1 + k, 2 + k), c("zs", 256 * k + lo, 256 * k + hi), Op.min)
+        ts(c("vo", 0, m), c("pl", 1, 1 + m), 4111.0, Op.min)
+        act(c("PS", 32 - 16 * m, 32), ind(Sw, c("vo", 0, m)), Fn.Copy)
+        act(c("PB", 32 - 16 * m, 32), ind(Pw, c("vo", 0, m)), Fn.Copy)
+
+    def hash_tail(o, n):
+        ab, s = c("AB", o, o + 2 * n), c("SS", o, o + 2 * n)
+        m = c("MM", o // 2, o // 2 + n)
+        ts(ab, ab, 4095, Op.bitwise_and)
+        tt(m, c("AB", o, o + n), c("AB", o + n, o + 2 * n), Op.mult)
+        ts(c("SS", o, o + n), m, 5, Op.arith_shift_right)
+        ts(c("SS", o + n, o + 2 * n), m, 9, Op.arith_shift_right)
+        tt(s, s, ab, Op.add)
+        ts(s, s, 4095, Op.bitwise_and)
+        if o == XC:
+            cp(c("HU", o, o + 2 * n), s)
+        else:
+            cp(c("HU", o, o + 2 * n, 2), c("SS", o, o + n))
+            cp(c("HU", o + 1, o + 2 * n, 2), c("SS", o + n, o + 2 * n))
+
+    def wmm(o, k, x):
+        return [(o, c("WB", 128 * k, 128 * k + 128), x), (o, c("WB", 128 * k + 256, 128 * k + 384), x)]
+
+    def col(p, home):
+        p0, p1 = [h for h in HC if h[0] <= p < h[1]][0]
+        return 32 * p0 + 16 * (p1 - p0) * home + 16 * (p - p0)
+
+    def decode(bk, at, buf, lo, n):
+        return [(c(bk, at, at + n), c("LK", 128 * k, 128 * k + 128), c(buf, 16 * lo + k, 16 * (lo + n), 16)) for k in range(16)]
+
+    def round_(r):
+        xo = 48 * r
+        rp, par, up = c("X", xo, xo + 16), c("X", xo + 16, xo + 32), c("X", xo + 32, xo + 48)
+        ts(par, ind(Ew, c("po", 0, 1)), sgn, Op.mult, off, Op.add)
+        trs, tot = [], 0
+        for dst, k, sem, land in ((above, 0, "lo", rp), (below, 1, "up", up)):
+            if dst is not None:
+                es = halves(core, dst, k)
+                trs.append(RemoteDMATransfer(dst_ids=[dst_id(dst)], dma_engine_mask=mask_of(es), remote_sem=T.sem[sem + str(r)], src=par[0], dst=land[0]))
+                tot += len(es)
+        sent = emit("G", [], [par], lambda: g.remote_dma_fused(trs, local_sem=T.sem["ls%d" % r]), 500.0, sem="ls%d" % r, inc=tot, chain=False)
+        if above is not None:
+            landed(up, "up%d" % r, len(halves(above, core, 1)), sent, FAR)
+        if below is not None:
+            landed(rp, "lo%d" % r, len(halves(below, core, 0)), sent, FAR)
+        act(c("b8"), par, Fn.Identity, bias=1.0, scale=-8.0)
+        cp(ind(Ew, c("po", 0, 1)), par)
+        if r == R - 1:
+            dma("Y", c("ec"), c("E", 0, W, rows=row0), 1 << 16)
+            ts(c("f2"), c("ec"), 0.0, Op.is_ge, 2.0, Op.mult)
+            ts(c("p3", 0, 256), c("ec"), -2.0, Op.is_le)
+            tt(c("yc"), c("p3", 0, 256), c("f2"), Op.add)
+            dma("Y", c("ST", 0, W, rows=row0), c("yc"), 1 << 17)
+        for k, (p0, p1) in enumerate(HC):
+            n, o, bk = 16 * (p1 - p0), 32 * p0, ("p0", "p6")[k % 2]
+            tt(c("C", 16 * p0, 16 * p1), ind(par, c("EX", p0, p1)), c("D16", 0, n), Op.add)
+            mms(wmm(c(bk, 0, n), 1, c("C", 16 * p0, 16 * p1)))
+            mms(wmm(c(bk, n, 2 * n), 0, c("C", 16 * p0, 16 * p1)))
+            ts(c("AB", o, o + n), c(bk, 0, n), c("wf", 7, 8), Op.add)
+            ts(c("AB", o + n, o + 2 * n), c(bk, n, 2 * n), c("wf", 6, 7), Op.add)
+            hash_tail(o, n)
+        act(c("NZ", 0, 240), c("C", 0, 240), Fn.Identity, bias=float(NEUTRAL))
+        if r == 0:
+            ts(c("f2"), c("PB"), 4096.0, Op.is_lt)
+            red(c("rm", 1, 2), c("f2"), Op.add)
+            ts(c("rm", 1, 2), c("rm", 1, 2), -1.0, Op.mult, 271.0, Op.add)
+            ts(c("rm", 0, 1), c("rm", 1, 2), 256.0, Op.min)
+        if r < 2:
+            stayers(r, 0, (256, 96)[r])
+
+        def fetch(c0, c1, on_a=0):
+            mid = c1 - on_a
+            for a, b in ((c0, mid), (mid, c1)):
+                if a < b:
+                    o = c("G2", 16 * a, 16 * b)
+                    if a == mid:
+                        act(o, ind(Sw, c("SU", a, b)), Fn.Copy)
+                    else:
+                        cp(o, ind(Sw, c("SU", a, b)))
+                    scan(c("MS", 16 * a, 16 * b), c("RM", 0, 16 * (b - a)), o, 0.0, Op.max, Op.min)
+                    follow("V")
+
+        def piece(k):
+            p0, p1 = SC[k]
+            n, bk, b3, c0 = 16 * (p1 - p0), ("p1", "p2")[k % 2], 256 * (k % 2), 16 * p0
+            for p in range(p0, p1):
+                act(c("FF", 512 * p, 512 * p + 512), ind(Ew, c("HU", 32 * p, 32 * p + 32)), Fn.Square, bias=c("b8", p, p + 1), scale=8.0)
+                follow("A")
+            o1, o2 = col(p0, 0), col(p0, 1)
+            mms([(c(bk, 0, 2 * n), c("ID"), c("TGh", 0, 2 * n)), (c(bk, 0, 2 * n), c("ID"), c("TGl", 0, 2 * n))] + decode(bk, 0, "FF", 32 * p0, 2 * n))
+            x1 = c("p3", b3, b3 + 2 * n, 2)
+            ts(c("p3", b3, b3 + 2 * n), c(bk, 0, 2 * n), 0.0, Op.not_equal, PEN, Op.mult)
+            tt(x1, x1, c("SS", o1, o1 + n), Op.add)
+            tt(c("mh", c0, c0 + n), c("p3", b3 + 1, b3 + 2 * n, 2), c("SS", o2, o2 + n), Op.add)
+            tt(x1, x1, c("mh", c0, c0 + n), Op.min)
+            tt(c("sl", c0, c0 + n), x1, c("NZ", c0, c0 + n), Op.min)
+            cp(c("SU", c0, c0 + n), c("sl", c0, c0 + n))
+            fetch(c0, c0 + n, ON_A.get(k, 0))
+
+        def extras():
+            x3, x2 = c("X", xo, xo + 48), c("X", xo, xo + 32)
+            mms(wmm(c("p5", 0, 48), 1, x3))
+            mms(wmm(c("p5", 48, 96), 0, x3))
+            for h, k in ((0, 1), (32, 0)):
+                mms([(c("p4", h, h + 32), c("ID"), c("OD"))] + wmm(c("p4", h, h + 32), k, x2))
+            cp(c("C", 240, 256), rp)
+            act(c("NZ", 240, 256), rp, Fn.Identity, bias=float(NEUTRAL))
+            for h in (0, 1):
+                red(c("p5", 48 * h + 31, 48 * h + 32), c("p4", 32 * h, 32 * h + 16), Op.max)
+                red(c("p5", 48 * h + 47, 48 * h + 48), c("p4", 32 * h + 16, 32 * h + 32), Op.max)
+            tt(c("AB", XC, XC + 96), c("p5", 0, 96), c("FX"), Op.add)
+            hash_tail(XC, 48)
+            ts(c("zi"), c("MM", XC // 2 + 16, XC // 2 + 32), 7, Op.arith_shift_right, 2047, Op.bitwise_and)
+            cp(c("zu"), c("zi"))
+            tt(c("YE"), ind(rp, c("EX")), c("D16"), Op.subtract)
+            if above is not None:
+                tt(c("CU", 0, 240), ind(up, c("EX", 0, 15)), c("D16", 0, 240), Op.add)
+                cp(c("CU", 240, 256), par)
+            for h in (0, 1):
+                o, f = XC + 48 * h, 768 * h
+                if above is not None:
+                    tt(c("FD", f + 512, f + 768), ind(Ew, c("HU", o + 32, o + 48)), c("CU"), Op.not_equal)
+                tt(c("FD", f, f + 256), ind(Ew, c("HU", o, o + 16)), c("YE"), Op.not_equal)
+                act(c("FD", f + 256, f + 512), ind(Ew, c("HU", o + 16, o + 32)), Fn.Abs, bias=1.0)
+            mms(decode("p0", 0, "FD", 0, 96))
+            x1 = c("p5", 128, 176)
+            ts(c("p5", 128, 224), c("p0", 0, 96), 0.0, Op.not_equal, PEN, Op.mult)
+            ts(c("ta"), c("p0", 16, 32), 0.0, Op.is_equal, PEN, Op.mult)
+            tt(c("mh", 240, 288), c("p5", 176, 224), c("SS", XC + 48, XC + 96), Op.add)
+            tt(x1, x1, c("SS", XC, XC + 48), Op.add)
+            tt(c("mh", 256, 272), c("mh", 256, 272), c("ta"), Op.add)
+            tt(x1, x1, c("mh", 240, 288), Op.min)
+            if above is not None:
+                sv = c("SV", 256 * r, 256 * r + 256)
+                ts(c("su2"), c("p5", 160, 176), float(ZERO), Op.min)
+                act(sv, ind(Sw, c("su2")), Fn.Copy)
+                rid, pid, _ = topo.addr(above)
+                back = emit("G", [], [sv], lambda: g.remote_dma(T.RP[:, 256 * r:256 * r + 256], sv[0], T.sem["rp%d" % r], T.sem["lr%d" % r], pid, rid, topo.mask(core, above)),
+                            500.0, sem="lr%d" % r, inc=len(topo.engines(core, above)), chain=False, lat=FAR + 2000.0)
+            else:
+                back = len(ops) - 1
+            if below is not None:
+                landed(c("RP", 256 * r, 256 * r + 256), "rp%d" % r, len(topo.engines(below, core)), back, 0.0 if above is not None else FAR)
+            tt(c("sl", 240, 256), c("p5", 128, 144), c("NZ", 240, 256), Op.min)
+            cp(c("SU", 240, 256), c("sl", 240, 256))
+            ts(c("tu"), c("p5", 144, 160), float(NEUTRAL), Op.min)
+            fetch(240, 256)
+            act(c("t256"), ind(Pw, c("tu")), Fn.Copy)
+            act(c("EVg"), ind(c("ENV"), c("zu")), Fn.Copy)
+            for h in (0, 1):
+                mms([(c("p4", 256 * h, 256 * h + 256), c("In1"), c("C", 0, 256)),
+                     (c("p4", 256 * h, 256 * h + 256), c("ID"), c("FD", 768 * h + 256, 768 * h + 512))])
+            act(c("sq"), c("p4"), Fn.Square, bias=-1.0)
+            mm(c("p4"), c("BO"), c("sq"), True, True)
+            act(c("sg"), c("p4"), Fn.Sign)
+            return back
+
+        def lower(a, b):
+            M = c("MS", 16 * a + 15, 16 * b, 16)
+            if below is not None:
+                tt(c("M5", a, b), M, c("RP", 256 * r + a, 256 * r + b), Op.min)
+                mm(c("p7", a, b), c("BO"), c("M5", a, b), True, True)
+                tt(c("D", a, b), c("M5", a, b), c("EVg", a, b), Op.subtract)
+                ts(c("p5", 256 + a, 256 + b), c("p7", a, b), c("thc", 0, 1), Op.is_lt, 8192.0, Op.mult)
+                tt(c("tp", a, b), c("p5", 256 + a, 256 + b), c("t256", a, b), Op.add)
+            else:
+                tt(c("D", a, b), M, c("EVg", a, b), Op.subtract)
+                cp(c("tp", a, b), c("t256", a, b))
+
+        piece(0)
+        back = extras()
+        for k in range(1, len(SC)):
+            piece(k)
+        cut = 16 * SC[-1][0]
+        for a, b in ((0, cut), (cut, 256)):
+            mms([(c("p6", a, b), c("I8"), c("sg", a, b)), (c("p6", a, b), c("I8"), c("sg", 256 + a, 256 + b)), (c("p6", a, b), c("BO"), c("MS", 16 * a + 15, 16 * b, 16))])
+            ts(c("good", a, b), c("p6", a, b), c("thc", 1, 2), Op.is_ge)
+            scan(c("pre", a, b), c("good", a, b), c("good", a, b), c("pre", a - 1, a) if a else 0.0, Op.add, Op.max)
+        soft.append((back, len(ops)))
+        lower(0, cut)
+        lower(cut, 256)
+        for k in range(4):
+            junk = c("junk", 256 * k, 256 * k + 256)
+            if k < 2:
+                act(junk, c("pre"), Fn.Sign, bias=c("pc", 9 + k, 10 + k), accum=c("acc", k, k + 1))
+            else:
+                ts(junk, c("pre"), c("pc", 9 + k, 10 + k), Op.is_le)
+                scan(junk, junk, junk, 0.0, Op.add, Op.max)
+        ts(c("ix", 0, 2), c("acc", 0, 2), -0.5, Op.mult, 128.0, Op.add)
+        cp(c("ix", 2, 4), c("junk", 767, 1024, 256))
+        tt(c("tm"), ind(c("tp"), c("ix")), c("mA"), Op.min)
+        tt(c("tB"), ind(c("tp"), c("ix")), c("tr"), Op.min)
+        act(c("PS", 32, 96), ind(c("D"), c("ix")), Fn.Abs)
+        if r < R - 1:
+            act(c("Ce"), ind(c("C"), c("ix")), Fn.Identity, bias=off, scale=sgn)
+        scan(c("tA"), c("RZ", 0, 64), c("tm"), 0.0, Op.mult, Op.max)
+        for k in range(4):
+            ts(c("eq", 64 * k, 64 * k + 64), c("tB"), c("tA", 16 * k + 15, 16 * k + 16), Op.is_equal, 2.0 ** (-1 - 32 * k), Op.mult)
+            mm(c("p7", 0, 64), c("LD"), c("eq", 64 * k, 64 * k + 64), k == 0, k == 3)
+        dup, tb = c("p3", 0, 64), c("PB", 32, 96)
+        tt(dup, c("p7", 0, 64), c("thr"), Op.is_ge)
+        tt(dup, dup, c("tr"), Op.mult)
+        tt(tb, dup, c("tB"), Op.max)
+        if r < 2:
+            ts(c("nb"), tb, 4096.0, Op.is_ge)
+            scan(c("qc"), c("ONE", 0, 64), c("nb"), 0.0, Op.add, Op.subtract)
+            ts(c("ov"), c("qc"), c("rm", 0, 1), Op.is_gt)
+            keys(r + 1, 16 * r, 96)
+        tt(c("tm"), tb, c("mA"), Op.min)
+        scan(c("tA"), c("RZ", 0, 64), c("tm"), 0.0, Op.mult, Op.max)
+        cp(c("so"), c("tA", 15, 64, 16))
+        cp(ind(Sw, c("so")), c("PS", 32, 96))
+        if r < R - 1:
+            cp(ind(Ew, c("so")), c("Ce"))
+        else:
+            cp(ind(c("ST"), c("so")), c("ONE", 0, 64))
+        if r == 0:
+            tt(c("rm", 1, 2), c("rm", 0, 1), c("qc", 63, 64), Op.subtract)
+            ts(c("rm", 1, 2), c("rm", 1, 2), 0.0, Op.max, 15.0, Op.add)
+            ts(c("rm", 0, 1), c("rm", 1, 2), 256.0, Op.min)
+        if r < 2:
+            ranks(r + 1, 16 * r, 96, 2)
+
+    cp(c("PS"), ind(Sw, c("qo")))
+    act(c("PB"), ind(Pw, c("qo")), Fn.Copy)
+    keys(0, 0, 256)
+    ranks(0, 0, 256, 7)
+    for r in range(R):
+        round_(r)
+    dma("Y", T.ys[:], c("S", 0, W), 1 << 20)
+    dma("A", T.yst[:], c("ST", 0, W, rows=row0), 1 << 17)
+    issue()

@@ -1,3 +1,4 @@
+import numpy as np
 from concourse.bass import DstId, RemoteDMATransfer
 from concourse.mybir import AluOpType as Op, AxisListType, ActivationFunctionType as Fn
 
@@ -8,7 +9,8 @@ ON_A = {0: 32, 1: 32, 2: 48, 3: 24}
 XC = 480
 MUL, OFF, PEN = 32768.0, 9437184.0, 16384.0
 NEUTRAL, ZERO = 4176, 4177
-CY, GA, SCA, PE, HOP, FAR = 1.04, 1.56, 3.8, 0.6, 100.0, 3600.0
+PLANS = [(0.83, 1.3, 0.83, 110.0, 3600.0, 92.0), (0.9, 1.4, 0.83, 180.0, 4600.0, 110.0), (1.0, 1.6, 0.83, 170.0, 6600.0, 125.0), (1.1, 1.9, 0.9, 240.0, 4600.0, 145.0)]
+SCA, TRIES, AMP, SPAN = 3.8, 120, 1500.0, 60
 B, F, I, U = "bfloat16", "float32", "int32", "uint16"
 _SB = {
     "E": (4176, B), "S": (4432, B), "ENV": (EV, B), "PLC": (4192, F), "ST": (4176, F),
@@ -19,7 +21,7 @@ _SB = {
     "BOz": (128, B), "BOh": (128, B), "LD": (128, B), "DG": (128, B), "WB": (512, B), "D16": (256, B), "LK": (2048, B),
     "tg": (16, F), "ti": (48, I), "TGh": (256, B), "TGl": (256, B),
     "EXi": (16, I), "EX": (16, U), "RM": (1536, B), "RZ": (256, B), "ONE": (256, B), "JT": (96, B), "JT1": (256, B), "K2": (256, B),
-    "OD": (32, B), "thr": (64, F), "qt": (64, F), "tr": (64, F), "mA": (64, F), "FX": (96, F), "G8": (8, F),
+    "OD": (32, B), "thr": (64, F), "nt": (64, B), "iv": (64, B), "n2": (128, F), "qt": (64, F), "tr": (64, F), "mA": (64, F), "FX": (96, F), "G8": (8, F),
     "X": (48 * R, B), "RP": (256 * R, B), "SV": (256 * R, B), "b8": (16, F), "C": (272, B), "CU": (256, B), "YE": (256, B), "NZ": (256, F),
     "AB": (576, I), "MM": (288, I), "SS": (576, I), "HU": (576, U), "zi": (16, I), "zu": (16, U),
     "FF": (7680, B), "FD": (1536, B), "mh": (288, F), "sl": (256, F), "SU": (256, U), "su2": (16, U), "G2": (4096, B), "MS": (4096, B),
@@ -53,7 +55,7 @@ def rank_program(g, core, T, topo):
     def ind(win, off):
         return (win[0].indirect(off[0]), win[1], off[1], 16 * off[3], win[4], False, True)
 
-    def emit(eng, outs, ins, call, dur, sem=None, inc=1, chain=True, after=(), lat=0.0, size=0, skip=()):
+    def emit(eng, outs, ins, call, dur, sem=None, inc=1, chain=True, after=(), lat=(0, 0), size=0, skip=()):
         k = len(ops)
         wr = [x for o in outs for x in o[1]]
         rd = [x for o in outs for x in o[2]] + [x for o in ins if isinstance(o, tuple) for x in o[1] + o[2]]
@@ -96,33 +98,64 @@ def rank_program(g, core, T, topo):
                 succ[j].append(k)
         for a, b in soft:
             more[a].append(b)
-        prio = [0.0] * n
-        for k in range(n - 1, -1, -1):
-            o = ops[k]
-            prio[k] = o["dur"] + o["lat"] + o["size"] / 200.0 + max([prio[j] + HOP for j in succ[k]] + [prio[j] for j in more[k]], default=0.0)
-        left = [len(o["deps"] | o["order"]) for o in ops]
-        start, done, free, seq, wire = [0.0] * n, [0.0] * n, {e: 0.0 for e in list(Q) + [None]}, {e: [] for e in Q}, [0.0]
-        ready = {k: 0.0 for k in range(n) if left[k] == 0}
-        while ready:
-            at = {k: max(t, free[ops[k]["eng"]]) for k, t in ready.items()}
-            e = ops[min(at, key=lambda k: (at[k], -prio[k]))]["eng"]
-            mine = [k for k in at if ops[k]["eng"] == e]
-            t0 = min(at[k] for k in mine)
-            k = max((j for j in mine if at[j] <= t0 + HOP), key=lambda j: (prio[j], -j))
-            o = ops[k]
-            del ready[k]
-            start[k] = at[k]
-            done[k] = at[k] + o["dur"] + o["lat"]
-            if o["size"]:
-                wire[0] = max(wire[0], at[k] + 1000.0) + o["size"] / 200.0
-                done[k] = wire[0] + 1000.0
-            if e is not None:
-                free[e] = at[k] + o["dur"]
-                seq[e].append(k)
-            for j in succ[k]:
-                left[j] -= 1
-                if left[j] == 0:
-                    ready[j] = max([done[i] + HOP for i in ops[j]["deps"]] + [done[i] if ops[j]["eng"] is None else start[i] for i in ops[j]["order"]])
+        pre = [sorted(o["deps"]) for o in ops]
+        aft = [sorted(o["order"]) for o in ops]
+
+        def run(p, took, reach=0.0, shift=()):
+            dur = [o["dur"][0] + p[0] * (o["dur"][1] + p[1] * o["dur"][2] + SCA * o["dur"][3]) + p[2] * o["dur"][4] for o in ops]
+            lat = [o["lat"][0] * p[4] + o["lat"][1] for o in ops]
+            hop, make = p[3], not took
+            start, done, free, wire = [0.0] * n, [0.0] * n, {e: 0.0 for e in list(Q) + [None]}, 0.0
+
+            def at(j):
+                return max([done[i] + hop for i in pre[j]] + [done[i] if ops[j]["eng"] is None else start[i] for i in aft[j]] + [0.0])
+            if make:
+                prio = [0.0] * n
+                for k in range(n - 1, -1, -1):
+                    prio[k] = dur[k] + lat[k] + ops[k]["size"] / 200.0 + max([prio[j] + hop for j in succ[k]] + [prio[j] for j in more[k]], default=0.0)
+                prio = [x + y for x, y in zip(prio, shift)]
+                left = [len(o["deps"] | o["order"]) for o in ops]
+                ready = {e: {} for e in free}
+                for k in range(n):
+                    if left[k] == 0:
+                        ready[ops[k]["eng"]][k] = 0.0
+            for step in range(n):
+                if make:
+                    t0, e = min(((max(free[e], min(d.values())), e) for e, d in ready.items() if d), key=lambda x: x[0])
+                    k = max((j for j, t in ready[e].items() if t <= t0 + hop * reach), key=lambda j: (prio[j], -j))
+                    t = max(ready[e].pop(k), free[e])
+                    took.append(k)
+                else:
+                    k = took[step]
+                    e = ops[k]["eng"]
+                    t = max(at(k), free[e])
+                start[k], done[k] = t, t + dur[k] + lat[k]
+                if ops[k]["size"]:
+                    wire = max(wire, t + 1000.0) + ops[k]["size"] / 200.0
+                    done[k] = wire + 1000.0
+                if e is not None:
+                    free[e] = t + dur[k]
+                if make:
+                    for j in succ[k]:
+                        left[j] -= 1
+                        if left[j] == 0:
+                            ready[ops[j]["eng"]][j] = at(j)
+            return max(done)
+
+        best = None
+        rs = np.random.RandomState(1)
+        for t in range(TRIES):
+            took = []
+            if t < 12:
+                how = (PLANS[t % 4], (0.5, 1.0, 2.0)[t // 4], [0.0] * n)
+            else:
+                lo = int(rs.randint(n))
+                how = (best[2][0], best[2][1], [x + (AMP * float(rs.randn()) if lo <= k < lo + SPAN else 0.0) for k, x in enumerate(best[2][2])])
+            run(how[0], took, how[1], how[2])
+            worth = sum(run(p, took) / p[5] for p in PLANS)
+            if best is None or worth < best[0]:
+                best = (worth, took, how)
+        seq = {e: [k for k in best[1] if ops[k]["eng"] == e] for e in Q}
         top, val = {}, {}
         for k in [k for e in Q for k in seq[e]] + [k for k in range(n) if ops[k]["eng"] is None]:
             top[ops[k]["sem"]] = val[k] = top.get(ops[k]["sem"], 0) + ops[k]["inc"]
@@ -153,8 +186,8 @@ def rank_program(g, core, T, topo):
 
     def cost(o, i, per, fix=50.0):
         if o[6] or i[6]:
-            return fix + CY * (o[3] * SCA if o[6] else i[3] * GA)
-        return CY * max(64.0, i[3] * per)
+            return (fix, 0, 0, o[3], 0) if o[6] else (fix, 0, i[3], 0, 0)
+        return (0, max(64.0, i[3] * per), 0, 0, 0)
 
     def half(*xs):
         return 0.5 if all(x[4] for x in xs) else 1.0
@@ -185,7 +218,7 @@ def rank_program(g, core, T, topo):
              lambda: g.scalar.activation(o[0], i[0], fn, bias=ap(bias), scale=ap(scale), accum_out=ap(accum)), cost(o, i, 1.0, 65.0))
 
     def mm(o, l, r, start, stop):
-        emit("P", [o], [l, r], lambda: g.tensor.matmul(o[0], l[0], r[0], start, stop), PE * max(64, r[3]) * (1 if r[4] else 4))
+        emit("P", [o], [l, r], lambda: g.tensor.matmul(o[0], l[0], r[0], start, stop), (0, 0, 0, 0, max(64, r[3]) * (1 if r[4] else 4)))
 
     def mms(parts):
         for k, (o, l, r) in enumerate(parts):
@@ -193,15 +226,15 @@ def rank_program(g, core, T, topo):
 
     def iota(o, pat, base, cm):
         if SCRATCH[o[1][0][0]][2] == I:
-            emit("G", [o], [], lambda: g.iota(o[0], pat, base, cm), 130 + 2 * CY * o[3])
+            emit("G", [o], [], lambda: g.iota(o[0], pat, base, cm), (130, 2 * o[3], 0, 0, 0))
         else:
-            emit("G", [o], [], lambda: g.iota(o[0], pat, base, cm, allow_small_or_imprecise_dtypes=True), 130 + 2 * CY * o[3])
+            emit("G", [o], [], lambda: g.iota(o[0], pat, base, cm, allow_small_or_imprecise_dtypes=True), (130, 2 * o[3], 0, 0, 0))
 
     n_dma = [0]
 
     def dma(eng, o, i, size, skip=()):
         n_dma[0] += 1
-        return emit(eng, [o] if isinstance(o, tuple) else [], [i], lambda: Q[eng].dma_start(ap(o), ap(i)), 100.0,
+        return emit(eng, [o] if isinstance(o, tuple) else [], [i], lambda: Q[eng].dma_start(ap(o), ap(i)), (100, 0, 0, 0, 0),
                     sem="d%d" % (n_dma[0] - 1), inc=16, size=size, skip=skip)
 
     def mask_of(es):
@@ -212,7 +245,7 @@ def rank_program(g, core, T, topo):
         return es[:len(es) // 2] if k == 0 else es[len(es) // 2:]
 
     def landed(o, sem, n, after, lat):
-        emit(None, [o], [], None, 0.0, sem=sem, inc=n, after=[after], lat=lat)
+        emit(None, [o], [], None, (0, 0, 0, 0, 0), sem=sem, inc=n, after=[after], lat=lat)
 
     def dst_id(dst):
         rid, pid, _ = topo.addr(dst)
@@ -318,6 +351,7 @@ def rank_program(g, core, T, topo):
     ms(c("nd"), 0.0)
     scan(c("thr"), c("qt"), c("nd"), 2.0 ** 51, Op.mult, Op.add)
     tt(c("qt", 0, 16), c("thr", 0, 16), c("D16", 0, 16), Op.mult)
+    ts(c("nt"), c("thr"), -1.0, Op.mult)
     red(c("pc", 13, 14), c("qt", 0, 16), Op.add)
     ts(c("LD"), c("BO"), c("pc", 13, 14), Op.mult)
     ts(c("tr"), c("qq", 0, 64), 4112.0, Op.add)
@@ -329,7 +363,7 @@ def rank_program(g, core, T, topo):
     ts(c("pc", 7, 8), c("pc", 7, 8), -15.0, Op.add, MUL, Op.mult)
     ts(c("pc", 9, 13), c("qq", 0, 64, 16), lcol, Op.add)
     ts(c("pc", 9, 11), c("pc", 9, 11), -1.0, Op.mult, -0.5, Op.add)
-    emit("G", [c("thb")], [c("thi")], lambda: g.partition_broadcast(T.thb[:], T.thi[0:1, :], 128), 180.0)
+    emit("G", [c("thb")], [c("thi")], lambda: g.partition_broadcast(T.thb[:], T.thi[0:1, :], 128), (180, 0, 0, 0, 0))
     tt(c("thf"), c("thb"), c("G8"), Op.mult)
     red(c("thc", 0, 1), c("thf"), Op.add)
     ts(c("thc", 1, 2), c("thc", 0, 1), 16384.0, Op.add)
@@ -424,11 +458,11 @@ def rank_program(g, core, T, topo):
                 es = halves(core, dst, k)
                 trs.append(RemoteDMATransfer(dst_ids=[dst_id(dst)], dma_engine_mask=mask_of(es), remote_sem=T.sem[sem + str(r)], src=par[0], dst=land[0]))
                 tot += len(es)
-        sent = emit("G", [], [par], lambda: g.remote_dma_fused(trs, local_sem=T.sem["ls%d" % r]), 500.0, sem="ls%d" % r, inc=tot, chain=False)
+        sent = emit("G", [], [par], lambda: g.remote_dma_fused(trs, local_sem=T.sem["ls%d" % r]), (500, 0, 0, 0, 0), sem="ls%d" % r, inc=tot, chain=False)
         if above is not None:
-            landed(up, "up%d" % r, len(halves(above, core, 1)), sent, FAR)
+            landed(up, "up%d" % r, len(halves(above, core, 1)), sent, (1, 0 if r else 2000))
         if below is not None:
-            landed(rp, "lo%d" % r, len(halves(below, core, 0)), sent, FAR)
+            landed(rp, "lo%d" % r, len(halves(below, core, 0)), sent, (1, 0 if r else 2000))
         act(c("b8"), par, Fn.Identity, bias=1.0, scale=-8.0)
         cp(ind(Ew, c("po", 0, 1)), par)
         if r == R - 1:
@@ -445,7 +479,7 @@ def rank_program(g, core, T, topo):
             ts(c("AB", o, o + n), c(bk, 0, n), c("wf", 7, 8), Op.add)
             ts(c("AB", o + n, o + 2 * n), c(bk, n, 2 * n), c("wf", 6, 7), Op.add)
             hash_tail(o, n)
-        act(c("NZ", 0, 240), c("C", 0, 240), Fn.Identity, bias=float(NEUTRAL))
+        act(c("NZ", 0, 16 * SC[-1][0]), c("C", 0, 16 * SC[-1][0]), Fn.Identity, bias=float(NEUTRAL))
         if r == 0:
             ts(c("f2"), c("PB"), 4096.0, Op.is_lt)
             red(c("rm", 1, 2), c("f2"), Op.add)
@@ -473,14 +507,22 @@ def rank_program(g, core, T, topo):
                 act(c("FF", 512 * p, 512 * p + 512), ind(Ew, c("HU", 32 * p, 32 * p + 32)), Fn.Square, bias=c("b8", p, p + 1), scale=8.0)
                 follow("A")
             o1, o2 = col(p0, 0), col(p0, 1)
-            mms([(c(bk, 0, 2 * n), c("ID"), c("TGh", 0, 2 * n)), (c(bk, 0, 2 * n), c("ID"), c("TGl", 0, 2 * n))] + decode(bk, 0, "FF", 32 * p0, 2 * n))
-            x1 = c("p3", b3, b3 + 2 * n, 2)
+            mms([(c(bk, 0, 2 * n), c("ID"), c("TGh", 0, 2 * n)), (c(bk, 0, 2 * n), c("ID"), c("TGl", 0, 2 * n))]
+                + [x for q in range(p0, p1, 2) for x in decode(bk, 32 * (q - p0), "FF", 32 * q, 32 * (min(q + 2, p1) - q))])
+            x1, sl = c("p3", b3, b3 + 2 * n, 2), c("sl", c0, c0 + n)
             ts(c("p3", b3, b3 + 2 * n), c(bk, 0, 2 * n), 0.0, Op.not_equal, PEN, Op.mult)
-            tt(x1, x1, c("SS", o1, o1 + n), Op.add)
+            last = k == len(SC) - 1
+            if last:
+                act(c("n2", 0, n), c("C", c0, c0 + n), Fn.Identity, bias=NEUTRAL - PEN, scale=PEN)
+                tt(sl, c("SS", o1, o1 + n), c("n2", 0, n), Op.min)
+            tt(x1, x1, sl if last else c("SS", o1, o1 + n), Op.add)
             tt(c("mh", c0, c0 + n), c("p3", b3 + 1, b3 + 2 * n, 2), c("SS", o2, o2 + n), Op.add)
             tt(x1, x1, c("mh", c0, c0 + n), Op.min)
-            tt(c("sl", c0, c0 + n), x1, c("NZ", c0, c0 + n), Op.min)
-            cp(c("SU", c0, c0 + n), c("sl", c0, c0 + n))
+            if last:
+                ts(c("SU", c0, c0 + n), x1, float(ZERO), Op.min)
+            else:
+                tt(sl, x1, c("NZ", c0, c0 + n), Op.min)
+                cp(c("SU", c0, c0 + n), sl)
             fetch(c0, c0 + n, ON_A.get(k, 0))
 
         def extras():
@@ -522,11 +564,11 @@ def rank_program(g, core, T, topo):
                 act(sv, ind(Sw, c("su2")), Fn.Copy)
                 rid, pid, _ = topo.addr(above)
                 back = emit("G", [], [sv], lambda: g.remote_dma(T.RP[:, 256 * r:256 * r + 256], sv[0], T.sem["rp%d" % r], T.sem["lr%d" % r], pid, rid, topo.mask(core, above)),
-                            500.0, sem="lr%d" % r, inc=len(topo.engines(core, above)), chain=False, lat=FAR + 2000.0)
+                            (500, 0, 0, 0, 0), sem="lr%d" % r, inc=len(topo.engines(core, above)), chain=False, lat=(1, 2000))
             else:
                 back = len(ops) - 1
             if below is not None:
-                landed(c("RP", 256 * r, 256 * r + 256), "rp%d" % r, len(topo.engines(below, core)), back, 0.0 if above is not None else FAR)
+                landed(c("RP", 256 * r, 256 * r + 256), "rp%d" % r, len(topo.engines(below, core)), back, (0 if above is not None else 1, 0))
             tt(c("sl", 240, 256), c("p5", 128, 144), c("NZ", 240, 256), Op.min)
             cp(c("SU", 240, 256), c("sl", 240, 256))
             ts(c("tu"), c("p5", 144, 160), float(NEUTRAL), Op.min)
@@ -580,15 +622,18 @@ def rank_program(g, core, T, topo):
         if r < R - 1:
             act(c("Ce"), ind(c("C"), c("ix")), Fn.Identity, bias=off, scale=sgn)
         scan(c("tA"), c("RZ", 0, 64), c("tm"), 0.0, Op.mult, Op.max)
+        ts(c("iv"), c("tB"), 4096.0, Op.is_ge, 2.0 ** 60, Op.mult)
+        mm(c("p7", 0, 64), c("ID"), c("nt"), True, False)
+        mm(c("p7", 0, 64), c("ID"), c("iv"), False, False)
         for k in range(4):
             ts(c("eq", 64 * k, 64 * k + 64), c("tB"), c("tA", 16 * k + 15, 16 * k + 16), Op.is_equal, 2.0 ** (-1 - 32 * k), Op.mult)
-            mm(c("p7", 0, 64), c("LD"), c("eq", 64 * k, 64 * k + 64), k == 0, k == 3)
+            mm(c("p7", 0, 64), c("LD"), c("eq", 64 * k, 64 * k + 64), False, k == 3)
         dup, tb = c("p3", 0, 64), c("PB", 32, 96)
-        tt(dup, c("p7", 0, 64), c("thr"), Op.is_ge)
-        tt(dup, dup, c("tr"), Op.mult)
+        if r < 2:
+            ts(c("nb"), c("p7", 0, 64), 0.0, Op.is_ge)
+        ts(dup, c("p7", 0, 64), 0.0, Op.is_ge, 8192.0, Op.mult)
         tt(tb, dup, c("tB"), Op.max)
         if r < 2:
-            ts(c("nb"), tb, 4096.0, Op.is_ge)
             scan(c("qc"), c("ONE", 0, 64), c("nb"), 0.0, Op.add, Op.subtract)
             ts(c("ov"), c("qc"), c("rm", 0, 1), Op.is_gt)
             keys(r + 1, 16 * r, 96)

@@ -5,35 +5,47 @@ from concourse.mybir import AluOpType as Op, AxisListType, ActivationFunctionTyp
 W, EV, R = 4096, 2048, 3
 HC = [(0, 4), (4, 15)]
 SC = [(0, 4), (4, 8), (8, 12), (12, 15)]
-ON_A = {0: 32, 1: 32, 2: 48, 3: 24}
+ON_V = {0: 32, 1: 16, 2: 16, 3: 24, 4: 0}
+FETCH = 32
+EARLY = ("p1", "p5", "p2", "p3", "p7")
+LATE = (("p4", "V"), ("p3", "V"), ("p7", "V"))
 XC = 480
 MUL, OFF, PEN = 32768.0, 9437184.0, 16384.0
-NEUTRAL, ZERO = 4176, 4177
-PLANS = [(0.83, 1.3, 0.83, 110.0, 3600.0, 92.0), (0.9, 1.4, 0.83, 180.0, 4600.0, 110.0), (1.0, 1.6, 0.83, 170.0, 6600.0, 125.0), (1.1, 1.9, 0.9, 240.0, 4600.0, 145.0)]
-SCA, TRIES, AMP, SPAN = 3.8, 120, 1500.0, 60
+NEUTRAL, NONE, PO = 4112, 4176, 16
+PLANS = [(0.83, 1.3, 0.83, 110.0, 3600.0, 80.0), (0.9, 1.4, 0.9, 180.0, 4600.0, 95.0), (1.0, 1.6, 1.0, 170.0, 6600.0, 110.0), (1.1, 1.9, 1.1, 240.0, 4600.0, 125.0)]
+SCA, AMP, SPAN = 3.8, 300.0, 150
+TRIES = 250
 B, F, I, U = "bfloat16", "float32", "int32", "uint16"
 _SB = {
-    "E": (4176, B), "S": (4432, B), "ENV": (EV, B), "PLC": (4192, F), "ST": (4176, F),
+    "E": (4176, B), "S": (4176, B), "VT": (4128, F), "ENV": (EV, B), "PLC": (PO + 4192, F), "ST": (4176, F),
     "qi": (16, I), "qo": (16, U), "wi": (2, I), "wf": (8, F), "wj": (4, I), "thi": (8, I), "thb": (8, I), "thf": (8, F), "thc": (2, F),
     "ec": (256, B), "sti": (256, I), "f1": (256, F), "f2": (256, F), "fx": (256, B), "yc": (256, F),
-    "pi": (4, I), "pc": (16, F), "qg": (128, F), "qq": (256, F), "jm": (256, F), "ri": (32, I), "rj": (32, I), "wt16": (32, F),
-    "BO": (128, B), "ID": (128, B), "IDF": (128, F), "I8": (128, B), "In22": (128, B), "In1": (128, B), "BO1k": (128, B),
-    "BOz": (128, B), "BOh": (128, B), "LD": (128, B), "DG": (128, B), "WB": (512, B), "D16": (256, B), "LK": (2048, B),
-    "tg": (16, F), "ti": (48, I), "TGh": (256, B), "TGl": (256, B),
-    "EXi": (16, I), "EX": (16, U), "RM": (1536, B), "RZ": (256, B), "ONE": (256, B), "JT": (96, B), "JT1": (256, B), "K2": (256, B),
-    "OD": (32, B), "thr": (64, F), "nt": (64, B), "iv": (64, B), "n2": (128, F), "qt": (64, F), "tr": (64, F), "mA": (64, F), "FX": (96, F), "G8": (8, F),
-    "X": (48 * R, B), "RP": (256 * R, B), "SV": (256 * R, B), "b8": (16, F), "C": (272, B), "CU": (256, B), "YE": (256, B), "NZ": (256, F),
-    "AB": (576, I), "MM": (288, I), "SS": (576, I), "HU": (576, U), "zi": (16, I), "zu": (16, U),
-    "FF": (7680, B), "FD": (1536, B), "mh": (288, F), "sl": (256, F), "SU": (256, U), "su2": (16, U), "G2": (4096, B), "MS": (4096, B),
-    "sq": (512, B), "sg": (512, B), "ta": (16, F), "tu": (16, U), "t256": (256, F), "tp": (272, F),
-    "EVg": (256, B), "M5": (256, B), "D": (272, B), "good": (256, B), "pre": (256, B), "junk": (1024, B), "acc": (4, F), "ix": (4, U),
+    "pi": (8, I), "pc": (24, F), "qg": (128, F), "qq": (256, F), "jm": (256, F), "ri": (32, I), "rj": (32, I), "wt16": (32, F),
+    "BO": (128, B), "ID": (128, B), "IDF": (128, F), "IQ": (128, F), "I8": (128, B), "In22": (128, B), "In1": (128, B), "BO1k": (128, B),
+    "BOz": (128, B), "BOh": (128, B), "BOn": (128, B), "LD": (128, B), "DG": (128, B), "PK": (128, B), "WB": (512, B), "D16": (256, B), "LK": (2048, B),
+    "tg": (16, F), "ti": (48, I), "TGh": (128, B), "TGl": (128, B), "ph": (16, F), "N15": (256, B),
+    "EXi": (16, I), "EX": (16, U), "RM": (1024, B), "RZ": (256, B), "ONE": (256, B), "JT": (96, B), "JT1": (256, B), "K2": (256, B),
+    "OD": (32, B), "thr": (64, F), "nt": (64, B), "iv": (64, B), "qt": (64, F), "tr": (64, F), "mA": (64, F), "FX": (96, F), "G8": (8, F),
+    "X": (48 * R, B), "RP": (256 * R, F), "SV": (256 * R, F), "b8": (16, F), "C": (272, B), "CU": (256, B), "YE": (256, B), "sp": (16, B), "vp": (16, F),
+    "AB": (576, I), "MM": (288, I), "SS": (576, I), "HU": (336, U), "zi": (16, I), "zu": (16, U),
+    "FF": (3840, B), "FU": (768, B), "FO": (1024, B), "df": (288, F), "sl": (288, F), "SU": (288, U), "nx": (48, F), "G2": (4096, F), "MS": (4096, F),
+    "fo": (64, F), "fm": (32, F), "KO": (32, F), "ta": (16, F), "tu": (16, U), "t256": (272, F), "tp": (272, F), "M": (256, B), "NG": (256, B), "N5": (256, B),
+    "TH": (256, B), "BOp": (128, B), "BO8": (128, B), "M5": (256, B), "D": (272, B), "good": (256, B), "pre": (256, B), "junk": (1024, B), "acc": (4, F), "ix": (4, U),
     "tB": (64, F), "tm": (64, F), "tA": (64, F), "eq": (256, B), "nd": (64, F), "so": (4, U), "Ce": (64, B),
     "PS": (256, B), "PB": (256, F), "nb": (64, B), "qc": (64, F), "ov": (64, B), "rm": (4, F), "KB": (256, F), "KA": (256, F), "cm": (4096, B),
     "pl": (4, F), "po": (2, U), "zs": (512, F), "vo": (2, U),
 }
-SCRATCH = {k: ("sbuf", [128, n], d) for k, (n, d) in _SB.items()}
 for _k in range(8):
-    SCRATCH["p%d" % _k] = ("psum", [128, 512], F)
+    _SB["p%d" % _k] = (512, F)
+_AT, _end = {}, 0
+for _k, (_n, _d) in _SB.items():
+    if _d == F and _n <= 64:
+        _AT[_k] = ("few", _end)
+        _end += -(-_n // 16) * 16
+    else:
+        _AT[_k] = (_k, 0)
+SCRATCH = {k: ("psum" if k[1:].isdigit() and k[0] == "p" else "sbuf", [128, n], d) for k, (n, d) in _SB.items() if _AT[k][0] == k}
+SCRATCH["few"] = ("sbuf", [128, _end], F)
 SEMAPHORES = ["V", "A", "P", "G"] + ["d%d" % k for k in range(24)] + [a + str(r) for a in ("lo", "up", "rp", "ls", "lr") for r in range(R)]
 
 
@@ -47,8 +59,10 @@ def rank_program(g, core, T, topo):
     ops, hist, bank, lastq, soft, line = [], {}, {}, {}, [], {}
 
     def c(name, lo=0, hi=None, step=1, rows=None):
+        hi = _SB[name][0] if hi is None else hi
+        name, base = _AT[name]
+        lo, hi = lo + base, hi + base
         where, shape, dt = SCRATCH[name]
-        hi = shape[1] if hi is None else hi
         ps = slice(0, 128) if rows is None else rows
         return (T[name][ps, lo:hi:step] if step != 1 else T[name][ps, lo:hi], [(name, lo, hi)], [], len(range(lo, hi, step)), dt in (B, U), where == "psum", False)
 
@@ -87,21 +101,21 @@ def rank_program(g, core, T, topo):
             order.add(lastq[eng])
         if size:
             lastq[eng] = k
-        ops.append(dict(eng=eng, deps=deps, order=order, call=call, dur=dur, sem=sem or eng, inc=inc, chain=chain, lat=lat, size=size))
+        ops.append(dict(eng=eng, deps=deps, order=order, ghost=set(), call=call, dur=dur, sem=sem or eng, inc=inc, chain=chain, lat=lat, size=size))
         return k
 
     def issue():
         n = len(ops)
         succ, more = [[] for _ in ops], [[] for _ in ops]
         for k, o in enumerate(ops):
-            for j in o["deps"] | o["order"]:
+            for j in o["deps"] | o["order"] | o["ghost"]:
                 succ[j].append(k)
         for a, b in soft:
             more[a].append(b)
-        pre = [sorted(o["deps"]) for o in ops]
+        pre = [sorted(o["deps"] | o["ghost"]) for o in ops]
         aft = [sorted(o["order"]) for o in ops]
 
-        def run(p, took, reach=0.0, shift=()):
+        def run(p, took, reach=0.0, shift=(), times=False):
             dur = [o["dur"][0] + p[0] * (o["dur"][1] + p[1] * o["dur"][2] + SCA * o["dur"][3]) + p[2] * o["dur"][4] for o in ops]
             lat = [o["lat"][0] * p[4] + o["lat"][1] for o in ops]
             hop, make = p[3], not took
@@ -114,7 +128,7 @@ def rank_program(g, core, T, topo):
                 for k in range(n - 1, -1, -1):
                     prio[k] = dur[k] + lat[k] + ops[k]["size"] / 200.0 + max([prio[j] + hop for j in succ[k]] + [prio[j] for j in more[k]], default=0.0)
                 prio = [x + y for x, y in zip(prio, shift)]
-                left = [len(o["deps"] | o["order"]) for o in ops]
+                left = [len(o["deps"] | o["order"] | o["ghost"]) for o in ops]
                 ready = {e: {} for e in free}
                 for k in range(n):
                     if left[k] == 0:
@@ -140,21 +154,54 @@ def rank_program(g, core, T, topo):
                         left[j] -= 1
                         if left[j] == 0:
                             ready[ops[j]["eng"]][j] = at(j)
-            return max(done)
+            return (start, done, dur) if times else max(done)
+
+        def pack(order, edges, dur, least):
+            at, lo, hi = [0.0] * n, {e: [] for e in Q}, {e: [] for e in Q}
+            for k in order:
+                t = max([at[j] + lag for j, lag in edges[k]] + [least[k]])
+                e = ops[k]["eng"]
+                if e is not None:
+                    a, b = lo[e], hi[e]
+                    i = len(a)
+                    while i > 0 and b[i - 1] > t:
+                        i -= 1
+                    while i < len(a) and t + dur[k] > a[i]:
+                        t = max(t, b[i])
+                        i += 1
+                    a.insert(i, t)
+                    b.insert(i, t + dur[k])
+                at[k] = t
+            return at
+
+        def justify(p, took, noise):
+            start, done, dur = run(p, took, times=True)
+            fore, back = [[] for _ in ops], [[] for _ in ops]
+            for k in range(n):
+                for j, lag in [(j, done[j] - start[j] + p[3]) for j in pre[k]] + [(j, done[j] - start[j] if ops[k]["eng"] is None else dur[j]) for j in aft[k]]:
+                    fore[k].append((j, lag))
+                    back[j].append((k, dur[k] + lag - dur[j]))
+            late = pack(sorted(range(n), key=lambda k: (-start[k] - dur[k], -k)), back, dur, [done[k] - start[k] - dur[k] for k in range(n)])
+            key = [-late[k] - dur[k] + noise[k] for k in range(n)]
+            for k in range(n):
+                key[k] = max([key[k]] + [key[j] for j, _ in fore[k]])
+            early = pack(sorted(range(n), key=lambda k: (key[k], k)), fore, dur, [0.0] * n)
+            return sorted(range(n), key=lambda k: (early[k], k))
 
         best = None
         rs = np.random.RandomState(1)
         for t in range(TRIES):
-            took = []
             if t < 12:
-                how = (PLANS[t % 4], (0.5, 1.0, 2.0)[t // 4], [0.0] * n)
+                took = []
+                run(PLANS[t % 4], took, (0.5, 1.0, 2.0)[t // 4], [0.0] * n)
+                for _ in range(3):
+                    took = justify(PLANS[t % 4], took, [0.0] * n)
             else:
                 lo = int(rs.randint(n))
-                how = (best[2][0], best[2][1], [x + (AMP * float(rs.randn()) if lo <= k < lo + SPAN else 0.0) for k, x in enumerate(best[2][2])])
-            run(how[0], took, how[1], how[2])
+                took = justify(PLANS[t % 4], best[1], [AMP * float(rs.randn()) if lo <= k < lo + SPAN else 0.0 for k in range(n)])
             worth = sum(run(p, took) / p[5] for p in PLANS)
             if best is None or worth < best[0]:
-                best = (worth, took, how)
+                best = (worth, took)
         seq = {e: [k for k in best[1] if ops[k]["eng"] == e] for e in Q}
         top, val = {}, {}
         for k in [k for e in Q for k in seq[e]] + [k for k in range(n) if ops[k]["eng"] is None]:
@@ -259,9 +306,12 @@ def rank_program(g, core, T, topo):
     dma("Y", c("ec"), T.ex[row0, :], 1 << 16)
     dma("Y", c("sti"), T.st[:], 1 << 17)
     parts_e = []
-    for k in range(8):
-        rows = slice(16 * k + 1, 16 * k + 16)
-        parts_e.append(dma("Y", c("E", 0, W, rows=rows), T.ex[rows, :], 15 << 13, skip=list(parts_e)))
+
+    def load_e(groups):
+        for k in groups:
+            rows = slice(16 * k + 1, 16 * k + 16)
+            parts_e.append(dma("Y", c("E", 0, W, rows=rows), T.ex[rows, :], 15 << 13, skip=list(parts_e)))
+    load_e(range(5))
     iota(c("pi", 0, 1), [[0, 1]], 0, 1)
     iota(c("qq"), [[1, 256]], 0, 0)
     iota(c("jm"), [[0, 16], [1, 16]], 0, 0)
@@ -270,20 +320,27 @@ def rank_program(g, core, T, topo):
     iota(c("EXi"), [[1, 16]], 0, 0)
     iota(c("ri", 0, 16), [[-1, 16]], 16, 1)
     iota(c("ri", 16, 32), [[1, 16]], 128, -1)
-    act(c("PLC", 0, 256), c("qq"), Fn.Copy)
+    act(c("PLC", PO, PO + 256), c("qq"), Fn.Copy)
     for k in (256, 512, 1024, 2048):
-        act(c("PLC", k, 2 * k), c("PLC", 0, k), Fn.Identity, bias=float(k))
-    act(c("PLC", W, 4192), c("PLC", 0, 96), Fn.Identity, bias=float(W))
-    ms(c("S", W, W + 16), -1.0)
-    ms(c("S", W + 16, ZERO), 255.0)
-    ms(c("S", ZERO, 4432), 0.0)
+        act(c("PLC", PO + k, PO + 2 * k), c("PLC", PO, PO + k), Fn.Identity, bias=float(k))
+    act(c("PLC", PO + W, PO + 4192), c("PLC", PO, PO + 96), Fn.Identity, bias=float(W))
+    ms(c("PLC", 0, PO), 2.0 ** 28)
+    ms(c("S", W, 4176), -1.0)
     ms(c("E", W, 4176), 240.0)
+    ms(c("VT", W, 4128), 2.0 ** 25)
     ms(c("RZ"), 1.0)
     ms(c("ONE"), 1.0)
     ms(c("RZ", 0, 256, 16), 0.0)
     ts(c("pi", 1, 2), c("pi", 0, 1), 15, Op.bitwise_and)
     ts(c("pi", 2, 3), c("pi", 0, 1), 4, Op.arith_shift_right)
+    ts(c("pi", 3, 4), c("pi", 0, 1), 1, Op.arith_shift_right)
+    ts(c("pi", 4, 5), c("pi", 0, 1), 1, Op.bitwise_and)
     cp(c("pc", 0, 3), c("pi", 0, 3))
+    cp(c("pc", 16, 17), c("pi", 3, 4))
+    ts(c("pc", 17, 18), c("pi", 4, 5), -65280.0, Op.mult, 65536.0, Op.add)
+    ts(c("pc", 18, 19), c("pi", 4, 5), 65280.0, Op.mult, -65536.0, Op.add)
+    ts(c("PK", 0, 128, 2), c("qq", 0, 64), c("pc", 16, 17), Op.is_equal, c("pc", 17, 18), Op.mult)
+    ts(c("PK", 1, 128, 2), c("qq", 0, 64), c("pc", 16, 17), Op.is_equal, c("pc", 18, 19), Op.mult)
     pcol, lcol, gcol = c("pc", 0, 1), c("pc", 1, 2), c("pc", 2, 3)
     ts(c("BO1k"), c("qg"), gcol, Op.is_equal, 1024.0, Op.mult)
     ts(c("ID"), c("qq", 0, 128), pcol, Op.is_equal)
@@ -305,7 +362,8 @@ def rank_program(g, core, T, topo):
     ts(c("p3", 0, 256), c("ec"), 1.0, Op.add)
     tt(c("p3", 0, 256), c("p3", 0, 256), c("f1"), Op.mult)
     tt(c("fx"), c("p3", 0, 256), c("ec"), Op.add)
-    dma("Y", c("E", 0, W, rows=row0), c("fx"), 1 << 16, skip=parts_e)
+    parts_e.append(dma("Y", c("E", 0, W, rows=row0), c("fx"), 1 << 16, skip=list(parts_e)))
+    load_e(range(5, 8))
     dma("Y", c("ENV"), T.env[:], 1 << 19)
     cp(c("EX"), c("EXi"))
     ts(c("BO"), c("BO1k"), 1.0 / 1024, Op.mult)
@@ -331,12 +389,24 @@ def rank_program(g, core, T, topo):
     ts(c("ti", 16, 32), c("ti", 0, 16), 0xFF00, Op.bitwise_and)
     ts(c("ti", 32, 48), c("ti", 0, 16), 0xFF, Op.bitwise_and)
     for name, lo in (("TGh", 16), ("TGl", 32)):
-        ts(c(name, 0, 32, 2), c("ti", lo, lo + 16), -1.0, Op.mult)
-        ts(c(name, 1, 32, 2), c("ti", lo, lo + 16), -1.0, Op.mult)
-        for k in (32, 64, 128):
+        ts(c(name, 0, 16), c("ti", lo, lo + 16), -1.0, Op.mult)
+        for k in (16, 32, 64):
             cp(c(name, k, 2 * k), c(name, 0, k))
-    ms(c("RM"), 0.0)
-    ms(c("RM", 0, 1536, 16), 255.0)
+    mm(c("p0", 0, 16), c("PK"), c("D16", 0, 16), True, True)
+    cp(c("ph"), c("p0", 0, 16))
+    ts(c("pc", 19, 20), c("p0", 15, 16), -1.0, Op.mult)
+    ms(c("RM", 0, 1), 2.0 ** 26)
+    tt(c("RM", 1, 16), c("ph", 0, 15), c("ph", 1, 16), Op.subtract)
+    for k in (16, 32, 64, 128, 256, 512):
+        cp(c("RM", k, 2 * k), c("RM", 0, k))
+    ts(c("N15"), c("ONE"), lcol, Op.mult, 15.0, Op.is_equal)
+    ts(c("N15"), c("N15"), -1.0, Op.mult)
+    ts(c("IQ"), c("IDF"), -2.0 ** -14, Op.mult)
+    ts(c("BOn"), c("BO"), -2.0 ** 30, Op.mult)
+    ms(c("KO", 0, 16), -PEN)
+    ms(c("KO", 16, 32), -4 * PEN)
+    ms(c("nx"), 0.0)
+    ms(c("FU", 256, 768), 1.0)
     ts(c("OD"), c("D16", 0, 32), 2.0 ** 25, Op.mult, -2.0 ** 25, Op.add)
     ms(c("FX"), 0.0)
     for h, k in ((0, 1), (48, 0)):
@@ -366,19 +436,26 @@ def rank_program(g, core, T, topo):
     emit("G", [c("thb")], [c("thi")], lambda: g.partition_broadcast(T.thb[:], T.thi[0:1, :], 128), (180, 0, 0, 0, 0))
     tt(c("thf"), c("thb"), c("G8"), Op.mult)
     red(c("thc", 0, 1), c("thf"), Op.add)
-    ts(c("thc", 1, 2), c("thc", 0, 1), 16384.0, Op.add)
+    ts(c("thc", 1, 2), c("thc", 0, 1), -0.5, Op.add)
     ms(c("C", 256, 272), 0.0)
     ms(c("D", 256, 272), 0.0)
-    ms(c("tp", 256, 272), 8000.0)
-    if above is None:
-        ms(c("FD"), 1.0)
+    ms(c("tp" if below is not None else "t256", 256, 272), 8000.0)
+    if below is not None:
+        cp(c("pi", 5, 6), c("thc", 0, 1))
+        ts(c("pi", 6, 7), c("pi", 5, 6), 4032, Op.bitwise_and)
+        ts(c("pi", 7, 8), c("pi", 5, 6), 63, Op.bitwise_and)
+        cp(c("pc", 20, 22), c("pi", 6, 8))
+        for k in (0, 1):
+            ts(c("TH", 128 * k, 128 * k + 128), c("I8"), c("pc", 20 + k, 21 + k), Op.mult)
+        ts(c("BOp"), c("BO"), 2.0 ** 30, Op.mult)
+        ts(c("BO8"), c("BO"), -8192.0, Op.mult)
     for r in range(R):
         if below is None:
             ms(c("X", 48 * r, 48 * r + 16), 240.0)
         if above is None:
             ms(c("X", 48 * r + 32, 48 * r + 48), 240.0)
 
-    Ew, Sw, Pw = c("E"), c("S"), c("PLC")
+    Ew, Sw, Vw, Pw = c("E"), c("S"), c("VT"), c("PLC", PO)
 
     def keys(r, lo, hi):
         for bk in ("p7", "p6"):
@@ -432,18 +509,33 @@ def rank_program(g, core, T, topo):
         ts(c("SS", o + n, o + 2 * n), m, 9, Op.arith_shift_right)
         tt(s, s, ab, Op.add)
         ts(s, s, 4095, Op.bitwise_and)
-        if o == XC:
-            cp(c("HU", o, o + 2 * n), s)
-        else:
-            cp(c("HU", o, o + 2 * n, 2), c("SS", o, o + n))
-            cp(c("HU", o + 1, o + 2 * n, 2), c("SS", o + n, o + 2 * n))
+        m = 2 * n if o == XC else n
+        cp(c("HU", o // 2, o // 2 + m), c("SS", o, o + m))
 
     def wmm(o, k, x):
         return [(o, c("WB", 128 * k, 128 * k + 128), x), (o, c("WB", 128 * k + 256, 128 * k + 384), x)]
 
-    def col(p, home):
-        p0, p1 = [h for h in HC if h[0] <= p < h[1]][0]
-        return 32 * p0 + 16 * (p1 - p0) * home + 16 * (p - p0)
+    def choose(z, h2, lo, n):
+        sl = c("sl", lo, lo + n)
+        ts(z, z, 0.0, Op.is_equal)
+        tt(sl, z, c("df", lo, lo + n), Op.mult)
+        tt(z, h2, sl, Op.add)
+        ts(c("SU", lo, lo + n), z, float(NEUTRAL), Op.min)
+
+    def begin_vt():
+        for k, bk in enumerate(EARLY):
+            mm(c(bk), c("ID"), c("S", 512 * k, 512 * k + 512), True, False)
+
+    def finish_vt():
+        for k, (bk, e) in enumerate([(x, None) for x in EARLY] + list(LATE)):
+            vt = c("VT", 512 * k, 512 * k + 512)
+            if e == "A":
+                mm(c(bk), c("ID"), c("S", 512 * k, 512 * k + 512), True, False)
+            mm(c(bk), c("PK"), c("E", 512 * k, 512 * k + 512), e == "V", True)
+            if e == "V":
+                tt(vt, c(bk), c("S", 512 * k, 512 * k + 512), Op.add)
+            else:
+                act(vt, c(bk), Fn.Copy)
 
     def decode(bk, at, buf, lo, n):
         return [(c(bk, at, at + n), c("LK", 128 * k, 128 * k + 128), c(buf, 16 * lo + k, 16 * (lo + n), 16)) for k in range(16)]
@@ -468,9 +560,14 @@ def rank_program(g, core, T, topo):
         if r == R - 1:
             dma("Y", c("ec"), c("E", 0, W, rows=row0), 1 << 16)
             ts(c("f2"), c("ec"), 0.0, Op.is_ge, 2.0, Op.mult)
-            ts(c("p3", 0, 256), c("ec"), -2.0, Op.is_le)
-            tt(c("yc"), c("p3", 0, 256), c("f2"), Op.add)
+            ts(c("f1"), c("ec"), -2.0, Op.is_le)
+            tt(c("yc"), c("f1"), c("f2"), Op.add)
             dma("Y", c("ST", 0, W, rows=row0), c("yc"), 1 << 17)
+        if r:
+            act(c("sp"), ind(Sw, c("po", 0, 1)), Fn.Copy)
+            mms([(c("p2", 0, 16), c("PK"), par), (c("p2", 0, 16), c("ID"), c("sp"))])
+            act(c("vp"), c("p2", 0, 16), Fn.Copy)
+            cp(ind(Vw, c("po", 0, 1)), c("vp"))
         for k, (p0, p1) in enumerate(HC):
             n, o, bk = 16 * (p1 - p0), 32 * p0, ("p0", "p6")[k % 2]
             tt(c("C", 16 * p0, 16 * p1), ind(par, c("EX", p0, p1)), c("D16", 0, n), Op.add)
@@ -479,7 +576,6 @@ def rank_program(g, core, T, topo):
             ts(c("AB", o, o + n), c(bk, 0, n), c("wf", 7, 8), Op.add)
             ts(c("AB", o + n, o + 2 * n), c(bk, n, 2 * n), c("wf", 6, 7), Op.add)
             hash_tail(o, n)
-        act(c("NZ", 0, 16 * SC[-1][0]), c("C", 0, 16 * SC[-1][0]), Fn.Identity, bias=float(NEUTRAL))
         if r == 0:
             ts(c("f2"), c("PB"), 4096.0, Op.is_lt)
             red(c("rm", 1, 2), c("f2"), Op.add)
@@ -487,81 +583,70 @@ def rank_program(g, core, T, topo):
             ts(c("rm", 0, 1), c("rm", 1, 2), 256.0, Op.min)
         if r < 2:
             stayers(r, 0, (256, 96)[r])
+        if r == 0:
+            finish_vt()
+        act(c("p5", 0, 240), c("C", 0, 240), Fn.Relu, bias=float(NEUTRAL), scale=-float(NEUTRAL))
+        for p0, p1 in HC:
+            n, o, h2 = 16 * (p1 - p0), 32 * p0, c("p5", 16 * p0, 16 * p1)
+            tt(h2, h2, c("SS", o + n, o + 2 * n), Op.max)
+            tt(c("df", 16 * p0, 16 * p1), c("SS", o, o + n), h2, Op.subtract)
+        mms([(c("p3", 0, 240), c("PK"), c("N15", 0, 240)), (c("p3", 0, 240), c("PK"), c("C", 0, 240))])
 
-        def fetch(c0, c1, on_a=0):
-            mid = c1 - on_a
-            for a, b in ((c0, mid), (mid, c1)):
-                if a < b:
+        def fetch(c0, c1, on_v):
+            mid = c1 - on_v
+            for lo, hi in ((c0, mid), (mid, c1)):
+                for a in range(lo, hi, FETCH):
+                    b = min(a + FETCH, hi)
                     o = c("G2", 16 * a, 16 * b)
-                    if a == mid:
-                        act(o, ind(Sw, c("SU", a, b)), Fn.Copy)
+                    if lo == mid:
+                        cp(o, ind(Vw, c("SU", a, b)))
                     else:
-                        cp(o, ind(Sw, c("SU", a, b)))
-                    scan(c("MS", 16 * a, 16 * b), c("RM", 0, 16 * (b - a)), o, 0.0, Op.max, Op.min)
+                        act(o, ind(Vw, c("SU", a, b)), Fn.Copy)
+                        follow("A")
+                    scan(c("MS", 16 * a, 16 * b), c("RM", 0, 16 * (b - a)), o, 0.0, Op.add, Op.min)
                     follow("V")
 
         def piece(k):
             p0, p1 = SC[k]
-            n, bk, b3, c0 = 16 * (p1 - p0), ("p1", "p2")[k % 2], 256 * (k % 2), 16 * p0
+            n, bk, c0 = 16 * (p1 - p0), ("p1", "p2")[k % 2], 16 * p0
             for p in range(p0, p1):
-                act(c("FF", 512 * p, 512 * p + 512), ind(Ew, c("HU", 32 * p, 32 * p + 32)), Fn.Square, bias=c("b8", p, p + 1), scale=8.0)
+                act(c("FF", 256 * p, 256 * p + 256), ind(Ew, c("HU", 16 * p, 16 * p + 16)), Fn.Square, bias=c("b8", p, p + 1), scale=8.0)
                 follow("A")
-            o1, o2 = col(p0, 0), col(p0, 1)
-            mms([(c(bk, 0, 2 * n), c("ID"), c("TGh", 0, 2 * n)), (c(bk, 0, 2 * n), c("ID"), c("TGl", 0, 2 * n))]
-                + [x for q in range(p0, p1, 2) for x in decode(bk, 32 * (q - p0), "FF", 32 * q, 32 * (min(q + 2, p1) - q))])
-            x1, sl = c("p3", b3, b3 + 2 * n, 2), c("sl", c0, c0 + n)
-            ts(c("p3", b3, b3 + 2 * n), c(bk, 0, 2 * n), 0.0, Op.not_equal, PEN, Op.mult)
-            last = k == len(SC) - 1
-            if last:
-                act(c("n2", 0, n), c("C", c0, c0 + n), Fn.Identity, bias=NEUTRAL - PEN, scale=PEN)
-                tt(sl, c("SS", o1, o1 + n), c("n2", 0, n), Op.min)
-            tt(x1, x1, sl if last else c("SS", o1, o1 + n), Op.add)
-            tt(c("mh", c0, c0 + n), c("p3", b3 + 1, b3 + 2 * n, 2), c("SS", o2, o2 + n), Op.add)
-            tt(x1, x1, c("mh", c0, c0 + n), Op.min)
-            if last:
-                ts(c("SU", c0, c0 + n), x1, float(ZERO), Op.min)
-            else:
-                tt(sl, x1, c("NZ", c0, c0 + n), Op.min)
-                cp(c("SU", c0, c0 + n), sl)
-            fetch(c0, c0 + n, ON_A.get(k, 0))
+            mms([(c(bk, 0, n), c("ID"), c("TGh", 0, n)), (c(bk, 0, n), c("ID"), c("TGl", 0, n))] + decode(bk, 0, "FF", c0, n))
+
+        def resolve(k):
+            p0, p1 = SC[k]
+            n, bk, c0 = 16 * (p1 - p0), ("p1", "p2")[k % 2], 16 * p0
+            choose(c(bk, 0, n), c("p5", c0, c0 + n), c0, n)
+            fetch(c0, c0 + n, ON_V[k])
 
         def extras():
-            x3, x2 = c("X", xo, xo + 48), c("X", xo, xo + 32)
-            mms(wmm(c("p5", 0, 48), 1, x3))
-            mms(wmm(c("p5", 48, 96), 0, x3))
+            x3, x2, hu = c("X", xo, xo + 48), c("X", xo, xo + 32), XC // 2
+            mms(wmm(c("p7", 0, 48), 1, x3))
+            mms(wmm(c("p7", 48, 96), 0, x3))
             for h, k in ((0, 1), (32, 0)):
-                mms([(c("p4", h, h + 32), c("ID"), c("OD"))] + wmm(c("p4", h, h + 32), k, x2))
-            cp(c("C", 240, 256), rp)
-            act(c("NZ", 240, 256), rp, Fn.Identity, bias=float(NEUTRAL))
+                mms([(c("p7", 96 + h, 128 + h), c("ID"), c("OD"))] + wmm(c("p7", 96 + h, 128 + h), k, x2))
             for h in (0, 1):
-                red(c("p5", 48 * h + 31, 48 * h + 32), c("p4", 32 * h, 32 * h + 16), Op.max)
-                red(c("p5", 48 * h + 47, 48 * h + 48), c("p4", 32 * h + 16, 32 * h + 32), Op.max)
-            tt(c("AB", XC, XC + 96), c("p5", 0, 96), c("FX"), Op.add)
+                red(c("p7", 48 * h + 31, 48 * h + 32), c("p7", 96 + 32 * h, 112 + 32 * h), Op.max)
+                red(c("p7", 48 * h + 47, 48 * h + 48), c("p7", 112 + 32 * h, 128 + 32 * h), Op.max)
+            tt(c("AB", XC, XC + 96), c("p7", 0, 96), c("FX"), Op.add)
             hash_tail(XC, 48)
-            ts(c("zi"), c("MM", XC // 2 + 16, XC // 2 + 32), 7, Op.arith_shift_right, 2047, Op.bitwise_and)
-            cp(c("zu"), c("zi"))
+            cp(c("C", 240, 256), rp)
+            act(c("nx", 0, 16), rp, Fn.Relu, bias=float(NEUTRAL), scale=-float(NEUTRAL))
+            h2 = c("p7", 192, 240)
+            tt(h2, c("SS", XC + 48, XC + 96), c("nx"), Op.max)
+            tt(c("df", 240, 288), c("SS", XC, XC + 48), h2, Op.subtract)
             tt(c("YE"), ind(rp, c("EX")), c("D16"), Op.subtract)
             if above is not None:
                 tt(c("CU", 0, 240), ind(up, c("EX", 0, 15)), c("D16", 0, 240), Op.add)
                 cp(c("CU", 240, 256), par)
-            for h in (0, 1):
-                o, f = XC + 48 * h, 768 * h
-                if above is not None:
-                    tt(c("FD", f + 512, f + 768), ind(Ew, c("HU", o + 32, o + 48)), c("CU"), Op.not_equal)
-                tt(c("FD", f, f + 256), ind(Ew, c("HU", o, o + 16)), c("YE"), Op.not_equal)
-                act(c("FD", f + 256, f + 512), ind(Ew, c("HU", o + 16, o + 32)), Fn.Abs, bias=1.0)
-            mms(decode("p0", 0, "FD", 0, 96))
-            x1 = c("p5", 128, 176)
-            ts(c("p5", 128, 224), c("p0", 0, 96), 0.0, Op.not_equal, PEN, Op.mult)
-            ts(c("ta"), c("p0", 16, 32), 0.0, Op.is_equal, PEN, Op.mult)
-            tt(c("mh", 240, 288), c("p5", 176, 224), c("SS", XC + 48, XC + 96), Op.add)
-            tt(x1, x1, c("SS", XC, XC + 48), Op.add)
-            tt(c("mh", 256, 272), c("mh", 256, 272), c("ta"), Op.add)
-            tt(x1, x1, c("mh", 240, 288), Op.min)
+                tt(c("FU", 512, 768), ind(Ew, c("HU", hu + 32, hu + 48)), c("CU"), Op.not_equal)
+            tt(c("FU", 0, 256), ind(Ew, c("HU", hu, hu + 16)), c("YE"), Op.not_equal)
+            mms(decode("p0", 0, "FU", 0, 48))
+            choose(c("p0", 0, 48), h2, 240, 48)
             if above is not None:
                 sv = c("SV", 256 * r, 256 * r + 256)
-                ts(c("su2"), c("p5", 160, 176), float(ZERO), Op.min)
-                act(sv, ind(Sw, c("su2")), Fn.Copy)
+                act(sv, ind(Vw, c("SU", 272, 288)), Fn.Identity, bias=c("pc", 19, 20))
                 rid, pid, _ = topo.addr(above)
                 back = emit("G", [], [sv], lambda: g.remote_dma(T.RP[:, 256 * r:256 * r + 256], sv[0], T.sem["rp%d" % r], T.sem["lr%d" % r], pid, rid, topo.mask(core, above)),
                             (500, 0, 0, 0, 0), sem="lr%d" % r, inc=len(topo.engines(core, above)), chain=False, lat=(1, 2000))
@@ -569,42 +654,72 @@ def rank_program(g, core, T, topo):
                 back = len(ops) - 1
             if below is not None:
                 landed(c("RP", 256 * r, 256 * r + 256), "rp%d" % r, len(topo.engines(below, core)), back, (0 if above is not None else 1, 0))
-            tt(c("sl", 240, 256), c("p5", 128, 144), c("NZ", 240, 256), Op.min)
-            cp(c("SU", 240, 256), c("sl", 240, 256))
-            ts(c("tu"), c("p5", 144, 160), float(NEUTRAL), Op.min)
-            fetch(240, 256)
-            act(c("t256"), ind(Pw, c("tu")), Fn.Copy)
-            act(c("EVg"), ind(c("ENV"), c("zu")), Fn.Copy)
+            fetch(240, 256, ON_V[len(SC)])
+            mms([(c("p3", 240, 256), c("PK"), c("N15", 0, 16)), (c("p3", 240, 256), c("PK"), c("C", 240, 256))])
+            ts(c("zi"), c("MM", XC // 2 + 16, XC // 2 + 32), 7, Op.arith_shift_right, 2047, Op.bitwise_and)
+            cp(c("zu"), c("zi"))
             for h in (0, 1):
-                mms([(c("p4", 256 * h, 256 * h + 256), c("In1"), c("C", 0, 256)),
-                     (c("p4", 256 * h, 256 * h + 256), c("ID"), c("FD", 768 * h + 256, 768 * h + 512))])
-            act(c("sq"), c("p4"), Fn.Square, bias=-1.0)
-            mm(c("p4"), c("BO"), c("sq"), True, True)
-            act(c("sg"), c("p4"), Fn.Sign)
+                fd, z = c("FO", 512 * h, 512 * h + 256), c("p4", 256 * h, 256 * h + 256)
+                act(fd, ind(Ew, c("HU", hu + 48 * h + 16, hu + 48 * h + 32)), Fn.Abs, bias=1.0)
+                mms([(z, c("In1"), c("C", 0, 256)), (z, c("ID"), fd)])
+            for h in (0, 1):
+                act(c("FO", 512 * h + 256, 512 * h + 512), c("p4", 256 * h, 256 * h + 256), Fn.Square, bias=-1.0)
+            mms(decode("p4", 0, "FO", 0, 64))
+            ts(c("fo"), c("p4", 0, 64), 0.0, Op.is_equal)
+            tt(c("ta"), c("fo", 0, 16), c("df", 256, 272), Op.mult)
+            tt(c("fm"), c("fo", 0, 32), c("fo", 32, 64), Op.max)
+            tt(c("ta"), c("ta"), c("SS", XC + 64, XC + 80), Op.add)
+            tt(c("fm"), c("fm"), c("KO"), Op.mult)
+            tt(c("fm", 0, 16), c("fm", 0, 16), c("fm", 16, 32), Op.add)
+            tt(c("ta"), c("ta"), c("fm", 0, 16), Op.add)
+            ts(c("tu"), c("ta"), PEN + PO, Op.add, float(NONE + PO), Op.min)
+            act(c("t256", 0, 256), ind(c("PLC"), c("tu")), Fn.Copy)
             return back
 
-        def lower(a, b):
-            M = c("MS", 16 * a + 15, 16 * b, 16)
-            if below is not None:
-                tt(c("M5", a, b), M, c("RP", 256 * r + a, 256 * r + b), Op.min)
-                mm(c("p7", a, b), c("BO"), c("M5", a, b), True, True)
-                tt(c("D", a, b), c("M5", a, b), c("EVg", a, b), Op.subtract)
-                ts(c("p5", 256 + a, 256 + b), c("p7", a, b), c("thc", 0, 1), Op.is_lt, 8192.0, Op.mult)
-                tt(c("tp", a, b), c("p5", 256 + a, 256 + b), c("t256", a, b), Op.add)
+        def first(a, b):
+            last, pack = c("MS", 16 * a + 15, 16 * b, 16), c("p3", a, b)
+            tt(c("M", a, b), last, pack, Op.subtract)
+            if a:
+                tt(c("NG", a, b), last, pack, Op.is_lt)
             else:
-                tt(c("D", a, b), M, c("EVg", a, b), Op.subtract)
-                cp(c("tp", a, b), c("t256", a, b))
+                act(c("NG", a, b), c("M", a, b), Fn.Relu, scale=-1.0)
+            if a == 240:
+                ts(c("M", a, b), c("M", a, b), 255.0, Op.min)
+
+        def count(a, b):
+            z = c("p6", a, b)
+            mms([(z, c("IQ"), c("t256", a, b)), (z, c("BOn"), c("NG", a, b)), (z, c("BO"), c("M", a, b))])
+            ts(c("good", a, b), z, c("thc", 1, 2), Op.is_ge)
+            scan(c("pre", a, b), c("good", a, b), c("good", a, b), c("pre", a - 1, a) if a else 0.0, Op.add, Op.max)
+
+        def lower(a, b):
+            env = ind(c("ENV"), c("zu", a // 16, b // 16))
+            if below is not None:
+                z = c("p7", a, b)
+                tt(c("M5", a, b), c("p0", 256 + a, 256 + b), c("M", a, b), Op.min)
+                mms([(z, c("TH", 0, 128), c("ONE", a, b)), (z, c("TH", 128, 256), c("ONE", a, b)), (z, c("BOp"), c("N5", a, b)), (z, c("BO8"), c("M5", a, b))])
+                tt(c("D", a, b), env, c("M5", a, b), Op.subtract)
+                tt(c("tp", a, b), z, c("t256", a, b), Op.max)
+            else:
+                tt(c("D", a, b), env, c("M", a, b), Op.subtract)
+                ops[-1]["ghost"].add(back)
 
         piece(0)
+        resolve(0)
         back = extras()
         for k in range(1, len(SC)):
             piece(k)
+            resolve(k)
         cut = 16 * SC[-1][0]
-        for a, b in ((0, cut), (cut, 256)):
-            mms([(c("p6", a, b), c("I8"), c("sg", a, b)), (c("p6", a, b), c("I8"), c("sg", 256 + a, 256 + b)), (c("p6", a, b), c("BO"), c("MS", 16 * a + 15, 16 * b, 16))])
-            ts(c("good", a, b), c("p6", a, b), c("thc", 1, 2), Op.is_ge)
-            scan(c("pre", a, b), c("good", a, b), c("good", a, b), c("pre", a - 1, a) if a else 0.0, Op.add, Op.max)
-        soft.append((back, len(ops)))
+        for a, b in ((240, 256), (0, cut), (cut, 240)):
+            first(a, b)
+        count(0, cut)
+        count(cut, 256)
+        if below is not None:
+            z = c("p0", 256, 512)
+            tt(z, c("p3", 0, 256), c("RP", 256 * r, 256 * r + 256), Op.subtract)
+            act(c("N5"), z, Fn.Relu)
+            act(z, z, Fn.Relu, scale=-1.0)
         lower(0, cut)
         lower(cut, 256)
         for k in range(4):
@@ -616,8 +731,9 @@ def rank_program(g, core, T, topo):
                 scan(junk, junk, junk, 0.0, Op.add, Op.max)
         ts(c("ix", 0, 2), c("acc", 0, 2), -0.5, Op.mult, 128.0, Op.add)
         cp(c("ix", 2, 4), c("junk", 767, 1024, 256))
-        tt(c("tm"), ind(c("tp"), c("ix")), c("mA"), Op.min)
-        tt(c("tB"), ind(c("tp"), c("ix")), c("tr"), Op.min)
+        tp = c("tp" if below is not None else "t256")
+        tt(c("tm"), ind(tp, c("ix")), c("mA"), Op.min)
+        tt(c("tB"), ind(tp, c("ix")), c("tr"), Op.min)
         act(c("PS", 32, 96), ind(c("D"), c("ix")), Fn.Abs)
         if r < R - 1:
             act(c("Ce"), ind(c("C"), c("ix")), Fn.Identity, bias=off, scale=sgn)
@@ -656,6 +772,7 @@ def rank_program(g, core, T, topo):
     act(c("PB"), ind(Pw, c("qo")), Fn.Copy)
     keys(0, 0, 256)
     ranks(0, 0, 256, 7)
+    begin_vt()
     for r in range(R):
         round_(r)
     dma("Y", T.ys[:], c("S", 0, W), 1 << 20)

@@ -3,18 +3,22 @@ from concourse.bass import DstId, RemoteDMATransfer
 from concourse.mybir import AluOpType as Op, AxisListType, ActivationFunctionType as Fn
 
 W, EV, R = 4096, 2048, 3
-HC = [(0, 4), (4, 15)]
+HC = [(0, 4), (4, 10), (10, 15)]
 SC = [(0, 4), (4, 8), (8, 12), (12, 15)]
-ON_V = {0: 32, 1: 16, 2: 16, 3: 24, 4: 0}
+ON_V = {0: 32, 1: 16, 2: 16, 3: 16, 4: 16}
+LEAD = 0
 FETCH = 32
 EARLY = ("p1", "p5", "p2", "p3", "p7")
 LATE = (("p4", "V"), ("p3", "V"), ("p7", "V"))
 XC = 480
 MUL, OFF, PEN = 32768.0, 9437184.0, 16384.0
 NEUTRAL, NONE, PO = 4112, 4176, 16
-PLANS = [(0.83, 1.3, 0.83, 110.0, 3600.0, 80.0), (0.9, 1.4, 0.9, 180.0, 4600.0, 95.0), (1.0, 1.6, 1.0, 170.0, 6600.0, 110.0), (1.1, 1.9, 1.1, 240.0, 4600.0, 125.0)]
+PLANS = [(0.87, 1.3, 0.87, 100.0, 2200.0, 80.0), (0.92, 1.5, 0.92, 140.0, 2600.0, 95.0), (1.0, 1.6, 1.0, 170.0, 1600.0, 105.0), (1.1, 1.8, 1.1, 200.0, 3000.0, 120.0)]
 SCA, AMP, SPAN = 3.8, 300.0, 150
-TRIES = 250
+TRIES = 1800
+SEED = 1
+EVERY = 7
+SLACK = 0.004
 B, F, I, U = "bfloat16", "float32", "int32", "uint16"
 _SB = {
     "E": (4176, B), "S": (4176, B), "VT": (4128, F), "ENV": (EV, B), "PLC": (PO + 4192, F), "ST": (4176, F),
@@ -53,10 +57,20 @@ def rank_program(g, core, T, topo):
     rank = T.rank_of(core)
     if rank is None:
         return
+    if not _ORDER:
+        program(g, T, topo, 1, True)
+    program(g, T, topo, rank, False)
+
+
+_ORDER = {}
+
+
+def program(g, T, topo, rank, plan):
+    core = T.cores[rank]
     below = T.cores[rank - 1] if rank > 0 else None
     above = T.cores[rank + 1] if rank + 1 < len(T.cores) else None
     Q = {"V": g.vector, "A": g.scalar, "P": g.tensor, "G": g, "Y": g.sync}
-    ops, hist, bank, lastq, soft, line = [], {}, {}, {}, [], {}
+    ops, hist, bank, lastq, soft, line, ahead, tag, seen = [], {}, {}, {}, [], {}, [], [-1], {}
 
     def c(name, lo=0, hi=None, step=1, rows=None):
         hi = _SB[name][0] if hi is None else hi
@@ -101,18 +115,33 @@ def rank_program(g, core, T, topo):
             order.add(lastq[eng])
         if size:
             lastq[eng] = k
-        ops.append(dict(eng=eng, deps=deps, order=order, ghost=set(), call=call, dur=dur, sem=sem or eng, inc=inc, chain=chain, lat=lat, size=size))
+        keys = [(tag[0], eng, sem, tuple(wr), tuple(rd)), (tag[0], eng, sem, tuple(wr))]
+        for x in keys:
+            seen[x] = seen.get(x, 0) + 1
+        ops.append(dict(eng=eng, deps=deps, order=order, keys=[(x, seen[x]) for x in keys], call=call, dur=dur, sem=sem or eng, inc=inc, chain=chain, lat=lat, size=size))
         return k
 
     def issue():
         n = len(ops)
+        for a, b in ahead:
+            ops[b]["order"].add(a)
+        rank_of, todo = {}, list(range(n - 1, -1, -1))
+        while todo:
+            k = todo[-1]
+            miss = [j for j in ops[k]["deps"] | ops[k]["order"] if j not in rank_of]
+            if miss:
+                todo.extend(sorted(miss, reverse=True))
+            else:
+                rank_of.setdefault(todo.pop(), len(rank_of))
+        ops[:] = [dict(ops[k], **{f: {rank_of[j] for j in ops[k][f]} for f in ("deps", "order")}) for k in sorted(range(n), key=rank_of.get)]
+        soft[:] = [(rank_of[a], rank_of[b]) for a, b in soft if rank_of[a] < rank_of[b]]
         succ, more = [[] for _ in ops], [[] for _ in ops]
         for k, o in enumerate(ops):
-            for j in o["deps"] | o["order"] | o["ghost"]:
+            for j in o["deps"] | o["order"]:
                 succ[j].append(k)
         for a, b in soft:
             more[a].append(b)
-        pre = [sorted(o["deps"] | o["ghost"]) for o in ops]
+        pre = [sorted(o["deps"]) for o in ops]
         aft = [sorted(o["order"]) for o in ops]
 
         def run(p, took, reach=0.0, shift=(), times=False):
@@ -128,7 +157,7 @@ def rank_program(g, core, T, topo):
                 for k in range(n - 1, -1, -1):
                     prio[k] = dur[k] + lat[k] + ops[k]["size"] / 200.0 + max([prio[j] + hop for j in succ[k]] + [prio[j] for j in more[k]], default=0.0)
                 prio = [x + y for x, y in zip(prio, shift)]
-                left = [len(o["deps"] | o["order"] | o["ghost"]) for o in ops]
+                left = [len(o["deps"] | o["order"]) for o in ops]
                 ready = {e: {} for e in free}
                 for k in range(n):
                     if left[k] == 0:
@@ -188,21 +217,92 @@ def rank_program(g, core, T, topo):
             early = pack(sorted(range(n), key=lambda k: (key[k], k)), fore, dur, [0.0] * n)
             return sorted(range(n), key=lambda k: (early[k], k))
 
-        best = None
-        rs = np.random.RandomState(1)
-        for t in range(TRIES):
+        fixed = [([o["dur"][0] + p[0] * (o["dur"][1] + p[1] * o["dur"][2] + SCA * o["dur"][3]) + p[2] * o["dur"][4] for o in ops],
+                  [o["lat"][0] * p[4] + o["lat"][1] for o in ops]) for p in PLANS]
+        eng, size = [o["eng"] for o in ops], [o["size"] for o in ops]
+
+        def times(i, took):
+            dur, lat = fixed[i]
+            hop, start, done, why, free, last, wire = PLANS[i][3], [0.0] * n, [0.0] * n, [-1] * n, {}, {}, 0.0
+            for k in took:
+                e, t, w = eng[k], 0.0, -1
+                for j in pre[k]:
+                    if done[j] + hop > t:
+                        t, w = done[j] + hop, j
+                if e is None:
+                    for j in aft[k]:
+                        if done[j] > t:
+                            t, w = done[j], j
+                else:
+                    if free.get(e, 0.0) > t:
+                        t, w = free[e], last[e]
+                    free[e], last[e] = t + dur[k], k
+                start[k], why[k], done[k] = t, w, t + dur[k] + lat[k]
+                if size[k]:
+                    wire = max(wire, t + 1000.0) + size[k] / 200.0
+                    done[k] = wire + 1000.0
+            return start, done, why
+
+        def worth_of(took):
+            return sum(max(times(i, took)[1]) / p[5] for i, p in enumerate(PLANS))
+
+        def move(i, took, rs):
+            start, done, why = times(i, took)
+            k, held = max(range(n), key=lambda x: done[x]), []
+            while why[k] >= 0:
+                if eng[why[k]] == eng[k] and why[k] not in pre[k] and why[k] not in aft[k]:
+                    held.append(k)
+                k = why[k]
+            if not held:
+                return took
+            x = held[int(rs.randint(len(held)))]
+            row = [k for k in took if eng[k] == eng[x]]
+            y = row[max(0, row.index(x) - 1 - int(rs.geometric(0.5) - 1))]
+            key = [0.0] * n
+            for at, k in enumerate(took):
+                key[k] = float(at)
+            if rs.rand() < 0.5:
+                key[x] = key[y] - 0.5
+                for k in range(x, -1, -1):
+                    for j in pre[k] + aft[k]:
+                        key[j] = min(key[j], key[k])
+            else:
+                key[y] = key[x] + 0.5
+                for k in range(y, n):
+                    for j in succ[k]:
+                        key[j] = max(key[j], key[k])
+            return sorted(range(n), key=lambda k: (key[k], k))
+
+        best = now = None
+        rs = np.random.RandomState(SEED)
+        for t in range(TRIES if plan else 0):
             if t < 12:
                 took = []
                 run(PLANS[t % 4], took, (0.5, 1.0, 2.0)[t // 4], [0.0] * n)
                 for _ in range(3):
                     took = justify(PLANS[t % 4], took, [0.0] * n)
-            else:
+            elif t % EVERY == 0:
                 lo = int(rs.randint(n))
-                took = justify(PLANS[t % 4], best[1], [AMP * float(rs.randn()) if lo <= k < lo + SPAN else 0.0 for k in range(n)])
-            worth = sum(run(p, took) / p[5] for p in PLANS)
+                took = justify(PLANS[t % 4], now[1], [AMP * float(rs.randn()) if lo <= k < lo + SPAN else 0.0 for k in range(n)])
+            else:
+                took = move(t % 4, now[1], rs)
+            worth = worth_of(took)
             if best is None or worth < best[0]:
                 best = (worth, took)
-        seq = {e: [k for k in best[1] if ops[k]["eng"] == e] for e in Q}
+            if t < 12:
+                now = best
+            elif worth < now[0] + SLACK * (1 - t / TRIES) * float(rs.rand()):
+                start = times(1, took)[0]
+                now = (worth, sorted(range(n), key=lambda k: (start[k], k)))
+        if plan:
+            for at, k in enumerate(best[1]):
+                _ORDER.update({x: at for x in ops[k]["keys"]})
+            return
+        place = []
+        for k, o in enumerate(ops):
+            place.append(max([_ORDER.get(o["keys"][0], _ORDER.get(o["keys"][1], 0))] + [place[j] for j in pre[k] + aft[k]]))
+        took = sorted(range(n), key=lambda k: (place[k], k))
+        seq = {e: [k for k in took if ops[k]["eng"] == e] for e in Q}
         top, val = {}, {}
         for k in [k for e in Q for k in seq[e]] + [k for k in range(n) if ops[k]["eng"] is None]:
             top[ops[k]["sem"]] = val[k] = top.get(ops[k]["sem"], 0) + ops[k]["inc"]
@@ -542,6 +642,7 @@ def rank_program(g, core, T, topo):
 
     def round_(r):
         xo = 48 * r
+        tag[0] = r
         rp, par, up = c("X", xo, xo + 16), c("X", xo + 16, xo + 32), c("X", xo + 32, xo + 48)
         ts(par, ind(Ew, c("po", 0, 1)), sgn, Op.mult, off, Op.add)
         trs, tot = [], 0
@@ -603,6 +704,7 @@ def rank_program(g, core, T, topo):
                     else:
                         act(o, ind(Vw, c("SU", a, b)), Fn.Copy)
                         follow("A")
+                        fetches.append(len(ops) - 1)
                     scan(c("MS", 16 * a, 16 * b), c("RM", 0, 16 * (b - a)), o, 0.0, Op.add, Op.min)
                     follow("V")
 
@@ -612,6 +714,7 @@ def rank_program(g, core, T, topo):
             for p in range(p0, p1):
                 act(c("FF", 256 * p, 256 * p + 256), ind(Ew, c("HU", 16 * p, 16 * p + 16)), Fn.Square, bias=c("b8", p, p + 1), scale=8.0)
                 follow("A")
+                tests.append(len(ops) - 1)
             mms([(c(bk, 0, n), c("ID"), c("TGh", 0, n)), (c(bk, 0, n), c("ID"), c("TGl", 0, n))] + decode(bk, 0, "FF", c0, n))
 
         def resolve(k):
@@ -702,14 +805,16 @@ def rank_program(g, core, T, topo):
                 tt(c("tp", a, b), z, c("t256", a, b), Op.max)
             else:
                 tt(c("D", a, b), env, c("M", a, b), Op.subtract)
-                ops[-1]["ghost"].add(back)
 
+        tests, fetches = [], []
         piece(0)
         resolve(0)
         back = extras()
         for k in range(1, len(SC)):
             piece(k)
             resolve(k)
+        ahead.extend((tests[-1], k) for k in fetches[LEAD:])
+        ahead.extend(zip(tests, tests[1:]))
         cut = 16 * SC[-1][0]
         for a, b in ((240, 256), (0, cut), (cut, 240)):
             first(a, b)

@@ -3,38 +3,45 @@ from concourse.bass import DstId, RemoteDMATransfer
 from concourse.mybir import AluOpType as Op, AxisListType, ActivationFunctionType as Fn
 
 W, EV, R = 4096, 2048, 3
-HC = [(0, 4), (4, 10), (10, 15)]
+HC = [(0, 3), (3, 8), (8, 15)]
 SC = [(0, 4), (4, 8), (8, 12), (12, 15)]
-ON_V = {0: 32, 1: 16, 2: 16, 3: 16, 4: 16}
+ON_V = {0: 32, 1: 32, 2: 0, 3: 16, 4: 0}
 LEAD = 0
+C_ON_V = 1
+SCAN = 16
+PSUM_FROM = 1
+OWN_AT = [(14, 14, 16), (10, 11, 13)]
+ON_A = 8
+CUTS = (0, 2560, 4096)
 FETCH = 32
-EARLY = ("p1", "p5", "p2", "p3", "p7")
-LATE = (("p4", "V"), ("p3", "V"), ("p7", "V"))
+BLOCKS = [("p1", "V", 0, 0), ("p5", "V", 0, 0), ("p2", "V", 0, 0), ("p3", "A", 0, 0), ("p7", "A", 0, 0), ("p2", "A", 0, 0), ("p3", "A", 0, 0), ("p4", "V", 1, 1)]
 XC = 480
-MUL, OFF, PEN = 32768.0, 9437184.0, 16384.0
+MUL, PEN = 32768.0, 16384.0
 NEUTRAL, NONE, PO = 4112, 4176, 16
-PLANS = [(0.87, 1.3, 0.87, 100.0, 2200.0, 80.0), (0.92, 1.5, 0.92, 140.0, 2600.0, 95.0), (1.0, 1.6, 1.0, 170.0, 1600.0, 105.0), (1.1, 1.8, 1.1, 200.0, 3000.0, 120.0)]
+PLANS = [(0.87, 1.3, 0.87, 100.0, 2200.0, 80.0, 200.0, 1000.0), (0.92, 1.5, 0.92, 140.0, 2600.0, 90.0, 210.0, 1000.0),
+         (1.0, 1.6, 1.0, 170.0, 1600.0, 100.0, 260.0, 900.0), (1.15, 1.7, 1.15, 200.0, 3000.0, 115.0, 200.0, 1100.0)]
 SCA, AMP, SPAN = 3.8, 300.0, 150
-TRIES = 1800
-SEED = 1
-EVERY = 7
-SLACK = 0.004
+TRIES = 11000
+SEED = 5
+EVERY = 20
+COPY = 50
+SLACK = 0.003
 B, F, I, U = "bfloat16", "float32", "int32", "uint16"
 _SB = {
     "E": (4176, B), "S": (4176, B), "VT": (4128, F), "ENV": (EV, B), "PLC": (PO + 4192, F), "ST": (4176, F),
     "qi": (16, I), "qo": (16, U), "wi": (2, I), "wf": (8, F), "wj": (4, I), "thi": (8, I), "thb": (8, I), "thf": (8, F), "thc": (2, F),
-    "ec": (256, B), "sti": (256, I), "f1": (256, F), "f2": (256, F), "fx": (256, B), "yc": (256, F),
+    "ec": (256, B), "ee": (256, B), "e1": (256, B), "In256": (128, B), "sti": (256, I), "f1": (256, F), "f2": (256, F), "fx": (256, B), "yc": (256, F),
     "pi": (8, I), "pc": (24, F), "qg": (128, F), "qq": (256, F), "jm": (256, F), "ri": (32, I), "rj": (32, I), "wt16": (32, F),
-    "BO": (128, B), "ID": (128, B), "IDF": (128, F), "IQ": (128, F), "I8": (128, B), "In22": (128, B), "In1": (128, B), "BO1k": (128, B),
+    "BO": (128, B), "ID": (128, B), "IDF": (128, F), "I8": (128, B), "In22": (128, B), "In44": (128, B), "BOm": (128, B), "IM": (128, B), "CST": (256, B), "rs": (16, F), "sf": (8, F), "fr": (64, F), "I4": (128, B), "In1": (128, B), "BO1k": (128, B),
     "BOz": (128, B), "BOh": (128, B), "BOn": (128, B), "LD": (128, B), "DG": (128, B), "PK": (128, B), "WB": (512, B), "D16": (256, B), "LK": (2048, B),
     "tg": (16, F), "ti": (48, I), "TGh": (128, B), "TGl": (128, B), "ph": (16, F), "N15": (256, B),
-    "EXi": (16, I), "EX": (16, U), "RM": (1024, B), "RZ": (256, B), "ONE": (256, B), "JT": (96, B), "JT1": (256, B), "K2": (256, B),
+    "EXi": (16, I), "EX": (16, U), "RM": (1024, B), "RZ": (256, B), "RZ2": (256, B), "ONE": (256, B), "JT": (96, B), "JT1": (256, B), "K2": (256, B),
     "OD": (32, B), "thr": (64, F), "nt": (64, B), "iv": (64, B), "qt": (64, F), "tr": (64, F), "mA": (64, F), "FX": (96, F), "G8": (8, F),
-    "X": (48 * R, B), "RP": (256 * R, F), "SV": (256 * R, F), "b8": (16, F), "C": (272, B), "CU": (256, B), "YE": (256, B), "sp": (16, B), "vp": (16, F),
+    "X": (48 * R, B), "RP": (256 * R, B), "SV": (256 * R, B), "fu": (256, F), "b8": (16, F), "C": (272, B), "CU": (256 * R, B), "YE": (256, B), "sp": (16, B), "vp": (16, F),
     "AB": (576, I), "MM": (288, I), "SS": (576, I), "HU": (336, U), "zi": (16, I), "zu": (16, U),
     "FF": (3840, B), "FU": (768, B), "FO": (1024, B), "df": (288, F), "sl": (288, F), "SU": (288, U), "nx": (48, F), "G2": (4096, F), "MS": (4096, F),
-    "fo": (64, F), "fm": (32, F), "KO": (32, F), "ta": (16, F), "tu": (16, U), "t256": (272, F), "tp": (272, F), "M": (256, B), "NG": (256, B), "N5": (256, B),
-    "TH": (256, B), "BOp": (128, B), "BO8": (128, B), "M5": (256, B), "D": (272, B), "good": (256, B), "pre": (256, B), "junk": (1024, B), "acc": (4, F), "ix": (4, U),
+    "fo": (64, F), "fm": (48, F), "KO": (16, F), "ta": (16, F), "tu": (16, U), "t256": (272, F), "tp": (272, F), "M": (256, B), "NG": (256, B), "N5": (256, B),
+    "TH": (512, B), "BOp": (128, B), "BO8": (128, B), "EVg": (256, B), "M5": (256, B), "D": (272, B), "good": (256, B), "pre": (256, B), "junk": (1024, B), "acc": (4, F), "ix": (4, U),
     "tB": (64, F), "tm": (64, F), "tA": (64, F), "eq": (256, B), "nd": (64, F), "so": (4, U), "Ce": (64, B),
     "PS": (256, B), "PB": (256, F), "nb": (64, B), "qc": (64, F), "ov": (64, B), "rm": (4, F), "KB": (256, F), "KA": (256, F), "cm": (4096, B),
     "pl": (4, F), "po": (2, U), "zs": (512, F), "vo": (2, U),
@@ -50,7 +57,7 @@ for _k, (_n, _d) in _SB.items():
         _AT[_k] = (_k, 0)
 SCRATCH = {k: ("psum" if k[1:].isdigit() and k[0] == "p" else "sbuf", [128, n], d) for k, (n, d) in _SB.items() if _AT[k][0] == k}
 SCRATCH["few"] = ("sbuf", [128, _end], F)
-SEMAPHORES = ["V", "A", "P", "G"] + ["d%d" % k for k in range(24)] + [a + str(r) for a in ("lo", "up", "rp", "ls", "lr") for r in range(R)]
+SEMAPHORES = ["V", "A", "P", "G"] + ["d%d" % k for k in range(32)] + [a + str(r) for a in ("lo", "up", "rp", "cu", "ls", "lr", "lc") for r in range(R)]
 
 
 def rank_program(g, core, T, topo):
@@ -116,9 +123,10 @@ def program(g, T, topo, rank, plan):
         if size:
             lastq[eng] = k
         keys = [(tag[0], eng, sem, tuple(wr), tuple(rd)), (tag[0], eng, sem, tuple(wr))]
+        keys.append((tag[0], eng, tuple((n, 0 if n in ("X", "RP", "SV") else lo) for n, lo, hi in wr)))
         for x in keys:
             seen[x] = seen.get(x, 0) + 1
-        ops.append(dict(eng=eng, deps=deps, order=order, keys=[(x, seen[x]) for x in keys], call=call, dur=dur, sem=sem or eng, inc=inc, chain=chain, lat=lat, size=size))
+        ops.append(dict(eng=eng, deps=deps, order=order, keys=[(x, seen[x]) for x in keys[:2]], twin=keys[2] + (seen[keys[2]],), call=call, dur=dur, sem=sem or eng, inc=inc, chain=chain, lat=lat, size=size))
         return k
 
     def issue():
@@ -174,8 +182,8 @@ def program(g, T, topo, rank, plan):
                     t = max(at(k), free[e])
                 start[k], done[k] = t, t + dur[k] + lat[k]
                 if ops[k]["size"]:
-                    wire = max(wire, t + 1000.0) + ops[k]["size"] / 200.0
-                    done[k] = wire + 1000.0
+                    wire = max(wire, t + p[7]) + ops[k]["size"] / p[6] + 60.0
+                    done[k] = wire + p[7]
                 if e is not None:
                     free[e] = t + dur[k]
                 if make:
@@ -220,34 +228,68 @@ def program(g, T, topo, rank, plan):
         fixed = [([o["dur"][0] + p[0] * (o["dur"][1] + p[1] * o["dur"][2] + SCA * o["dur"][3]) + p[2] * o["dur"][4] for o in ops],
                   [o["lat"][0] * p[4] + o["lat"][1] for o in ops]) for p in PLANS]
         eng, size = [o["eng"] for o in ops], [o["size"] for o in ops]
+        behind, near = [], []
+        for k in range(n):
+            far = 0
+            for j in pre[k]:
+                far |= behind[j]
+            near.append([j for j in pre[k] if not far >> j & 1])
+            for j in pre[k]:
+                far |= 1 << j
+            behind.append(far)
 
-        def times(i, took):
+        def times(i, took, known=None, same=0):
             dur, lat = fixed[i]
-            hop, start, done, why, free, last, wire = PLANS[i][3], [0.0] * n, [0.0] * n, [-1] * n, {}, {}, 0.0
-            for k in took:
-                e, t, w = eng[k], 0.0, -1
-                for j in pre[k]:
-                    if done[j] + hop > t:
-                        t, w = done[j] + hop, j
+            hop, start, done, why, free, last, wire = PLANS[i][3], [0.0] * n, [0.0] * n, [-1] * n, dict.fromkeys(Q, 0.0), dict.fromkeys(Q, -1), 0.0
+            if same:
+                start, done, why = list(known[0]), list(known[1]), list(known[2])
+                for e in Q:
+                    for k in rows[e]:
+                        if place[k] < same and start[k] + dur[k] > free[e]:
+                            free[e], last[e] = start[k] + dur[k], k
+                            break
+                wire = max([done[k] - PLANS[i][7] for k in moved if place[k] < same] + [0.0])
+            for k in took[same:]:
+                e, t, w = eng[k], -hop, -1
+                for j in near[k]:
+                    if done[j] > t:
+                        t, w = done[j], j
+                t += hop
                 if e is None:
                     for j in aft[k]:
                         if done[j] > t:
                             t, w = done[j], j
                 else:
-                    if free.get(e, 0.0) > t:
+                    if free[e] > t:
                         t, w = free[e], last[e]
                     free[e], last[e] = t + dur[k], k
                 start[k], why[k], done[k] = t, w, t + dur[k] + lat[k]
                 if size[k]:
-                    wire = max(wire, t + 1000.0) + size[k] / 200.0
-                    done[k] = wire + 1000.0
+                    wire = max(wire, t + PLANS[i][7]) + size[k] / PLANS[i][6] + 60.0
+                    done[k] = wire + PLANS[i][7]
             return start, done, why
 
-        def worth_of(took):
-            return sum(max(times(i, took)[1]) / p[5] for i, p in enumerate(PLANS))
+        held, place, rows, moved = [], [0] * n, {}, [k for k in range(n) if size[k]]
 
-        def move(i, took, rs):
-            start, done, why = times(i, took)
+        def hold(took):
+            held[:] = took
+            for at, k in enumerate(took):
+                place[k] = at
+            for e in Q:
+                rows[e] = [k for k in reversed(took) if eng[k] == e]
+
+        def worth_of(took, i0, bound):
+            got, same = [None] * len(PLANS), 0
+            while bound and same < n and took[same] == held[same]:
+                same += 1
+            for i in [(i0 + d) % len(PLANS) for d in range(len(PLANS))]:
+                got[i] = times(i, took, bound and bound[i], same)
+                if bound and max(got[i][1]) > max(bound[i][1]) + 0.004 * PLANS[i][5] * 1000:
+                    return 1e9, got
+            return sum(max(x[1]) / p[5] for x, p in zip(got, PLANS)) / 1000, got
+
+        def move(now, i, rs):
+            took, (start, done, why) = now[1], now[2][i]
             k, held = max(range(n), key=lambda x: done[x]), []
             while why[k] >= 0:
                 if eng[why[k]] == eng[k] and why[k] not in pre[k] and why[k] not in aft[k]:
@@ -262,15 +304,33 @@ def program(g, T, topo, rank, plan):
             for at, k in enumerate(took):
                 key[k] = float(at)
             if rs.rand() < 0.5:
-                key[x] = key[y] - 0.5
-                for k in range(x, -1, -1):
-                    for j in pre[k] + aft[k]:
-                        key[j] = min(key[j], key[k])
+                to, todo = key[y] - 0.5, [x]
+                while todo:
+                    k = todo.pop()
+                    key[k] = to
+                    todo.extend(j for j in near[k] + aft[k] if key[j] > to)
             else:
-                key[y] = key[x] + 0.5
-                for k in range(y, n):
-                    for j in succ[k]:
-                        key[j] = max(key[j], key[k])
+                to, todo = key[x] + 0.5, [y]
+                while todo:
+                    k = todo.pop()
+                    key[k] = to
+                    todo.extend(j for j in succ[k] if key[j] < to)
+            return sorted(range(n), key=lambda k: (key[k], k))
+
+        twin = {}
+        for k, o in enumerate(ops):
+            twin.setdefault(o["twin"][1:], {})[o["twin"][0]] = k
+
+        def copy_round(i, took, a, b):
+            start = times(i, took)[0]
+            both = [(x[a], x[b]) for x in twin.values() if a in x and b in x]
+            shift = min(start[y] for _, y in both if eng[y] == "G") - min(start[x] for x, _ in both if eng[x] == "G")
+            key = list(start)
+            for x, y in both:
+                key[y] = start[x] + shift
+            for k in range(n):
+                for j in pre[k] + aft[k]:
+                    key[k] = max(key[k], key[j])
             return sorted(range(n), key=lambda k: (key[k], k))
 
         best = now = None
@@ -281,19 +341,24 @@ def program(g, T, topo, rank, plan):
                 run(PLANS[t % 4], took, (0.5, 1.0, 2.0)[t // 4], [0.0] * n)
                 for _ in range(3):
                     took = justify(PLANS[t % 4], took, [0.0] * n)
+            elif t % COPY < 2:
+                a = int(rs.randint(R))
+                took = copy_round(1, now[1], a, (a + 1 + int(rs.randint(R - 1))) % R)
+                took = justify(PLANS[1], took, [0.0] * n) if t % COPY else took
             elif t % EVERY == 0:
                 lo = int(rs.randint(n))
                 took = justify(PLANS[t % 4], now[1], [AMP * float(rs.randn()) if lo <= k < lo + SPAN else 0.0 for k in range(n)])
             else:
-                took = move(t % 4, now[1], rs)
-            worth = worth_of(took)
+                took = move(now, t % 4, rs)
+            worth, got = worth_of(took, t, now[2] if t >= 12 else None)
             if best is None or worth < best[0]:
-                best = (worth, took)
+                best = (worth, took, got)
             if t < 12:
                 now = best
+                hold(now[1])
             elif worth < now[0] + SLACK * (1 - t / TRIES) * float(rs.rand()):
-                start = times(1, took)[0]
-                now = (worth, sorted(range(n), key=lambda k: (start[k], k)))
+                now = (worth, sorted(range(n), key=lambda k: (got[1][0][k], k)), got)
+                hold(now[1])
         if plan:
             for at, k in enumerate(best[1]):
                 _ORDER.update({x: at for x in ops[k]["keys"]})
@@ -377,6 +442,12 @@ def program(g, T, topo, rank, plan):
         else:
             emit("G", [o], [], lambda: g.iota(o[0], pat, base, cm, allow_small_or_imprecise_dtypes=True), (130, 2 * o[3], 0, 0, 0))
 
+    def fill(o, v):
+        iota(o, [[0, o[3]]], v, 0)
+
+    def sc(o, i, scale=1.0, bias=0.0):
+        act(o, i, Fn.Identity, bias=bias, scale=scale)
+
     n_dma = [0]
 
     def dma(eng, o, i, size, skip=()):
@@ -403,15 +474,9 @@ def program(g, T, topo, rank, plan):
     dma("Y", c("S", 0, W), T.su[:], 1 << 20)
     dma("A", c("wi"), T.wt[:], 1024)
     dma("A", c("thi", rows=slice(0, 1)), T.th[:], 32)
-    dma("Y", c("ec"), T.ex[row0, :], 1 << 16)
+    dma("Y", c("ec"), T.su[row0, :], 1 << 16)
     dma("Y", c("sti"), T.st[:], 1 << 17)
-    parts_e = []
-
-    def load_e(groups):
-        for k in groups:
-            rows = slice(16 * k + 1, 16 * k + 16)
-            parts_e.append(dma("Y", c("E", 0, W, rows=rows), T.ex[rows, :], 15 << 13, skip=list(parts_e)))
-    load_e(range(5))
+    dma("Y", c("E", 0, CUTS[1]), T.ex[:, 0:CUTS[1]], 256 * CUTS[1])
     iota(c("pi", 0, 1), [[0, 1]], 0, 1)
     iota(c("qq"), [[1, 256]], 0, 0)
     iota(c("jm"), [[0, 16], [1, 16]], 0, 0)
@@ -420,12 +485,14 @@ def program(g, T, topo, rank, plan):
     iota(c("EXi"), [[1, 16]], 0, 0)
     iota(c("ri", 0, 16), [[-1, 16]], 16, 1)
     iota(c("ri", 16, 32), [[1, 16]], 128, -1)
-    act(c("PLC", PO, PO + 256), c("qq"), Fn.Copy)
-    for k in (256, 512, 1024, 2048):
-        act(c("PLC", PO + k, PO + 2 * k), c("PLC", PO, PO + k), Fn.Identity, bias=float(k))
-    act(c("PLC", PO + W, PO + 4192), c("PLC", PO, PO + 96), Fn.Identity, bias=float(W))
+    ms(c("FF", 0, 1024), 1.0)
+    scan(c("PLC", PO, PO + 1024), c("FF", 0, 1024), c("FF", 0, 1024), -1.0, Op.mult, Op.add)
+    sc(c("PLC", PO + 1024, PO + 2048), c("PLC", PO, PO + 1024), 1.0, 1024.0)
+    sc(c("PLC", PO + 2048, PO + 3072), c("PLC", PO, PO + 1024), 1.0, 2048.0)
+    sc(c("PLC", PO + 3072, PO + 3584), c("PLC", PO, PO + 512), 1.0, 3072.0)
+    ts(c("PLC", PO + 3584, PO + 4192), c("PLC", PO, PO + 608), 3584.0, Op.add)
     ms(c("PLC", 0, PO), 2.0 ** 28)
-    ms(c("S", W, 4176), -1.0)
+    ms(c("S", W, 4176), -64.0)
     ms(c("E", W, 4176), 240.0)
     ms(c("VT", W, 4128), 2.0 ** 25)
     ms(c("RZ"), 1.0)
@@ -447,24 +514,23 @@ def program(g, T, topo, rank, plan):
     ts(c("D16"), c("jm"), lcol, Op.is_equal)
     ts(c("qi"), c("qi"), 8191, Op.bitwise_and)
     ts(c("qo"), c("qi"), 4111.0, Op.min)
-    ts(c("K2"), c("D16"), OFF + 2.0 ** 24, Op.mult, -2.0 ** 24, Op.add)
+    ts(c("K2"), c("D16"), 2.0 ** 24 - 1, Op.mult, -2.0 ** 24, Op.add)
+    ts(c("RZ2"), c("RZ"), 2.0 ** 26, Op.mult, -2.0 ** 26, Op.add)
     ts(c("BOz"), c("BO1k"), MUL / 1024, Op.mult)
     ts(c("BOh"), c("BO1k"), MUL / 2048, Op.mult)
     ts(c("IDF"), c("qq", 0, 128), pcol, Op.is_equal)
+    ts(c("BOm"), c("BO1k"), -MUL / 2048, Op.mult)
+    ts(c("IM"), c("ID"), MUL, Op.mult)
+    fill(c("CST", 0, 16 * ON_A), 127)
+    iota(c("CST", 16 * ON_A, 256), [[-16, 16 - ON_A], [0, 16]], 255 - 8 * ON_A, 0)
     ts(c("pc", 3, 4), lcol, 15.0, Op.is_equal, 305.0, Op.mult)
     tt(c("pc", 3, 4), c("pc", 3, 4), lcol, Op.add)
     ts(c("DG"), c("ID"), c("pc", 3, 4), Op.mult, -MUL, Op.mult)
-    ts(c("pc", 5, 6), lcol, 0.0, Op.is_equal, -2.0, Op.mult)
-    ts(c("pc", 4, 5), c("pc", 5, 6), 1.0, Op.add)
     ts(c("pc", 6, 7), lcol, 4096.0, Op.add)
-    sgn, off = c("pc", 4, 5), c("pc", 5, 6)
-    ts(c("f1"), c("sti"), 1.0, Op.is_equal, -2.0, Op.mult)
-    ts(c("p3", 0, 256), c("ec"), 1.0, Op.add)
-    tt(c("p3", 0, 256), c("p3", 0, 256), c("f1"), Op.mult)
-    tt(c("fx"), c("p3", 0, 256), c("ec"), Op.add)
-    parts_e.append(dma("Y", c("E", 0, W, rows=row0), c("fx"), 1 << 16, skip=list(parts_e)))
-    load_e(range(5, 8))
-    dma("Y", c("ENV"), T.env[:], 1 << 19)
+    ts(c("pc", 4, 5), lcol, 0.0, Op.is_equal, 256.0, Op.mult)
+    ts(c("pc", 5, 6), lcol, 0.0, Op.is_equal, -256.0, Op.mult)
+    ts(c("f1"), c("sti"), 1.0, Op.is_equal, -256.0, Op.mult)
+    tt(c("fx"), c("f1"), c("ec"), Op.add)
     cp(c("EX"), c("EXi"))
     ts(c("BO"), c("BO1k"), 1.0 / 1024, Op.mult)
     ts(c("wj", 0, 2), c("wi"), 4032, Op.bitwise_and)
@@ -473,16 +539,18 @@ def program(g, T, topo, rank, plan):
     cp(c("wf", 4, 6), c("wi"))
     ts(c("wf", 6, 8), c("wi"), -1.0, Op.mult)
     for k in range(4):
-        ts(c("WB", 128 * k, 128 * k + 128), c("BO"), c("wf", k, k + 1), Op.mult)
+        sc(c("WB", 128 * k, 128 * k + 128), c("BO"), c("wf", k, k + 1))
     ts(c("ri"), c("ri"), 15, Op.bitwise_and)
     ts(c("rj"), c("ri"), 3.0, Op.add)
     ts(c("rj"), c("rj"), 2, Op.arith_shift_right)
     tt(c("rj"), c("rj"), c("ri"), Op.add)
     ts(c("wt16"), c("rj"), 1.0, Op.max, 235.0, Op.add)
-    ms(c("LK"), 0.0)
+    fill(c("LK", 0, 1024), 0)
+    for k in (1024, 1536):
+        ms(c("LK", k, k + 512), 0.0)
     ts(c("G8"), c("qq", 0, 8), gcol, Op.is_equal)
     for k in range(8):
-        ts(c("LK", 16 * k, 16 * k + 129 * 15 + 1, 129), c("wt16", 0, 16), c("G8", k, k + 1), Op.mult)
+        sc(c("LK", 16 * k, 16 * k + 129 * 15 + 1, 129), c("wt16", 0, 16), c("G8", k, k + 1))
     ts(c("tg"), c("wt16", 16, 32), 80.0, Op.mult, 3917.0 + 11328.0, Op.add)
     ts(c("qt", 16, 32), c("D16", 0, 16), -30208.0, Op.mult)
     tt(c("ti", 0, 16), c("tg"), c("qt", 16, 32), Op.add)
@@ -491,102 +559,127 @@ def program(g, T, topo, rank, plan):
     for name, lo in (("TGh", 16), ("TGl", 32)):
         ts(c(name, 0, 16), c("ti", lo, lo + 16), -1.0, Op.mult)
         for k in (16, 32, 64):
-            cp(c(name, k, 2 * k), c(name, 0, k))
+            sc(c(name, k, 2 * k), c(name, 0, k))
     mm(c("p0", 0, 16), c("PK"), c("D16", 0, 16), True, True)
-    cp(c("ph"), c("p0", 0, 16))
-    ts(c("pc", 19, 20), c("p0", 15, 16), -1.0, Op.mult)
+    sc(c("ph"), c("p0", 0, 16))
     ms(c("RM", 0, 1), 2.0 ** 26)
     tt(c("RM", 1, 16), c("ph", 0, 15), c("ph", 1, 16), Op.subtract)
-    for k in (16, 32, 64, 128, 256, 512):
-        cp(c("RM", k, 2 * k), c("RM", 0, k))
-    ts(c("N15"), c("ONE"), lcol, Op.mult, 15.0, Op.is_equal)
-    ts(c("N15"), c("N15"), -1.0, Op.mult)
-    ts(c("IQ"), c("IDF"), -2.0 ** -14, Op.mult)
-    ts(c("BOn"), c("BO"), -2.0 ** 30, Op.mult)
-    ms(c("KO", 0, 16), -PEN)
-    ms(c("KO", 16, 32), -4 * PEN)
-    ms(c("nx"), 0.0)
-    ms(c("FU", 256, 768), 1.0)
-    ts(c("OD"), c("D16", 0, 32), 2.0 ** 25, Op.mult, -2.0 ** 25, Op.add)
-    ms(c("FX"), 0.0)
+    for k in (16, 32, 64, 128):
+        sc(c("RM", k, 2 * k), c("RM", 0, k))
+    ts(c("pc", 23, 24), lcol, 15.0, Op.is_equal, -1.0, Op.mult)
+    sc(c("N15"), c("ONE"), c("pc", 23, 24))
+    sc(c("BOn"), c("BO"), -2.0 ** 45)
+    fill(c("nx"), 0)
+    fill(c("FU", 256, 768), 1)
+    sc(c("OD"), c("D16", 0, 32), 2.0 ** 25, -2.0 ** 25)
+    fill(c("FX"), 0)
     for h, k in ((0, 1), (48, 0)):
-        ts(c("FX", h, h + 16), c("ONE", 0, 16), c("wf", 6 + k, 7 + k), Op.mult)
-        ts(c("FX", h + 16, h + 31), c("ONE", 0, 15), c("wf", 4 + k, 5 + k), Op.mult)
-        ts(c("FX", h + 32, h + 47), c("ONE", 0, 15), c("wf", 4 + k, 5 + k), Op.mult)
-    ts(c("I8"), c("ID"), 8192.0, Op.mult)
-    ts(c("In22"), c("ID"), -2.0 ** 22, Op.mult)
-    ts(c("In1"), c("ID"), -1.0, Op.mult)
-    ts(c("JT"), c("qq", 0, 96), -2.0, Op.mult)
+        sc(c("FX", h, h + 16), c("ONE", 0, 16), c("wf", 6 + k, 7 + k))
+        sc(c("FX", h + 16, h + 31), c("ONE", 0, 15), c("wf", 4 + k, 5 + k))
+        sc(c("FX", h + 32, h + 47), c("ONE", 0, 15), c("wf", 4 + k, 5 + k))
+    sc(c("I8"), c("ID"), 8192.0)
+    sc(c("In22"), c("ID"), -2.0 ** 22)
+    sc(c("In44"), c("ID"), -2.0 ** 44)
+    sc(c("I4"), c("ID"), 4608.0)
+    sc(c("In1"), c("ID"), -1.0)
+    sc(c("In256"), c("ID"), -256.0)
+    iota(c("JT"), [[-2, 96]], 0, 0)
     ms(c("qt"), 0.25)
-    ms(c("nd"), 0.0)
+    fill(c("nd"), 0)
     scan(c("thr"), c("qt"), c("nd"), 2.0 ** 51, Op.mult, Op.add)
     tt(c("qt", 0, 16), c("thr", 0, 16), c("D16", 0, 16), Op.mult)
-    ts(c("nt"), c("thr"), -1.0, Op.mult)
+    sc(c("nt"), c("thr"), -1.0)
     red(c("pc", 13, 14), c("qt", 0, 16), Op.add)
-    ts(c("LD"), c("BO"), c("pc", 13, 14), Op.mult)
-    ts(c("tr"), c("qq", 0, 64), 4112.0, Op.add)
-    ts(c("mA"), c("qq", 0, 64), 4113.0, Op.add)
+    sc(c("LD"), c("BO"), c("pc", 13, 14))
+    iota(c("tr"), [[1, 64]], 4112, 0)
+    iota(c("mA"), [[1, 64]], 4113, 0)
     tt(c("mA"), c("mA"), c("D16", 0, 64), Op.mult)
-    ts(c("mA"), c("mA"), -1.0, Op.add)
+    sc(c("mA"), c("mA"), 1.0, -1.0)
     tt(c("pc", 7, 8), c("pc", 3, 4), lcol, Op.subtract)
     ts(c("pc", 8, 9), c("pc", 7, 8), -31.0, Op.add, MUL, Op.mult)
     ts(c("pc", 7, 8), c("pc", 7, 8), -15.0, Op.add, MUL, Op.mult)
     ts(c("pc", 9, 13), c("qq", 0, 64, 16), lcol, Op.add)
+    sc(c("sf", 0, 4), c("pc", 9, 13), 1.0 / 128)
+    sc(c("sf", 4, 8), c("pc", 9, 13), 1.0, 4112.0)
+    sc(c("fr"), c("qq", 0, 64), 1.0 / 128)
     ts(c("pc", 9, 11), c("pc", 9, 11), -1.0, Op.mult, -0.5, Op.add)
     emit("G", [c("thb")], [c("thi")], lambda: g.partition_broadcast(T.thb[:], T.thi[0:1, :], 128), (180, 0, 0, 0, 0))
     tt(c("thf"), c("thb"), c("G8"), Op.mult)
     red(c("thc", 0, 1), c("thf"), Op.add)
-    ts(c("thc", 1, 2), c("thc", 0, 1), -0.5, Op.add)
-    ms(c("C", 256, 272), 0.0)
-    ms(c("D", 256, 272), 0.0)
-    ms(c("tp" if below is not None else "t256", 256, 272), 8000.0)
+    fill(c("C", 256, 272), 0)
+    fill(c("D", 256, 272), 0)
+    fill(c("tp" if below is not None else "t256", 256, 272), 8000)
+    cp(c("pi", 5, 6), c("thc", 0, 1))
+    ts(c("pi", 6, 7), c("pi", 5, 6), 4032, Op.bitwise_and)
+    ts(c("pi", 7, 8), c("pi", 5, 6), 63, Op.bitwise_and)
+    cp(c("pc", 20, 22), c("pi", 6, 8))
+    sc(c("pc", 14, 15), c("pc", 20, 21), -MUL)
+    sc(c("pc", 15, 16), c("pc", 21, 22), -MUL, MUL / 4)
+    for k in (0, 1):
+        sc(c("TH", 256 + 128 * k, 384 + 128 * k), c("ID"), c("pc", 14 + k, 15 + k))
     if below is not None:
-        cp(c("pi", 5, 6), c("thc", 0, 1))
-        ts(c("pi", 6, 7), c("pi", 5, 6), 4032, Op.bitwise_and)
-        ts(c("pi", 7, 8), c("pi", 5, 6), 63, Op.bitwise_and)
-        cp(c("pc", 20, 22), c("pi", 6, 8))
         for k in (0, 1):
-            ts(c("TH", 128 * k, 128 * k + 128), c("I8"), c("pc", 20 + k, 21 + k), Op.mult)
-        ts(c("BOp"), c("BO"), 2.0 ** 30, Op.mult)
-        ts(c("BO8"), c("BO"), -8192.0, Op.mult)
+            sc(c("TH", 128 * k, 128 * k + 128), c("I8"), c("pc", 20 + k, 21 + k))
+        sc(c("BOp"), c("BO"), 2.0 ** 30)
+        sc(c("BO8"), c("BO"), -8192.0)
     for r in range(R):
         if below is None:
-            ms(c("X", 48 * r, 48 * r + 16), 240.0)
+            sc(c("X", 48 * r, 48 * r + 16), c("ONE", 0, 16), 240.0)
         if above is None:
-            ms(c("X", 48 * r + 32, 48 * r + 48), 240.0)
+            sc(c("X", 48 * r + 32, 48 * r + 48), c("ONE", 0, 16), 240.0)
 
     Ew, Sw, Vw, Pw = c("E"), c("S"), c("VT"), c("PLC", PO)
 
     def keys(r, lo, hi):
-        for bk in ("p7", "p6"):
+        for bk in ("p7", "p6") if r else ("p7", "p6", "p0"):
             parts = [(c(bk, lo, hi), c("ID"), c("JT1" if r == 0 else "JT", lo, hi))]
             if bk == "p7":
                 parts.append((c(bk, lo, hi), c("ID"), c("K2", lo, hi)))
             parts.append((c(bk, lo, hi), c("BO1k"), c("PS", lo, hi)))
             if r:
-                parts += [(c(bk, 32, 96), c("In22"), c("nb")), (c(bk, 32, 96), c("In22"), c("ov"))]
+                parts += [(c(bk, 32, 96), c("In44"), c("nb")), (c(bk, 32, 96), c("In22"), c("ov"))]
             mms(parts)
 
     def ranks(r, lo, hi, on_v):
         n = hi - lo
-        scan(c("KA", lo, hi), c("RZ", 0, n), c("p7", lo, hi), 0.0, Op.mult, Op.max)
-        act(c("KB", lo, hi), c("p6", lo, hi), Fn.Identity, bias=OFF + 1)
+        for a in range(lo, hi, 128):
+            b = min(a + 128, hi)
+            scan(c("KA", a, b), c("RZ2", 0, b - a), c("p7", a, b), 0.0, Op.add, Op.max)
+        if r:
+            act(c("KB", lo, hi), c("p6", lo, hi), Fn.Copy)
+        kb_v, kb_a = (c("KB", lo, hi), c("KB", lo, hi)) if r else (c("p6", lo, hi), c("p0", lo, hi))
         z = c("p4", lo, hi)
         mm(z, c("DG"), c("ONE", 0, n), True, False)
         mm(z, c("IDF"), c("PB", lo, hi), False, False)
         if r:
-            mm(c("p4", 32, 96), c("I8"), c("ov"), False, False)
+            mm(c("p4", 32, 96), c("I4"), c("ov"), False, False)
         ks = list(range(n // 16))
         kv, ka = ks[:on_v], ks[on_v:]
+        if r == 0:
+            mm(z, c("IM"), c("CST"), False, False)
+            order = [k for pair in zip(range(ON_A), range(ON_A, 16)) for k in pair] + list(range(2 * ON_A, 16))
+            for k in order:
+                o, key = c("cm", n * k + 16 * k, n * k + n), c("KA", 16 * k + 15, 16 * k + 16)
+                if k < ON_A:
+                    act(o, c("p0", 16 * k, n), Fn.Sign, bias=key, scale=-1.0, accum=c("rs", k, k + 1))
+                else:
+                    ts(o, c("p6", 16 * k, n), key, Op.is_lt, 2.0, Op.mult)
+                    red(c("rs", k, k + 1), o, Op.add)
+                if k < 15:
+                    mm(c("p4", 16 * k + 16, n), c("BOh"), c("cm", n * k + 16 * k + 16, n * k + n), False, False)
+            for a in (8, 0):
+                tt(c("YE", 16 * a, 16 * a + 128), ind(c("rs", a, a + 8), c("EX", 0, 8)), c("D16", 0, 128), Op.mult)
+                mm(c("p4", 16 * a, 16 * a + 128), c("BOm"), c("YE", 16 * a, 16 * a + 128), False, a == 0)
+            kv = ka = []
         order = []
         for j in range(max(len(kv), len(ka))):
             order += kv[j:j + 1] + ka[j:j + 1]
         for k in order:
             o, key = c("cm", n * k, n * k + n), c("KA", lo + 16 * k + 15, lo + 16 * k + 16)
             if k in kv:
-                ts(o, c("KB", lo, hi), key, Op.is_lt, len(ka) / 2 if k == 0 else 0.0, Op.add)
+                ts(o, kb_v, key, Op.is_lt, len(ka) / 2 if k == 0 else 0.0, Op.add)
             else:
-                act(o, c("KB", lo, hi), Fn.Sign, bias=key, scale=-1.0)
+                act(o, kb_a, Fn.Sign, bias=key, scale=-1.0)
             mm(z, c("BOz" if k in kv else "BOh"), o, False, k == order[-1])
         red(c("pl", 0, 1), z, Op.min, True)
         ts(c("po", 0, 1), c("pl", 0, 1), c("pc", 6, 7), Op.min)
@@ -600,14 +693,19 @@ def program(g, T, topo, rank, plan):
         act(c("PS", 32 - 16 * m, 32), ind(Sw, c("vo", 0, m)), Fn.Copy)
         act(c("PB", 32 - 16 * m, 32), ind(Pw, c("vo", 0, m)), Fn.Copy)
 
-    def hash_tail(o, n):
+    def hash_tail(o, n, bk=None):
         ab, s = c("AB", o, o + 2 * n), c("SS", o, o + 2 * n)
         m = c("MM", o // 2, o // 2 + n)
         ts(ab, ab, 4095, Op.bitwise_and)
-        tt(m, c("AB", o, o + n), c("AB", o + n, o + 2 * n), Op.mult)
+        if bk is None:
+            tt(m, c("AB", o, o + n), c("AB", o + n, o + 2 * n), Op.mult)
+        else:
+            ab = c(bk, 0, 2 * n)
+            cp(ab, c("AB", o, o + 2 * n))
+            tt(m, c(bk, 0, n), c("AB", o + n, o + 2 * n), Op.mult)
         ts(c("SS", o, o + n), m, 5, Op.arith_shift_right)
         ts(c("SS", o + n, o + 2 * n), m, 9, Op.arith_shift_right)
-        tt(s, s, ab, Op.add)
+        tt(s, ab, s, Op.add)
         ts(s, s, 4095, Op.bitwise_and)
         m = 2 * n if o == XC else n
         cp(c("HU", o // 2, o // 2 + m), c("SS", o, o + m))
@@ -622,29 +720,37 @@ def program(g, T, topo, rank, plan):
         tt(z, h2, sl, Op.add)
         ts(c("SU", lo, lo + n), z, float(NEUTRAL), Op.min)
 
-    def begin_vt():
-        for k, bk in enumerate(EARLY):
-            mm(c(bk), c("ID"), c("S", 512 * k, 512 * k + 512), True, False)
-
-    def finish_vt():
-        for k, (bk, e) in enumerate([(x, None) for x in EARLY] + list(LATE)):
+    def build_vt(now):
+        for k, (bk, e, begin, end) in enumerate(BLOCKS):
             vt = c("VT", 512 * k, 512 * k + 512)
-            if e == "A":
+            if e == "A" and begin == now:
                 mm(c(bk), c("ID"), c("S", 512 * k, 512 * k + 512), True, False)
-            mm(c(bk), c("PK"), c("E", 512 * k, 512 * k + 512), e == "V", True)
-            if e == "V":
-                tt(vt, c(bk), c("S", 512 * k, 512 * k + 512), Op.add)
-            else:
-                act(vt, c(bk), Fn.Copy)
+            if end == now:
+                mm(c(bk), c("PK"), c("E", 512 * k, 512 * k + 512), e == "V", True)
+                if e == "V":
+                    tt(vt, c(bk), c("S", 512 * k, 512 * k + 512), Op.add)
+                else:
+                    act(vt, c(bk), Fn.Copy)
 
-    def decode(bk, at, buf, lo, n):
-        return [(c(bk, at, at + n), c("LK", 128 * k, 128 * k + 128), c(buf, 16 * lo + k, 16 * (lo + n), 16)) for k in range(16)]
+    def old_vt(par):
+        act(c("sp"), ind(Sw, c("po", 0, 1)), Fn.Identity, bias=c("pc", 4, 5))
+        cp(ind(Sw, c("po", 0, 1)), c("sp"))
+        mms([(c("p2", 0, 16), c("PK"), par), (c("p2", 0, 16), c("ID"), c("sp"))])
+        act(c("vp"), c("p2", 0, 16), Fn.Copy)
+        cp(ind(Vw, c("po", 0, 1)), c("vp"))
+
+    def decode(bk, buf, lo, n, start):
+        o = c(bk, 0, n)
+        for k0 in range(0, 16, 4):
+            parts = [(c("LK", 128 * k, 128 * k + 128), c(buf, 16 * lo + k, 16 * (lo + n), 16), start and k == 0, k == 15) for k in range(k0, k0 + 4)]
+            emit("P", [o], [x for q in parts for x in q[:2]], lambda parts=parts: [g.tensor.matmul(o[0], l[0], x[0], a, b).then_inc(T.sem["P"], 1) for l, x, a, b in parts],
+                 (0, 0, 0, 0, 4 * max(64, n)), inc=4, chain=False)
 
     def round_(r):
         xo = 48 * r
         tag[0] = r
         rp, par, up = c("X", xo, xo + 16), c("X", xo + 16, xo + 32), c("X", xo + 32, xo + 48)
-        ts(par, ind(Ew, c("po", 0, 1)), sgn, Op.mult, off, Op.add)
+        cp(par, ind(Ew, c("po", 0, 1)))
         trs, tot = [], 0
         for dst, k, sem, land in ((above, 0, "lo", rp), (below, 1, "up", up)):
             if dst is not None:
@@ -657,26 +763,38 @@ def program(g, T, topo, rank, plan):
         if below is not None:
             landed(rp, "lo%d" % r, len(halves(below, core, 0)), sent, (1, 0 if r else 2000))
         act(c("b8"), par, Fn.Identity, bias=1.0, scale=-8.0)
-        cp(ind(Ew, c("po", 0, 1)), par)
-        if r == R - 1:
-            dma("Y", c("ec"), c("E", 0, W, rows=row0), 1 << 16)
-            ts(c("f2"), c("ec"), 0.0, Op.is_ge, 2.0, Op.mult)
-            ts(c("f1"), c("ec"), -2.0, Op.is_le)
-            tt(c("yc"), c("f1"), c("f2"), Op.add)
-            dma("Y", c("ST", 0, W, rows=row0), c("yc"), 1 << 17)
         if r:
-            act(c("sp"), ind(Sw, c("po", 0, 1)), Fn.Copy)
-            mms([(c("p2", 0, 16), c("PK"), par), (c("p2", 0, 16), c("ID"), c("sp"))])
-            act(c("vp"), c("p2", 0, 16), Fn.Copy)
-            cp(ind(Vw, c("po", 0, 1)), c("vp"))
+            old_vt(par)
+        if r == R - 1:
+            dma("Y", c("ee"), c("E", 0, W, rows=row0), 1 << 16)
+            dma("Y", c("ec"), c("S", 0, W, rows=row0), 1 << 16)
+            ts(c("e1"), c("ec"), 0.0, Op.is_lt, -1.0, Op.mult)
+            ts(c("ee"), c("ee"), 0.0, Op.is_ge, 2.0, Op.mult)
+            mms([(c("p7", 256, 512), c("ID"), c("ec")), (c("p7", 256, 512), c("In256"), c("e1"))])
+            cp(c("fx"), c("p7", 256, 512))
+            dma("Y", c("S", 0, W, rows=row0), c("fx"), 1 << 16)
+            mms([(c("p7", 256, 512), c("ID"), c("ee")), (c("p7", 256, 512), c("ID"), c("e1"))])
+            cp(c("yc"), c("p7", 256, 512))
+            dma("Y", c("ST", 0, W, rows=row0), c("yc"), 1 << 17)
         for k, (p0, p1) in enumerate(HC):
             n, o, bk = 16 * (p1 - p0), 32 * p0, ("p0", "p6")[k % 2]
-            tt(c("C", 16 * p0, 16 * p1), ind(par, c("EX", p0, p1)), c("D16", 0, n), Op.add)
+            if k < C_ON_V:
+                tt(c("C", 16 * p0, 16 * p1), ind(par, c("EX", p0, p1)), c("D16", 0, n), Op.add)
+            else:
+                for p in range(p0, p1):
+                    act(c("C", 16 * p, 16 * p + 16), c("D16", 0, 16), Fn.Identity, bias=c("X", xo + 16 + p, xo + 17 + p))
             mms(wmm(c(bk, 0, n), 1, c("C", 16 * p0, 16 * p1)))
             mms(wmm(c(bk, n, 2 * n), 0, c("C", 16 * p0, 16 * p1)))
             ts(c("AB", o, o + n), c(bk, 0, n), c("wf", 7, 8), Op.add)
             ts(c("AB", o + n, o + 2 * n), c(bk, n, 2 * n), c("wf", 6, 7), Op.add)
-            hash_tail(o, n)
+            hash_tail(o, n, bk if k >= PSUM_FROM else None)
+        cu, told = c("CU", 256 * r, 256 * r + 240), len(ops) - 1
+        if below is not None:
+            rid, pid, _ = topo.addr(below)
+            told = emit("G", [], [c("C", 0, 240)], lambda: g.remote_dma(cu[0], c("C", 0, 240)[0], T.sem["cu%d" % r], T.sem["lc%d" % r], pid, rid, topo.mask(core, below)),
+                        (500, 0, 0, 0, 0), sem="lc%d" % r, inc=len(topo.engines(core, below)), chain=False, after=[sent])
+        if above is not None:
+            landed(cu, "cu%d" % r, len(topo.engines(above, core)), told, (1, 1000))
         if r == 0:
             ts(c("f2"), c("PB"), 4096.0, Op.is_lt)
             red(c("rm", 1, 2), c("f2"), Op.add)
@@ -685,7 +803,8 @@ def program(g, T, topo, rank, plan):
         if r < 2:
             stayers(r, 0, (256, 96)[r])
         if r == 0:
-            finish_vt()
+            build_vt(1)
+            old_vt(par)
         act(c("p5", 0, 240), c("C", 0, 240), Fn.Relu, bias=float(NEUTRAL), scale=-float(NEUTRAL))
         for p0, p1 in HC:
             n, o, h2 = 16 * (p1 - p0), 32 * p0, c("p5", 16 * p0, 16 * p1)
@@ -705,8 +824,10 @@ def program(g, T, topo, rank, plan):
                         act(o, ind(Vw, c("SU", a, b)), Fn.Copy)
                         follow("A")
                         fetches.append(len(ops) - 1)
-                    scan(c("MS", 16 * a, 16 * b), c("RM", 0, 16 * (b - a)), o, 0.0, Op.add, Op.min)
-                    follow("V")
+                    for x in range(a, b, SCAN):
+                        y = min(x + SCAN, b)
+                        scan(c("MS", 16 * x, 16 * y), c("RM", 0, 16 * (y - x)), c("G2", 16 * x, 16 * y), 0.0, Op.add, Op.min)
+                        follow("V")
 
         def piece(k):
             p0, p1 = SC[k]
@@ -715,7 +836,9 @@ def program(g, T, topo, rank, plan):
                 act(c("FF", 256 * p, 256 * p + 256), ind(Ew, c("HU", 16 * p, 16 * p + 16)), Fn.Square, bias=c("b8", p, p + 1), scale=8.0)
                 follow("A")
                 tests.append(len(ops) - 1)
-            mms([(c(bk, 0, n), c("ID"), c("TGh", 0, n)), (c(bk, 0, n), c("ID"), c("TGl", 0, n))] + decode(bk, 0, "FF", c0, n))
+            mm(c(bk, 0, n), c("ID"), c("TGh", 0, n), True, False)
+            mm(c(bk, 0, n), c("ID"), c("TGl", 0, n), False, False)
+            decode(bk, "FF", c0, n, False)
 
         def resolve(k):
             p0, p1 = SC[k]
@@ -734,25 +857,26 @@ def program(g, T, topo, rank, plan):
                 red(c("p7", 48 * h + 47, 48 * h + 48), c("p7", 112 + 32 * h, 128 + 32 * h), Op.max)
             tt(c("AB", XC, XC + 96), c("p7", 0, 96), c("FX"), Op.add)
             hash_tail(XC, 48)
-            cp(c("C", 240, 256), rp)
+            act(c("C", 240, 256), rp, Fn.Copy)
             act(c("nx", 0, 16), rp, Fn.Relu, bias=float(NEUTRAL), scale=-float(NEUTRAL))
             h2 = c("p7", 192, 240)
             tt(h2, c("SS", XC + 48, XC + 96), c("nx"), Op.max)
             tt(c("df", 240, 288), c("SS", XC, XC + 48), h2, Op.subtract)
-            tt(c("YE"), ind(rp, c("EX")), c("D16"), Op.subtract)
             if above is not None:
-                tt(c("CU", 0, 240), ind(up, c("EX", 0, 15)), c("D16", 0, 240), Op.add)
-                cp(c("CU", 240, 256), par)
-                tt(c("FU", 512, 768), ind(Ew, c("HU", hu + 32, hu + 48)), c("CU"), Op.not_equal)
+                act(c("CU", 256 * r + 240, 256 * r + 256), par, Fn.Copy)
+                tt(c("FU", 512, 768), ind(Ew, c("HU", hu + 32, hu + 48)), c("CU", 256 * r, 256 * r + 256), Op.not_equal)
+            tt(c("YE"), ind(rp, c("EX")), c("D16"), Op.subtract)
             tt(c("FU", 0, 256), ind(Ew, c("HU", hu, hu + 16)), c("YE"), Op.not_equal)
-            mms(decode("p0", 0, "FU", 0, 48))
+            decode("p0", "FU", 0, 48, True)
             choose(c("p0", 0, 48), h2, 240, 48)
             if above is not None:
                 sv = c("SV", 256 * r, 256 * r + 256)
-                act(sv, ind(Vw, c("SU", 272, 288)), Fn.Identity, bias=c("pc", 19, 20))
+                mm(c("p1", 256, 512), c("PK"), c("CU", 256 * r, 256 * r + 256), True, True)
+                act(c("fu"), c("p1", 256, 512), Fn.Copy)
+                tt(sv, ind(Vw, c("SU", 272, 288)), c("fu"), Op.subtract)
                 rid, pid, _ = topo.addr(above)
                 back = emit("G", [], [sv], lambda: g.remote_dma(T.RP[:, 256 * r:256 * r + 256], sv[0], T.sem["rp%d" % r], T.sem["lr%d" % r], pid, rid, topo.mask(core, above)),
-                            (500, 0, 0, 0, 0), sem="lr%d" % r, inc=len(topo.engines(core, above)), chain=False, lat=(1, 2000))
+                            (500, 0, 0, 0, 0), sem="lr%d" % r, inc=len(topo.engines(core, above)), chain=False, lat=(1, 1300))
             else:
                 back = len(ops) - 1
             if below is not None:
@@ -762,21 +886,24 @@ def program(g, T, topo, rank, plan):
             ts(c("zi"), c("MM", XC // 2 + 16, XC // 2 + 32), 7, Op.arith_shift_right, 2047, Op.bitwise_and)
             cp(c("zu"), c("zi"))
             for h in (0, 1):
-                fd, z = c("FO", 512 * h, 512 * h + 256), c("p4", 256 * h, 256 * h + 256)
+                fd, z = c("FO", 256 * h, 256 * h + 256), c("p4", 256 * h, 256 * h + 256)
                 act(fd, ind(Ew, c("HU", hu + 48 * h + 16, hu + 48 * h + 32)), Fn.Abs, bias=1.0)
+                owns.append(len(ops) - 1)
                 mms([(z, c("In1"), c("C", 0, 256)), (z, c("ID"), fd)])
-            for h in (0, 1):
-                act(c("FO", 512 * h + 256, 512 * h + 512), c("p4", 256 * h, 256 * h + 256), Fn.Square, bias=-1.0)
-            mms(decode("p4", 0, "FO", 0, 64))
-            ts(c("fo"), c("p4", 0, 64), 0.0, Op.is_equal)
-            tt(c("ta"), c("fo", 0, 16), c("df", 256, 272), Op.mult)
-            tt(c("fm"), c("fo", 0, 32), c("fo", 32, 64), Op.max)
+            act(c("FO", 512, 1024), c("p4"), Fn.Square, bias=-1.0)
+            owns.append(len(ops) - 1)
+            decode("p4", "FO", 0, 64, True)
+            sc(c("KO"), c("df", 256, 272), -1 / PEN)
+            ts(c("fo", 0, 32), c("p4", 0, 32), 0.0, Op.is_equal, -PEN, Op.mult)
+            ts(c("fo", 32, 64), c("p4", 32, 64), 0.0, Op.is_equal, -4 * PEN, Op.mult)
+            tt(c("ta"), c("fo", 0, 16), c("KO"), Op.mult)
+            tt(c("fm"), c("fo", 0, 48), c("fo", 16, 64), Op.min)
             tt(c("ta"), c("ta"), c("SS", XC + 64, XC + 80), Op.add)
-            tt(c("fm"), c("fm"), c("KO"), Op.mult)
-            tt(c("fm", 0, 16), c("fm", 0, 16), c("fm", 16, 32), Op.add)
+            tt(c("fm", 0, 16), c("fm", 0, 16), c("fm", 32, 48), Op.add)
             tt(c("ta"), c("ta"), c("fm", 0, 16), Op.add)
             ts(c("tu"), c("ta"), PEN + PO, Op.add, float(NONE + PO), Op.min)
             act(c("t256", 0, 256), ind(c("PLC"), c("tu")), Fn.Copy)
+            act(c("EVg"), ind(c("ENV"), c("zu")), Fn.Copy)
             return back
 
         def first(a, b):
@@ -790,23 +917,22 @@ def program(g, T, topo, rank, plan):
                 ts(c("M", a, b), c("M", a, b), 255.0, Op.min)
 
         def count(a, b):
-            z = c("p6", a, b)
-            mms([(z, c("IQ"), c("t256", a, b)), (z, c("BOn"), c("NG", a, b)), (z, c("BO"), c("M", a, b))])
-            ts(c("good", a, b), z, c("thc", 1, 2), Op.is_ge)
+            z = c("p1" if a else "p6", a, b)
+            mms([(z, c("TH", 256, 384), c("ONE", a, b)), (z, c("TH", 384, 512), c("ONE", a, b)), (z, c("BOn"), c("NG", a, b)), (z, c("BOz"), c("M", a, b))])
+            tt(c("good", a, b), z, c("t256", a, b), Op.is_ge)
             scan(c("pre", a, b), c("good", a, b), c("good", a, b), c("pre", a - 1, a) if a else 0.0, Op.add, Op.max)
 
         def lower(a, b):
-            env = ind(c("ENV"), c("zu", a // 16, b // 16))
+            m5, d = c("M" if below is None else "M5", a, b), c("p2" if a else "p4", a, b)
             if below is not None:
-                z = c("p7", a, b)
-                tt(c("M5", a, b), c("p0", 256 + a, 256 + b), c("M", a, b), Op.min)
-                mms([(z, c("TH", 0, 128), c("ONE", a, b)), (z, c("TH", 128, 256), c("ONE", a, b)), (z, c("BOp"), c("N5", a, b)), (z, c("BO8"), c("M5", a, b))])
-                tt(c("D", a, b), env, c("M5", a, b), Op.subtract)
+                z = c("p6" if a else "p7", a, b)
+                tt(m5, c("RP", 256 * r + a, 256 * r + b), c("M", a, b), Op.min)
+                mms([(z, c("TH", 0, 128), c("ONE", a, b)), (z, c("TH", 128, 256), c("ONE", a, b)), (z, c("BOp"), c("N5", a, b)), (z, c("BO8"), m5)])
                 tt(c("tp", a, b), z, c("t256", a, b), Op.max)
-            else:
-                tt(c("D", a, b), env, c("M", a, b), Op.subtract)
+            mms([(d, c("In1"), c("EVg", a, b)), (d, c("ID"), m5)])
+            act(c("D", a, b), d, Fn.Abs)
 
-        tests, fetches = [], []
+        tests, fetches, owns = [], [], []
         piece(0)
         resolve(0)
         back = extras()
@@ -815,16 +941,14 @@ def program(g, T, topo, rank, plan):
             resolve(k)
         ahead.extend((tests[-1], k) for k in fetches[LEAD:])
         ahead.extend(zip(tests, tests[1:]))
+        ahead.extend((k, (tests + fetches)[at]) for k, at in zip(owns, OWN_AT[min(r, 1)]))
         cut = 16 * SC[-1][0]
         for a, b in ((240, 256), (0, cut), (cut, 240)):
             first(a, b)
         count(0, cut)
         count(cut, 256)
         if below is not None:
-            z = c("p0", 256, 512)
-            tt(z, c("p3", 0, 256), c("RP", 256 * r, 256 * r + 256), Op.subtract)
-            act(c("N5"), z, Fn.Relu)
-            act(z, z, Fn.Relu, scale=-1.0)
+            act(c("N5"), c("RP", 256 * r, 256 * r + 256), Fn.Relu, scale=-1.0)
         lower(0, cut)
         lower(cut, 256)
         for k in range(4):
@@ -838,46 +962,58 @@ def program(g, T, topo, rank, plan):
         cp(c("ix", 2, 4), c("junk", 767, 1024, 256))
         tp = c("tp" if below is not None else "t256")
         tt(c("tm"), ind(tp, c("ix")), c("mA"), Op.min)
+        act(c("PS", 32, 96), ind(c("D"), c("ix")), Fn.Identity, bias=c("pc", 5, 6) if r < R - 1 else 0.0)
+        if r == R - 1:
+            tt(c("tB"), ind(tp, c("ix")), c("fr"), Op.add)
+            scan(c("tA"), c("RZ", 0, 64), c("tm"), 0.0, Op.mult, Op.max)
+            for k in range(4):
+                z, own = c("zs", 64 * k, 64 * k + 64), c("tA", 16 * k + 15, 16 * k + 16)
+                if k % 2:
+                    act(z, c("tB"), Fn.Identity, bias=own, scale=-1.0)
+                else:
+                    ts(z, c("tB"), own, Op.subtract)
+                red(c("acc", k, k + 1), z, Op.min, True)
+                ts(c("pl", k, k + 1), c("acc", k, k + 1), c("sf", k, k + 1), Op.not_equal, c("sf", 4 + k, 5 + k), Op.mult)
+                ts(c("so", k, k + 1), c("pl", k, k + 1), own, Op.max)
+            cp(ind(Sw, c("so")), c("PS", 32, 96))
+            cp(ind(c("ST"), c("so")), c("ONE", 0, 64))
+            return
         tt(c("tB"), ind(tp, c("ix")), c("tr"), Op.min)
-        act(c("PS", 32, 96), ind(c("D"), c("ix")), Fn.Abs)
-        if r < R - 1:
-            act(c("Ce"), ind(c("C"), c("ix")), Fn.Identity, bias=off, scale=sgn)
+        act(c("Ce"), ind(c("C"), c("ix")), Fn.Copy)
         scan(c("tA"), c("RZ", 0, 64), c("tm"), 0.0, Op.mult, Op.max)
-        ts(c("iv"), c("tB"), 4096.0, Op.is_ge, 2.0 ** 60, Op.mult)
+        act(c("iv"), c("tB"), Fn.Relu, bias=-4096 * 2.0 ** 56, scale=2.0 ** 56)
         mm(c("p7", 0, 64), c("ID"), c("nt"), True, False)
         mm(c("p7", 0, 64), c("ID"), c("iv"), False, False)
         for k in range(4):
             ts(c("eq", 64 * k, 64 * k + 64), c("tB"), c("tA", 16 * k + 15, 16 * k + 16), Op.is_equal, 2.0 ** (-1 - 32 * k), Op.mult)
             mm(c("p7", 0, 64), c("LD"), c("eq", 64 * k, 64 * k + 64), False, k == 3)
         dup, tb = c("p3", 0, 64), c("PB", 32, 96)
-        if r < 2:
-            ts(c("nb"), c("p7", 0, 64), 0.0, Op.is_ge)
-        ts(dup, c("p7", 0, 64), 0.0, Op.is_ge, 8192.0, Op.mult)
+        ts(c("nb"), c("p7", 0, 64), 0.0, Op.is_ge)
+        ts(dup, c("p7", 0, 64), 0.0, Op.is_ge, 4608.0, Op.mult)
         tt(tb, dup, c("tB"), Op.max)
-        if r < 2:
-            scan(c("qc"), c("ONE", 0, 64), c("nb"), 0.0, Op.add, Op.subtract)
-            ts(c("ov"), c("qc"), c("rm", 0, 1), Op.is_gt)
-            keys(r + 1, 16 * r, 96)
+        scan(c("qc"), c("ONE", 0, 64), c("nb"), 0.0, Op.add, Op.subtract)
+        ts(c("ov"), c("qc"), c("rm", 0, 1), Op.is_gt)
+        keys(r + 1, 16 * r, 96)
         tt(c("tm"), tb, c("mA"), Op.min)
         scan(c("tA"), c("RZ", 0, 64), c("tm"), 0.0, Op.mult, Op.max)
         cp(c("so"), c("tA", 15, 64, 16))
         cp(ind(Sw, c("so")), c("PS", 32, 96))
-        if r < R - 1:
-            cp(ind(Ew, c("so")), c("Ce"))
-        else:
-            cp(ind(c("ST"), c("so")), c("ONE", 0, 64))
+        cp(ind(Ew, c("so")), c("Ce"))
         if r == 0:
             tt(c("rm", 1, 2), c("rm", 0, 1), c("qc", 63, 64), Op.subtract)
             ts(c("rm", 1, 2), c("rm", 1, 2), 0.0, Op.max, 15.0, Op.add)
             ts(c("rm", 0, 1), c("rm", 1, 2), 256.0, Op.min)
-        if r < 2:
-            ranks(r + 1, 16 * r, 96, 2)
+        ranks(r + 1, 16 * r, 96, 2)
 
     cp(c("PS"), ind(Sw, c("qo")))
+    dma("Y", c("S", 0, W, rows=row0), c("fx"), 1 << 16)
+    for a, b in zip(CUTS[1:], CUTS[2:]):
+        dma("Y", c("E", a, b), T.ex[:, a:b], 256 * (b - a))
+    dma("Y", c("ENV"), T.env[:], 1 << 19)
     act(c("PB"), ind(Pw, c("qo")), Fn.Copy)
     keys(0, 0, 256)
     ranks(0, 0, 256, 7)
-    begin_vt()
+    build_vt(0)
     for r in range(R):
         round_(r)
     dma("Y", T.ys[:], c("S", 0, W), 1 << 20)

import numpy as np
from concourse.bass import DstId, RemoteDMATransfer
from concourse.mybir import AluOpType as Op, AxisListType, ActivationFunctionType as Fn

W, EV, R = 4096, 2048, 3
HC = [(0, 3), (3, 8), (8, 15)]
SC = [(0, 4), (4, 8), (8, 12), (12, 15)]
ON_V = {0: 32, 1: 32, 2: 0, 3: 16, 4: 0}
LEAD = 0
C_ON_V = 1
SCAN = 16
PSUM_FROM = 1
OWN_AT = [(14, 14, 16), (10, 11, 13)]
ON_A = 8
CUTS = (0, 2560, 4096)
FETCH = 32
BLOCKS = [("p1", "V", 0, 0), ("p5", "V", 0, 0), ("p2", "V", 0, 0), ("p3", "A", 0, 0), ("p7", "A", 0, 0), ("p2", "A", 0, 0), ("p3", "A", 0, 0), ("p4", "V", 1, 1)]
XC = 480
MUL, PEN = 32768.0, 16384.0
NEUTRAL, NONE, PO = 4112, 4176, 16
PLANS = [(0.87, 1.3, 0.87, 100.0, 2200.0, 80.0, 200.0, 1000.0), (0.92, 1.5, 0.92, 140.0, 2600.0, 90.0, 210.0, 1000.0),
         (1.0, 1.6, 1.0, 170.0, 1600.0, 100.0, 260.0, 900.0), (1.15, 1.7, 1.15, 200.0, 3000.0, 115.0, 200.0, 1100.0)]
SCA, AMP, SPAN = 3.8, 300.0, 150
TRIES = 11000
SEED = 5
EVERY = 20
COPY = 50
SLACK = 0.003
B, F, I, U = "bfloat16", "float32", "int32", "uint16"
_SB = {
    "E": (4176, B), "S": (4176, B), "VT": (4128, F), "ENV": (EV, B), "PLC": (PO + 4192, F), "ST": (4176, F),
    "qi": (16, I), "qo": (16, U), "wi": (2, I), "wf": (8, F), "wj": (4, I), "thi": (8, I), "thb": (8, I), "thf": (8, F), "thc": (2, F),
    "ec": (256, B), "ee": (256, B), "e1": (256, B), "In256": (128, B), "sti": (256, I), "f1": (256, F), "f2": (256, F), "fx": (256, B), "yc": (256, F),
    "pi": (8, I), "pc": (24, F), "qg": (128, F), "qq": (256, F), "jm": (256, F), "ri": (32, I), "rj": (32, I), "wt16": (32, F),
    "BO": (128, B), "ID": (128, B), "IDF": (128, F), "I8": (128, B), "In22": (128, B), "In44": (128, B), "BOm": (128, B), "IM": (128, B), "CST": (256, B), "rs": (16, F), "sf": (8, F), "fr": (64, F), "I4": (128, B), "In1": (128, B), "BO1k": (128, B),
    "BOz": (128, B), "BOh": (128, B), "BOn": (128, B), "LD": (128, B), "DG": (128, B), "PK": (128, B), "WB": (512, B), "D16": (256, B), "LK": (2048, B),
    "tg": (16, F), "ti": (48, I), "TGh": (128, B), "TGl": (128, B), "ph": (16, F), "N15": (256, B),
    "EXi": (16, I), "EX": (16, U), "RM": (1024, B), "RZ": (256, B), "RZ2": (256, B), "ONE": (256, B), "JT": (96, B), "JT1": (256, B), "K2": (256, B),
    "OD": (32, B), "thr": (64, F), "nt": (64, B), "iv": (64, B), "qt": (64, F), "tr": (64, F), "mA": (64, F), "FX": (96, F), "G8": (8, F),
    "X": (48 * R, B), "RP": (256 * R, B), "SV": (256 * R, B), "fu": (256, F), "b8": (16, F), "C": (272, B), "CU": (256 * R, B), "YE": (256, B), "sp": (16, B), "vp": (16, F),
    "AB": (576, I), "MM": (288, I), "SS": (576, I), "HU": (336, U), "zi": (16, I), "zu": (16, U),
    "FF": (3840, B), "FU": (768, B), "FO": (1024, B), "df": (288, F), "sl": (288, F), "SU": (288, U), "nx": (48, F), "G2": (4096, F), "MS": (4096, F),
    "fo": (64, F), "fm": (48, F), "KO": (16, F), "ta": (16, F), "tu": (16, U), "t256": (272, F), "tp": (272, F), "M": (256, B), "NG": (256, B), "N5": (256, B),
    "TH": (512, B), "BOp": (128, B), "BO8": (128, B), "EVg": (256, B), "M5": (256, B), "D": (272, B), "good": (256, B), "pre": (256, B), "junk": (1024, B), "acc": (4, F), "ix": (4, U),
    "tB": (64, F), "tm": (64, F), "tA": (64, F), "eq": (256, B), "nd": (64, F), "so": (4, U), "Ce": (64, B),
    "PS": (256, B), "PB": (256, F), "nb": (64, B), "qc": (64, F), "ov": (64, B), "rm": (4, F), "KB": (256, F), "KA": (256, F), "cm": (4096, B),
    "pl": (4, F), "po": (2, U), "zs": (512, F), "vo": (2, U),
}
for _k in range(8):
    _SB["p%d" % _k] = (512, F)
_AT, _end = {}, 0
for _k, (_n, _d) in _SB.items():
    if _d == F and _n <= 64:
        _AT[_k] = ("few", _end)
        _end += -(-_n // 16) * 16
    else:
        _AT[_k] = (_k, 0)
SCRATCH = {k: ("psum" if k[1:].isdigit() and k[0] == "p" else "sbuf", [128, n], d) for k, (n, d) in _SB.items() if _AT[k][0] == k}
SCRATCH["few"] = ("sbuf", [128, _end], F)
SEMAPHORES = ["V", "A", "P", "G"] + ["d%d" % k for k in range(32)] + [a + str(r) for a in ("lo", "up", "rp", "cu", "ls", "lr", "lc") for r in range(R)]


def rank_program(g, core, T, topo):
    rank = T.rank_of(core)
    if rank is None:
        return
    if not _ORDER:
        program(g, T, topo, 1, True)
    program(g, T, topo, rank, False)


_ORDER = {}


def program(g, T, topo, rank, plan):
    core = T.cores[rank]
    below = T.cores[rank - 1] if rank > 0 else None
    above = T.cores[rank + 1] if rank + 1 < len(T.cores) else None
    Q = {"V": g.vector, "A": g.scalar, "P": g.tensor, "G": g, "Y": g.sync}
    ops, hist, bank, lastq, soft, line, ahead, tag, seen = [], {}, {}, {}, [], {}, [], [-1], {}

    def c(name, lo=0, hi=None, step=1, rows=None):
        hi = _SB[name][0] if hi is None else hi
        name, base = _AT[name]
        lo, hi = lo + base, hi + base
        where, shape, dt = SCRATCH[name]
        ps = slice(0, 128) if rows is None else rows
        return (T[name][ps, lo:hi:step] if step != 1 else T[name][ps, lo:hi], [(name, lo, hi)], [], len(range(lo, hi, step)), dt in (B, U), where == "psum", False)

    def ind(win, off):
        return (win[0].indirect(off[0]), win[1], off[1], 16 * off[3], win[4], False, True)

    def emit(eng, outs, ins, call, dur, sem=None, inc=1, chain=True, after=(), lat=(0, 0), size=0, skip=()):
        k = len(ops)
        wr = [x for o in outs for x in o[1]]
        rd = [x for o in outs for x in o[2]] + [x for o in ins if isinstance(o, tuple) for x in o[1] + o[2]]
        deps, order = set(), set(after)
        for is_wr, acc in ((True, wr), (False, rd)):
            for (n, lo, hi) in acc:
                if SCRATCH[n][0] == "psum":
                    st = bank.setdefault(n, [eng, [], []])
                    if st[0] != eng:
                        st[:] = [eng, [], st[1]]
                    deps.update(st[2])
                    if eng == "P":
                        order.update(st[1][-1:])
                    if k not in st[1]:
                        st[1].append(k)
                    if eng == "P":
                        continue
                for (a, b, w, j) in hist.get(n, []):
                    if a < hi and lo < b and (w or is_wr) and j not in skip:
                        deps.add(j)
        for (n, lo, hi) in rd:
            hist.setdefault(n, []).append((lo, hi, False, k))
        for (n, lo, hi) in wr:
            h = hist.setdefault(n, [])
            h[:] = [x for x in h if x[3] in skip or not (lo <= x[0] and x[1] <= hi)] + [(lo, hi, True, k)]
        deps.discard(k)
        order.discard(k)
        if size and eng in lastq:
            order.add(lastq[eng])
        if size:
            lastq[eng] = k
        keys = [(tag[0], eng, sem, tuple(wr), tuple(rd)), (tag[0], eng, sem, tuple(wr))]
        keys.append((tag[0], eng, tuple((n, 0 if n in ("X", "RP", "SV") else lo) for n, lo, hi in wr)))
        for x in keys:
            seen[x] = seen.get(x, 0) + 1
        ops.append(dict(eng=eng, deps=deps, order=order, keys=[(x, seen[x]) for x in keys[:2]], twin=keys[2] + (seen[keys[2]],), call=call, dur=dur, sem=sem or eng, inc=inc, chain=chain, lat=lat, size=size))
        return k

    def issue():
        n = len(ops)
        for a, b in ahead:
            ops[b]["order"].add(a)
        rank_of, todo = {}, list(range(n - 1, -1, -1))
        while todo:
            k = todo[-1]
            miss = [j for j in ops[k]["deps"] | ops[k]["order"] if j not in rank_of]
            if miss:
                todo.extend(sorted(miss, reverse=True))
            else:
                rank_of.setdefault(todo.pop(), len(rank_of))
        ops[:] = [dict(ops[k], **{f: {rank_of[j] for j in ops[k][f]} for f in ("deps", "order")}) for k in sorted(range(n), key=rank_of.get)]
        soft[:] = [(rank_of[a], rank_of[b]) for a, b in soft if rank_of[a] < rank_of[b]]
        succ, more = [[] for _ in ops], [[] for _ in ops]
        for k, o in enumerate(ops):
            for j in o["deps"] | o["order"]:
                succ[j].append(k)
        for a, b in soft:
            more[a].append(b)
        pre = [sorted(o["deps"]) for o in ops]
        aft = [sorted(o["order"]) for o in ops]

        def run(p, took, reach=0.0, shift=(), times=False):
            dur = [o["dur"][0] + p[0] * (o["dur"][1] + p[1] * o["dur"][2] + SCA * o["dur"][3]) + p[2] * o["dur"][4] for o in ops]
            lat = [o["lat"][0] * p[4] + o["lat"][1] for o in ops]
            hop, make = p[3], not took
            start, done, free, wire = [0.0] * n, [0.0] * n, {e: 0.0 for e in list(Q) + [None]}, 0.0

            def at(j):
                return max([done[i] + hop for i in pre[j]] + [done[i] if ops[j]["eng"] is None else start[i] for i in aft[j]] + [0.0])
            if make:
                prio = [0.0] * n
                for k in range(n - 1, -1, -1):
                    prio[k] = dur[k] + lat[k] + ops[k]["size"] / 200.0 + max([prio[j] + hop for j in succ[k]] + [prio[j] for j in more[k]], default=0.0)
                prio = [x + y for x, y in zip(prio, shift)]
                left = [len(o["deps"] | o["order"]) for o in ops]
                ready = {e: {} for e in free}
                for k in range(n):
                    if left[k] == 0:
                        ready[ops[k]["eng"]][k] = 0.0
            for step in range(n):
                if make:
                    t0, e = min(((max(free[e], min(d.values())), e) for e, d in ready.items() if d), key=lambda x: x[0])
                    k = max((j for j, t in ready[e].items() if t <= t0 + hop * reach), key=lambda j: (prio[j], -j))
                    t = max(ready[e].pop(k), free[e])
                    took.append(k)
                else:
                    k = took[step]
                    e = ops[k]["eng"]
                    t = max(at(k), free[e])
                start[k], done[k] = t, t + dur[k] + lat[k]
                if ops[k]["size"]:
                    wire = max(wire, t + p[7]) + ops[k]["size"] / p[6] + 60.0
                    done[k] = wire + p[7]
                if e is not None:
                    free[e] = t + dur[k]
                if make:
                    for j in succ[k]:
                        left[j] -= 1
                        if left[j] == 0:
                            ready[ops[j]["eng"]][j] = at(j)
            return (start, done, dur) if times else max(done)

        def pack(order, edges, dur, least):
            at, lo, hi = [0.0] * n, {e: [] for e in Q}, {e: [] for e in Q}
            for k in order:
                t = max([at[j] + lag for j, lag in edges[k]] + [least[k]])
                e = ops[k]["eng"]
                if e is not None:
                    a, b = lo[e], hi[e]
                    i = len(a)
                    while i > 0 and b[i - 1] > t:
                        i -= 1
                    while i < len(a) and t + dur[k] > a[i]:
                        t = max(t, b[i])
                        i += 1
                    a.insert(i, t)
                    b.insert(i, t + dur[k])
                at[k] = t
            return at

        def justify(p, took, noise):
            start, done, dur = run(p, took, times=True)
            fore, back = [[] for _ in ops], [[] for _ in ops]
            for k in range(n):
                for j, lag in [(j, done[j] - start[j] + p[3]) for j in pre[k]] + [(j, done[j] - start[j] if ops[k]["eng"] is None else dur[j]) for j in aft[k]]:
                    fore[k].append((j, lag))
                    back[j].append((k, dur[k] + lag - dur[j]))
            late = pack(sorted(range(n), key=lambda k: (-start[k] - dur[k], -k)), back, dur, [done[k] - start[k] - dur[k] for k in range(n)])
            key = [-late[k] - dur[k] + noise[k] for k in range(n)]
            for k in range(n):
                key[k] = max([key[k]] + [key[j] for j, _ in fore[k]])
            early = pack(sorted(range(n), key=lambda k: (key[k], k)), fore, dur, [0.0] * n)
            return sorted(range(n), key=lambda k: (early[k], k))

        fixed = [([o["dur"][0] + p[0] * (o["dur"][1] + p[1] * o["dur"][2] + SCA * o["dur"][3]) + p[2] * o["dur"][4] for o in ops],
                  [o["lat"][0] * p[4] + o["lat"][1] for o in ops]) for p in PLANS]
        eng, size = [o["eng"] for o in ops], [o["size"] for o in ops]
        behind, near = [], []
        for k in range(n):
            far = 0
            for j in pre[k]:
                far |= behind[j]
            near.append([j for j in pre[k] if not far >> j & 1])
            for j in pre[k]:
                far |= 1 << j
            behind.append(far)

        def times(i, took, known=None, same=0):
            dur, lat = fixed[i]
            hop, start, done, why, free, last, wire = PLANS[i][3], [0.0] * n, [0.0] * n, [-1] * n, dict.fromkeys(Q, 0.0), dict.fromkeys(Q, -1), 0.0
            if same:
                start, done, why = list(known[0]), list(known[1]), list(known[2])
                for e in Q:
                    for k in rows[e]:
                        if place[k] < same and start[k] + dur[k] > free[e]:
                            free[e], last[e] = start[k] + dur[k], k
                            break
                wire = max([done[k] - PLANS[i][7] for k in moved if place[k] < same] + [0.0])
            for k in took[same:]:
                e, t, w = eng[k], -hop, -1
                for j in near[k]:
                    if done[j] > t:
                        t, w = done[j], j
                t += hop
                if e is None:
                    for j in aft[k]:
                        if done[j] > t:
                            t, w = done[j], j
                else:
                    if free[e] > t:
                        t, w = free[e], last[e]
                    free[e], last[e] = t + dur[k], k
                start[k], why[k], done[k] = t, w, t + dur[k] + lat[k]
                if size[k]:
                    wire = max(wire, t + PLANS[i][7]) + size[k] / PLANS[i][6] + 60.0
                    done[k] = wire + PLANS[i][7]
            return start, done, why

        held, place, rows, moved = [], [0] * n, {}, [k for k in range(n) if size[k]]

        def hold(took):
            held[:] = took
            for at, k in enumerate(took):
                place[k] = at
            for e in Q:
                rows[e] = [k for k in reversed(took) if eng[k] == e]

        def worth_of(took, i0, bound):
            got, same = [None] * len(PLANS), 0
            while bound and same < n and took[same] == held[same]:
                same += 1
            for i in [(i0 + d) % len(PLANS) for d in range(len(PLANS))]:
                got[i] = times(i, took, bound and bound[i], same)
                if bound and max(got[i][1]) > max(bound[i][1]) + 0.004 * PLANS[i][5] * 1000:
                    return 1e9, got
            return sum(max(x[1]) / p[5] for x, p in zip(got, PLANS)) / 1000, got

        def move(now, i, rs):
            took, (start, done, why) = now[1], now[2][i]
            k, held = max(range(n), key=lambda x: done[x]), []
            while why[k] >= 0:
                if eng[why[k]] == eng[k] and why[k] not in pre[k] and why[k] not in aft[k]:
                    held.append(k)
                k = why[k]
            if not held:
                return took
            x = held[int(rs.randint(len(held)))]
            row = [k for k in took if eng[k] == eng[x]]
            y = row[max(0, row.index(x) - 1 - int(rs.geometric(0.5) - 1))]
            key = [0.0] * n
            for at, k in enumerate(took):
                key[k] = float(at)
            if rs.rand() < 0.5:
                to, todo = key[y] - 0.5, [x]
                while todo:
                    k = todo.pop()
                    key[k] = to
                    todo.extend(j for j in near[k] + aft[k] if key[j] > to)
            else:
                to, todo = key[x] + 0.5, [y]
                while todo:
                    k = todo.pop()
                    key[k] = to
                    todo.extend(j for j in succ[k] if key[j] < to)
            return sorted(range(n), key=lambda k: (key[k], k))

        twin = {}
        for k, o in enumerate(ops):
            twin.setdefault(o["twin"][1:], {})[o["twin"][0]] = k

        def copy_round(i, took, a, b):
            start = times(i, took)[0]
            both = [(x[a], x[b]) for x in twin.values() if a in x and b in x]
            shift = min(start[y] for _, y in both if eng[y] == "G") - min(start[x] for x, _ in both if eng[x] == "G")
            key = list(start)
            for x, y in both:
                key[y] = start[x] + shift
            for k in range(n):
                for j in pre[k] + aft[k]:
                    key[k] = max(key[k], key[j])
            return sorted(range(n), key=lambda k: (key[k], k))

        best = now = None
        rs = np.random.RandomState(SEED)
        for t in range(TRIES if plan else 0):
            if t < 12:
                took = []
                run(PLANS[t % 4], took, (0.5, 1.0, 2.0)[t // 4], [0.0] * n)
                for _ in range(3):
                    took = justify(PLANS[t % 4], took, [0.0] * n)
            elif t % COPY < 2:
                a = int(rs.randint(R))
                took = copy_round(1, now[1], a, (a + 1 + int(rs.randint(R - 1))) % R)
                took = justify(PLANS[1], took, [0.0] * n) if t % COPY else took
            elif t % EVERY == 0:
                lo = int(rs.randint(n))
                took = justify(PLANS[t % 4], now[1], [AMP * float(rs.randn()) if lo <= k < lo + SPAN else 0.0 for k in range(n)])
            else:
                took = move(now, t % 4, rs)
            worth, got = worth_of(took, t, now[2] if t >= 12 else None)
            if best is None or worth < best[0]:
                best = (worth, took, got)
            if t < 12:
                now = best
                hold(now[1])
            elif worth < now[0] + SLACK * (1 - t / TRIES) * float(rs.rand()):
                now = (worth, sorted(range(n), key=lambda k: (got[1][0][k], k)), got)
                hold(now[1])
        if plan:
            for at, k in enumerate(best[1]):
                _ORDER.update({x: at for x in ops[k]["keys"]})
            return
        place = []
        for k, o in enumerate(ops):
            place.append(max([_ORDER.get(o["keys"][0], _ORDER.get(o["keys"][1], 0))] + [place[j] for j in pre[k] + aft[k]]))
        took = sorted(range(n), key=lambda k: (place[k], k))
        seq = {e: [k for k in took if ops[k]["eng"] == e] for e in Q}
        top, val = {}, {}
        for k in [k for e in Q for k in seq[e]] + [k for k in range(n) if ops[k]["eng"] is None]:
            top[ops[k]["sem"]] = val[k] = top.get(ops[k]["sem"], 0) + ops[k]["inc"]
        for e in Q:
            seen = {}
            for k in seq[e]:
                want = {}
                for j in ops[k]["deps"]:
                    s = ops[j]["sem"]
                    if seen.get(s, 0) < val[j] and not e == s == "P":
                        want[s] = max(want.get(s, 0), val[j])
                for s, v in sorted(want.items()):
                    Q[e].wait_ge(T.sem[s], v)
                    seen[s] = v
                r = ops[k]["call"]()
                if ops[k]["chain"]:
                    r.then_inc(T.sem[ops[k]["sem"]], ops[k]["inc"])
        for s, v in sorted(top.items()):
            g.wait_ge(T.sem[s], v)

    def follow(key):
        if key in line:
            soft.append((line[key], len(ops) - 1))
        line[key] = len(ops) - 1

    def ap(x):
        return x[0] if isinstance(x, tuple) else x

    def cost(o, i, per, fix=50.0):
        if o[6] or i[6]:
            return (fix, 0, 0, o[3], 0) if o[6] else (fix, 0, i[3], 0, 0)
        return (0, max(64.0, i[3] * per), 0, 0, 0)

    def half(*xs):
        return 0.5 if all(x[4] for x in xs) else 1.0

    def ts(o, i, s1, op0, s2=None, op1=None):
        if op1 is None:
            emit("V", [o], [i, s1], lambda: g.vector.tensor_scalar(o[0], i[0], ap(s1), None, op0), cost(o, i, half(o, i)))
        else:
            emit("V", [o], [i, s1, s2], lambda: g.vector.tensor_scalar(o[0], i[0], ap(s1), ap(s2), op0, op1), cost(o, i, half(o, i)))

    def tt(o, a, b, op):
        emit("V", [o], [a, b], lambda: g.vector.tensor_tensor(o[0], a[0], b[0], op), cost(o, a, 1.0 if a[5] or b[5] else 2.0))

    def cp(o, i):
        emit("V", [o], [i], lambda: g.vector.tensor_copy(o[0], i[0]), cost(o, i, half(o, i)))

    def ms(o, v):
        emit("V", [o], [], lambda: g.vector.memset(o[0], v), cost(o, o, half(o)))

    def red(o, i, op, ab=False):
        emit("V", [o], [i], lambda: g.vector.tensor_reduce(o[0], i[0], AxisListType.X, op, apply_absolute_value=ab), cost(o, i, 1.0))

    def scan(o, d0, d1, init, op0, op1):
        emit("V", [o], [d0, d1, init], lambda: g.vector.tensor_tensor_scan(o[0], d0[0], d1[0], ap(init), op0, op1), cost(o, d0, half(o, d0, d1)))

    def act(o, i, fn, bias=0.0, scale=1.0, accum=None):
        emit("A", [o] + ([accum] if accum else []), [i, bias, scale],
             lambda: g.scalar.activation(o[0], i[0], fn, bias=ap(bias), scale=ap(scale), accum_out=ap(accum)), cost(o, i, 1.0, 65.0))

    def mm(o, l, r, start, stop):
        emit("P", [o], [l, r], lambda: g.tensor.matmul(o[0], l[0], r[0], start, stop), (0, 0, 0, 0, max(64, r[3]) * (1 if r[4] else 4)))

    def mms(parts):
        for k, (o, l, r) in enumerate(parts):
            mm(o, l, r, k == 0, k == len(parts) - 1)

    def iota(o, pat, base, cm):
        if SCRATCH[o[1][0][0]][2] == I:
            emit("G", [o], [], lambda: g.iota(o[0], pat, base, cm), (130, 2 * o[3], 0, 0, 0))
        else:
            emit("G", [o], [], lambda: g.iota(o[0], pat, base, cm, allow_small_or_imprecise_dtypes=True), (130, 2 * o[3], 0, 0, 0))

    def fill(o, v):
        iota(o, [[0, o[3]]], v, 0)

    def sc(o, i, scale=1.0, bias=0.0):
        act(o, i, Fn.Identity, bias=bias, scale=scale)

    n_dma = [0]

    def dma(eng, o, i, size, skip=()):
        n_dma[0] += 1
        return emit(eng, [o] if isinstance(o, tuple) else [], [i], lambda: Q[eng].dma_start(ap(o), ap(i)), (100, 0, 0, 0, 0),
                    sem="d%d" % (n_dma[0] - 1), inc=16, size=size, skip=skip)

    def mask_of(es):
        return sum(1 << e for e in es)

    def halves(src, dst, k):
        es = topo.engines(src, dst)
        return es[:len(es) // 2] if k == 0 else es[len(es) // 2:]

    def landed(o, sem, n, after, lat):
        emit(None, [o], [], None, (0, 0, 0, 0, 0), sem=sem, inc=n, after=[after], lat=lat)

    def dst_id(dst):
        rid, pid, _ = topo.addr(dst)
        return DstId(rid=rid, pnc=pid)

    row0 = slice(0, 128, 16)
    dma("Y", c("qi"), T.qu[:], 8192)
    dma("Y", c("S", 0, W), T.su[:], 1 << 20)
    dma("A", c("wi"), T.wt[:], 1024)
    dma("A", c("thi", rows=slice(0, 1)), T.th[:], 32)
    dma("Y", c("ec"), T.su[row0, :], 1 << 16)
    dma("Y", c("sti"), T.st[:], 1 << 17)
    dma("Y", c("E", 0, CUTS[1]), T.ex[:, 0:CUTS[1]], 256 * CUTS[1])
    iota(c("pi", 0, 1), [[0, 1]], 0, 1)
    iota(c("qq"), [[1, 256]], 0, 0)
    iota(c("jm"), [[0, 16], [1, 16]], 0, 0)
    iota(c("qg"), [[1, 8], [0, 16]], 0, 0)
    iota(c("JT1"), [[-2, 16], [-32, 16]], 0, 0)
    iota(c("EXi"), [[1, 16]], 0, 0)
    iota(c("ri", 0, 16), [[-1, 16]], 16, 1)
    iota(c("ri", 16, 32), [[1, 16]], 128, -1)
    ms(c("FF", 0, 1024), 1.0)
    scan(c("PLC", PO, PO + 1024), c("FF", 0, 1024), c("FF", 0, 1024), -1.0, Op.mult, Op.add)
    sc(c("PLC", PO + 1024, PO + 2048), c("PLC", PO, PO + 1024), 1.0, 1024.0)
    sc(c("PLC", PO + 2048, PO + 3072), c("PLC", PO, PO + 1024), 1.0, 2048.0)
    sc(c("PLC", PO + 3072, PO + 3584), c("PLC", PO, PO + 512), 1.0, 3072.0)
    ts(c("PLC", PO + 3584, PO + 4192), c("PLC", PO, PO + 608), 3584.0, Op.add)
    ms(c("PLC", 0, PO), 2.0 ** 28)
    ms(c("S", W, 4176), -64.0)
    ms(c("E", W, 4176), 240.0)
    ms(c("VT", W, 4128), 2.0 ** 25)
    ms(c("RZ"), 1.0)
    ms(c("ONE"), 1.0)
    ms(c("RZ", 0, 256, 16), 0.0)
    ts(c("pi", 1, 2), c("pi", 0, 1), 15, Op.bitwise_and)
    ts(c("pi", 2, 3), c("pi", 0, 1), 4, Op.arith_shift_right)
    ts(c("pi", 3, 4), c("pi", 0, 1), 1, Op.arith_shift_right)
    ts(c("pi", 4, 5), c("pi", 0, 1), 1, Op.bitwise_and)
    cp(c("pc", 0, 3), c("pi", 0, 3))
    cp(c("pc", 16, 17), c("pi", 3, 4))
    ts(c("pc", 17, 18), c("pi", 4, 5), -65280.0, Op.mult, 65536.0, Op.add)
    ts(c("pc", 18, 19), c("pi", 4, 5), 65280.0, Op.mult, -65536.0, Op.add)
    ts(c("PK", 0, 128, 2), c("qq", 0, 64), c("pc", 16, 17), Op.is_equal, c("pc", 17, 18), Op.mult)
    ts(c("PK", 1, 128, 2), c("qq", 0, 64), c("pc", 16, 17), Op.is_equal, c("pc", 18, 19), Op.mult)
    pcol, lcol, gcol = c("pc", 0, 1), c("pc", 1, 2), c("pc", 2, 3)
    ts(c("BO1k"), c("qg"), gcol, Op.is_equal, 1024.0, Op.mult)
    ts(c("ID"), c("qq", 0, 128), pcol, Op.is_equal)
    ts(c("D16"), c("jm"), lcol, Op.is_equal)
    ts(c("qi"), c("qi"), 8191, Op.bitwise_and)
    ts(c("qo"), c("qi"), 4111.0, Op.min)
    ts(c("K2"), c("D16"), 2.0 ** 24 - 1, Op.mult, -2.0 ** 24, Op.add)
    ts(c("RZ2"), c("RZ"), 2.0 ** 26, Op.mult, -2.0 ** 26, Op.add)
    ts(c("BOz"), c("BO1k"), MUL / 1024, Op.mult)
    ts(c("BOh"), c("BO1k"), MUL / 2048, Op.mult)
    ts(c("IDF"), c("qq", 0, 128), pcol, Op.is_equal)
    ts(c("BOm"), c("BO1k"), -MUL / 2048, Op.mult)
    ts(c("IM"), c("ID"), MUL, Op.mult)
    fill(c("CST", 0, 16 * ON_A), 127)
    iota(c("CST", 16 * ON_A, 256), [[-16, 16 - ON_A], [0, 16]], 255 - 8 * ON_A, 0)
    ts(c("pc", 3, 4), lcol, 15.0, Op.is_equal, 305.0, Op.mult)
    tt(c("pc", 3, 4), c("pc", 3, 4), lcol, Op.add)
    ts(c("DG"), c("ID"), c("pc", 3, 4), Op.mult, -MUL, Op.mult)
    ts(c("pc", 6, 7), lcol, 4096.0, Op.add)
    ts(c("pc", 4, 5), lcol, 0.0, Op.is_equal, 256.0, Op.mult)
    ts(c("pc", 5, 6), lcol, 0.0, Op.is_equal, -256.0, Op.mult)
    ts(c("f1"), c("sti"), 1.0, Op.is_equal, -256.0, Op.mult)
    tt(c("fx"), c("f1"), c("ec"), Op.add)
    cp(c("EX"), c("EXi"))
    ts(c("BO"), c("BO1k"), 1.0 / 1024, Op.mult)
    ts(c("wj", 0, 2), c("wi"), 4032, Op.bitwise_and)
    ts(c("wj", 2, 4), c("wi"), 63, Op.bitwise_and)
    cp(c("wf", 0, 4), c("wj"))
    cp(c("wf", 4, 6), c("wi"))
    ts(c("wf", 6, 8), c("wi"), -1.0, Op.mult)
    for k in range(4):
        sc(c("WB", 128 * k, 128 * k + 128), c("BO"), c("wf", k, k + 1))
    ts(c("ri"), c("ri"), 15, Op.bitwise_and)
    ts(c("rj"), c("ri"), 3.0, Op.add)
    ts(c("rj"), c("rj"), 2, Op.arith_shift_right)
    tt(c("rj"), c("rj"), c("ri"), Op.add)
    ts(c("wt16"), c("rj"), 1.0, Op.max, 235.0, Op.add)
    fill(c("LK", 0, 1024), 0)
    for k in (1024, 1536):
        ms(c("LK", k, k + 512), 0.0)
    ts(c("G8"), c("qq", 0, 8), gcol, Op.is_equal)
    for k in range(8):
        sc(c("LK", 16 * k, 16 * k + 129 * 15 + 1, 129), c("wt16", 0, 16), c("G8", k, k + 1))
    ts(c("tg"), c("wt16", 16, 32), 80.0, Op.mult, 3917.0 + 11328.0, Op.add)
    ts(c("qt", 16, 32), c("D16", 0, 16), -30208.0, Op.mult)
    tt(c("ti", 0, 16), c("tg"), c("qt", 16, 32), Op.add)
    ts(c("ti", 16, 32), c("ti", 0, 16), 0xFF00, Op.bitwise_and)
    ts(c("ti", 32, 48), c("ti", 0, 16), 0xFF, Op.bitwise_and)
    for name, lo in (("TGh", 16), ("TGl", 32)):
        ts(c(name, 0, 16), c("ti", lo, lo + 16), -1.0, Op.mult)
        for k in (16, 32, 64):
            sc(c(name, k, 2 * k), c(name, 0, k))
    mm(c("p0", 0, 16), c("PK"), c("D16", 0, 16), True, True)
    sc(c("ph"), c("p0", 0, 16))
    ms(c("RM", 0, 1), 2.0 ** 26)
    tt(c("RM", 1, 16), c("ph", 0, 15), c("ph", 1, 16), Op.subtract)
    for k in (16, 32, 64, 128):
        sc(c("RM", k, 2 * k), c("RM", 0, k))
    ts(c("pc", 23, 24), lcol, 15.0, Op.is_equal, -1.0, Op.mult)
    sc(c("N15"), c("ONE"), c("pc", 23, 24))
    sc(c("BOn"), c("BO"), -2.0 ** 45)
    fill(c("nx"), 0)
    fill(c("FU", 256, 768), 1)
    sc(c("OD"), c("D16", 0, 32), 2.0 ** 25, -2.0 ** 25)
    fill(c("FX"), 0)
    for h, k in ((0, 1), (48, 0)):
        sc(c("FX", h, h + 16), c("ONE", 0, 16), c("wf", 6 + k, 7 + k))
        sc(c("FX", h + 16, h + 31), c("ONE", 0, 15), c("wf", 4 + k, 5 + k))
        sc(c("FX", h + 32, h + 47), c("ONE", 0, 15), c("wf", 4 + k, 5 + k))
    sc(c("I8"), c("ID"), 8192.0)
    sc(c("In22"), c("ID"), -2.0 ** 22)
    sc(c("In44"), c("ID"), -2.0 ** 44)
    sc(c("I4"), c("ID"), 4608.0)
    sc(c("In1"), c("ID"), -1.0)
    sc(c("In256"), c("ID"), -256.0)
    iota(c("JT"), [[-2, 96]], 0, 0)
    ms(c("qt"), 0.25)
    fill(c("nd"), 0)
    scan(c("thr"), c("qt"), c("nd"), 2.0 ** 51, Op.mult, Op.add)
    tt(c("qt", 0, 16), c("thr", 0, 16), c("D16", 0, 16), Op.mult)
    sc(c("nt"), c("thr"), -1.0)
    red(c("pc", 13, 14), c("qt", 0, 16), Op.add)
    sc(c("LD"), c("BO"), c("pc", 13, 14))
    iota(c("tr"), [[1, 64]], 4112, 0)
    iota(c("mA"), [[1, 64]], 4113, 0)
    tt(c("mA"), c("mA"), c("D16", 0, 64), Op.mult)
    sc(c("mA"), c("mA"), 1.0, -1.0)
    tt(c("pc", 7, 8), c("pc", 3, 4), lcol, Op.subtract)
    ts(c("pc", 8, 9), c("pc", 7, 8), -31.0, Op.add, MUL, Op.mult)
    ts(c("pc", 7, 8), c("pc", 7, 8), -15.0, Op.add, MUL, Op.mult)
    ts(c("pc", 9, 13), c("qq", 0, 64, 16), lcol, Op.add)
    sc(c("sf", 0, 4), c("pc", 9, 13), 1.0 / 128)
    sc(c("sf", 4, 8), c("pc", 9, 13), 1.0, 4112.0)
    sc(c("fr"), c("qq", 0, 64), 1.0 / 128)
    ts(c("pc", 9, 11), c("pc", 9, 11), -1.0, Op.mult, -0.5, Op.add)
    emit("G", [c("thb")], [c("thi")], lambda: g.partition_broadcast(T.thb[:], T.thi[0:1, :], 128), (180, 0, 0, 0, 0))
    tt(c("thf"), c("thb"), c("G8"), Op.mult)
    red(c("thc", 0, 1), c("thf"), Op.add)
    fill(c("C", 256, 272), 0)
    fill(c("D", 256, 272), 0)
    fill(c("tp" if below is not None else "t256", 256, 272), 8000)
    cp(c("pi", 5, 6), c("thc", 0, 1))
    ts(c("pi", 6, 7), c("pi", 5, 6), 4032, Op.bitwise_and)
    ts(c("pi", 7, 8), c("pi", 5, 6), 63, Op.bitwise_and)
    cp(c("pc", 20, 22), c("pi", 6, 8))
    sc(c("pc", 14, 15), c("pc", 20, 21), -MUL)
    sc(c("pc", 15, 16), c("pc", 21, 22), -MUL, MUL / 4)
    for k in (0, 1):
        sc(c("TH", 256 + 128 * k, 384 + 128 * k), c("ID"), c("pc", 14 + k, 15 + k))
    if below is not None:
        for k in (0, 1):
            sc(c("TH", 128 * k, 128 * k + 128), c("I8"), c("pc", 20 + k, 21 + k))
        sc(c("BOp"), c("BO"), 2.0 ** 30)
        sc(c("BO8"), c("BO"), -8192.0)
    for r in range(R):
        if below is None:
            sc(c("X", 48 * r, 48 * r + 16), c("ONE", 0, 16), 240.0)
        if above is None:
            sc(c("X", 48 * r + 32, 48 * r + 48), c("ONE", 0, 16), 240.0)

    Ew, Sw, Vw, Pw = c("E"), c("S"), c("VT"), c("PLC", PO)

    def keys(r, lo, hi):
        for bk in ("p7", "p6") if r else ("p7", "p6", "p0"):
            parts = [(c(bk, lo, hi), c("ID"), c("JT1" if r == 0 else "JT", lo, hi))]
            if bk == "p7":
                parts.append((c(bk, lo, hi), c("ID"), c("K2", lo, hi)))
            parts.append((c(bk, lo, hi), c("BO1k"), c("PS", lo, hi)))
            if r:
                parts += [(c(bk, 32, 96), c("In44"), c("nb")), (c(bk, 32, 96), c("In22"), c("ov"))]
            mms(parts)

    def ranks(r, lo, hi, on_v):
        n = hi - lo
        for a in range(lo, hi, 128):
            b = min(a + 128, hi)
            scan(c("KA", a, b), c("RZ2", 0, b - a), c("p7", a, b), 0.0, Op.add, Op.max)
        if r:
            act(c("KB", lo, hi), c("p6", lo, hi), Fn.Copy)
        kb_v, kb_a = (c("KB", lo, hi), c("KB", lo, hi)) if r else (c("p6", lo, hi), c("p0", lo, hi))
        z = c("p4", lo, hi)
        mm(z, c("DG"), c("ONE", 0, n), True, False)
        mm(z, c("IDF"), c("PB", lo, hi), False, False)
        if r:
            mm(c("p4", 32, 96), c("I4"), c("ov"), False, False)
        ks = list(range(n // 16))
        kv, ka = ks[:on_v], ks[on_v:]
        if r == 0:
            mm(z, c("IM"), c("CST"), False, False)
            order = [k for pair in zip(range(ON_A), range(ON_A, 16)) for k in pair] + list(range(2 * ON_A, 16))
            for k in order:
                o, key = c("cm", n * k + 16 * k, n * k + n), c("KA", 16 * k + 15, 16 * k + 16)
                if k < ON_A:
                    act(o, c("p0", 16 * k, n), Fn.Sign, bias=key, scale=-1.0, accum=c("rs", k, k + 1))
                else:
                    ts(o, c("p6", 16 * k, n), key, Op.is_lt, 2.0, Op.mult)
                    red(c("rs", k, k + 1), o, Op.add)
                if k < 15:
                    mm(c("p4", 16 * k + 16, n), c("BOh"), c("cm", n * k + 16 * k + 16, n * k + n), False, False)
            for a in (8, 0):
                tt(c("YE", 16 * a, 16 * a + 128), ind(c("rs", a, a + 8), c("EX", 0, 8)), c("D16", 0, 128), Op.mult)
                mm(c("p4", 16 * a, 16 * a + 128), c("BOm"), c("YE", 16 * a, 16 * a + 128), False, a == 0)
            kv = ka = []
        order = []
        for j in range(max(len(kv), len(ka))):
            order += kv[j:j + 1] + ka[j:j + 1]
        for k in order:
            o, key = c("cm", n * k, n * k + n), c("KA", lo + 16 * k + 15, lo + 16 * k + 16)
            if k in kv:
                ts(o, kb_v, key, Op.is_lt, len(ka) / 2 if k == 0 else 0.0, Op.add)
            else:
                act(o, kb_a, Fn.Sign, bias=key, scale=-1.0)
            mm(z, c("BOz" if k in kv else "BOh"), o, False, k == order[-1])
        red(c("pl", 0, 1), z, Op.min, True)
        ts(c("po", 0, 1), c("pl", 0, 1), c("pc", 6, 7), Op.min)

    def stayers(r, lo, hi):
        m = 2 - r
        for k in range(m):
            act(c("zs", 256 * k + lo, 256 * k + hi), c("p4", lo, hi), Fn.Abs, bias=c("pc", 7 + k, 8 + k))
            red(c("pl", 1 + k, 2 + k), c("zs", 256 * k + lo, 256 * k + hi), Op.min)
        ts(c("vo", 0, m), c("pl", 1, 1 + m), 4111.0, Op.min)
        act(c("PS", 32 - 16 * m, 32), ind(Sw, c("vo", 0, m)), Fn.Copy)
        act(c("PB", 32 - 16 * m, 32), ind(Pw, c("vo", 0, m)), Fn.Copy)

    def hash_tail(o, n, bk=None):
        ab, s = c("AB", o, o + 2 * n), c("SS", o, o + 2 * n)
        m = c("MM", o // 2, o // 2 + n)
        ts(ab, ab, 4095, Op.bitwise_and)
        if bk is None:
            tt(m, c("AB", o, o + n), c("AB", o + n, o + 2 * n), Op.mult)
        else:
            ab = c(bk, 0, 2 * n)
            cp(ab, c("AB", o, o + 2 * n))
            tt(m, c(bk, 0, n), c("AB", o + n, o + 2 * n), Op.mult)
        ts(c("SS", o, o + n), m, 5, Op.arith_shift_right)
        ts(c("SS", o + n, o + 2 * n), m, 9, Op.arith_shift_right)
        tt(s, ab, s, Op.add)
        ts(s, s, 4095, Op.bitwise_and)
        m = 2 * n if o == XC else n
        cp(c("HU", o // 2, o // 2 + m), c("SS", o, o + m))

    def wmm(o, k, x):
        return [(o, c("WB", 128 * k, 128 * k + 128), x), (o, c("WB", 128 * k + 256, 128 * k + 384), x)]

    def choose(z, h2, lo, n):
        sl = c("sl", lo, lo + n)
        ts(z, z, 0.0, Op.is_equal)
        tt(sl, z, c("df", lo, lo + n), Op.mult)
        tt(z, h2, sl, Op.add)
        ts(c("SU", lo, lo + n), z, float(NEUTRAL), Op.min)

    def build_vt(now):
        for k, (bk, e, begin, end) in enumerate(BLOCKS):
            vt = c("VT", 512 * k, 512 * k + 512)
            if e == "A" and begin == now:
                mm(c(bk), c("ID"), c("S", 512 * k, 512 * k + 512), True, False)
            if end == now:
                mm(c(bk), c("PK"), c("E", 512 * k, 512 * k + 512), e == "V", True)
                if e == "V":
                    tt(vt, c(bk), c("S", 512 * k, 512 * k + 512), Op.add)
                else:
                    act(vt, c(bk), Fn.Copy)

    def old_vt(par):
        act(c("sp"), ind(Sw, c("po", 0, 1)), Fn.Identity, bias=c("pc", 4, 5))
        cp(ind(Sw, c("po", 0, 1)), c("sp"))
        mms([(c("p2", 0, 16), c("PK"), par), (c("p2", 0, 16), c("ID"), c("sp"))])
        act(c("vp"), c("p2", 0, 16), Fn.Copy)
        cp(ind(Vw, c("po", 0, 1)), c("vp"))

    def decode(bk, buf, lo, n, start):
        o = c(bk, 0, n)
        for k0 in range(0, 16, 4):
            parts = [(c("LK", 128 * k, 128 * k + 128), c(buf, 16 * lo + k, 16 * (lo + n), 16), start and k == 0, k == 15) for k in range(k0, k0 + 4)]
            emit("P", [o], [x for q in parts for x in q[:2]], lambda parts=parts: [g.tensor.matmul(o[0], l[0], x[0], a, b).then_inc(T.sem["P"], 1) for l, x, a, b in parts],
                 (0, 0, 0, 0, 4 * max(64, n)), inc=4, chain=False)

    def round_(r):
        xo = 48 * r
        tag[0] = r
        rp, par, up = c("X", xo, xo + 16), c("X", xo + 16, xo + 32), c("X", xo + 32, xo + 48)
        cp(par, ind(Ew, c("po", 0, 1)))
        trs, tot = [], 0
        for dst, k, sem, land in ((above, 0, "lo", rp), (below, 1, "up", up)):
            if dst is not None:
                es = halves(core, dst, k)
                trs.append(RemoteDMATransfer(dst_ids=[dst_id(dst)], dma_engine_mask=mask_of(es), remote_sem=T.sem[sem + str(r)], src=par[0], dst=land[0]))
                tot += len(es)
        sent = emit("G", [], [par], lambda: g.remote_dma_fused(trs, local_sem=T.sem["ls%d" % r]), (500, 0, 0, 0, 0), sem="ls%d" % r, inc=tot, chain=False)
        if above is not None:
            landed(up, "up%d" % r, len(halves(above, core, 1)), sent, (1, 0 if r else 2000))
        if below is not None:
            landed(rp, "lo%d" % r, len(halves(below, core, 0)), sent, (1, 0 if r else 2000))
        act(c("b8"), par, Fn.Identity, bias=1.0, scale=-8.0)
        if r:
            old_vt(par)
        if r == R - 1:
            dma("Y", c("ee"), c("E", 0, W, rows=row0), 1 << 16)
            dma("Y", c("ec"), c("S", 0, W, rows=row0), 1 << 16)
            ts(c("e1"), c("ec"), 0.0, Op.is_lt, -1.0, Op.mult)
            ts(c("ee"), c("ee"), 0.0, Op.is_ge, 2.0, Op.mult)
            mms([(c("p7", 256, 512), c("ID"), c("ec")), (c("p7", 256, 512), c("In256"), c("e1"))])
            cp(c("fx"), c("p7", 256, 512))
            dma("Y", c("S", 0, W, rows=row0), c("fx"), 1 << 16)
            mms([(c("p7", 256, 512), c("ID"), c("ee")), (c("p7", 256, 512), c("ID"), c("e1"))])
            cp(c("yc"), c("p7", 256, 512))
            dma("Y", c("ST", 0, W, rows=row0), c("yc"), 1 << 17)
        for k, (p0, p1) in enumerate(HC):
            n, o, bk = 16 * (p1 - p0), 32 * p0, ("p0", "p6")[k % 2]
            if k < C_ON_V:
                tt(c("C", 16 * p0, 16 * p1), ind(par, c("EX", p0, p1)), c("D16", 0, n), Op.add)
            else:
                for p in range(p0, p1):
                    act(c("C", 16 * p, 16 * p + 16), c("D16", 0, 16), Fn.Identity, bias=c("X", xo + 16 + p, xo + 17 + p))
            mms(wmm(c(bk, 0, n), 1, c("C", 16 * p0, 16 * p1)))
            mms(wmm(c(bk, n, 2 * n), 0, c("C", 16 * p0, 16 * p1)))
            ts(c("AB", o, o + n), c(bk, 0, n), c("wf", 7, 8), Op.add)
            ts(c("AB", o + n, o + 2 * n), c(bk, n, 2 * n), c("wf", 6, 7), Op.add)
            hash_tail(o, n, bk if k >= PSUM_FROM else None)
        cu, told = c("CU", 256 * r, 256 * r + 240), len(ops) - 1
        if below is not None:
            rid, pid, _ = topo.addr(below)
            told = emit("G", [], [c("C", 0, 240)], lambda: g.remote_dma(cu[0], c("C", 0, 240)[0], T.sem["cu%d" % r], T.sem["lc%d" % r], pid, rid, topo.mask(core, below)),
                        (500, 0, 0, 0, 0), sem="lc%d" % r, inc=len(topo.engines(core, below)), chain=False, after=[sent])
        if above is not None:
            landed(cu, "cu%d" % r, len(topo.engines(above, core)), told, (1, 1000))
        if r == 0:
            ts(c("f2"), c("PB"), 4096.0, Op.is_lt)
            red(c("rm", 1, 2), c("f2"), Op.add)
            ts(c("rm", 1, 2), c("rm", 1, 2), -1.0, Op.mult, 271.0, Op.add)
            ts(c("rm", 0, 1), c("rm", 1, 2), 256.0, Op.min)
        if r < 2:
            stayers(r, 0, (256, 96)[r])
        if r == 0:
            build_vt(1)
            old_vt(par)
        act(c("p5", 0, 240), c("C", 0, 240), Fn.Relu, bias=float(NEUTRAL), scale=-float(NEUTRAL))
        for p0, p1 in HC:
            n, o, h2 = 16 * (p1 - p0), 32 * p0, c("p5", 16 * p0, 16 * p1)
            tt(h2, h2, c("SS", o + n, o + 2 * n), Op.max)
            tt(c("df", 16 * p0, 16 * p1), c("SS", o, o + n), h2, Op.subtract)
        mms([(c("p3", 0, 240), c("PK"), c("N15", 0, 240)), (c("p3", 0, 240), c("PK"), c("C", 0, 240))])

        def fetch(c0, c1, on_v):
            mid = c1 - on_v
            for lo, hi in ((c0, mid), (mid, c1)):
                for a in range(lo, hi, FETCH):
                    b = min(a + FETCH, hi)
                    o = c("G2", 16 * a, 16 * b)
                    if lo == mid:
                        cp(o, ind(Vw, c("SU", a, b)))
                    else:
                        act(o, ind(Vw, c("SU", a, b)), Fn.Copy)
                        follow("A")
                        fetches.append(len(ops) - 1)
                    for x in range(a, b, SCAN):
                        y = min(x + SCAN, b)
                        scan(c("MS", 16 * x, 16 * y), c("RM", 0, 16 * (y - x)), c("G2", 16 * x, 16 * y), 0.0, Op.add, Op.min)
                        follow("V")

        def piece(k):
            p0, p1 = SC[k]
            n, bk, c0 = 16 * (p1 - p0), ("p1", "p2")[k % 2], 16 * p0
            for p in range(p0, p1):
                act(c("FF", 256 * p, 256 * p + 256), ind(Ew, c("HU", 16 * p, 16 * p + 16)), Fn.Square, bias=c("b8", p, p + 1), scale=8.0)
                follow("A")
                tests.append(len(ops) - 1)
            mm(c(bk, 0, n), c("ID"), c("TGh", 0, n), True, False)
            mm(c(bk, 0, n), c("ID"), c("TGl", 0, n), False, False)
            decode(bk, "FF", c0, n, False)

        def resolve(k):
            p0, p1 = SC[k]
            n, bk, c0 = 16 * (p1 - p0), ("p1", "p2")[k % 2], 16 * p0
            choose(c(bk, 0, n), c("p5", c0, c0 + n), c0, n)
            fetch(c0, c0 + n, ON_V[k])

        def extras():
            x3, x2, hu = c("X", xo, xo + 48), c("X", xo, xo + 32), XC // 2
            mms(wmm(c("p7", 0, 48), 1, x3))
            mms(wmm(c("p7", 48, 96), 0, x3))
            for h, k in ((0, 1), (32, 0)):
                mms([(c("p7", 96 + h, 128 + h), c("ID"), c("OD"))] + wmm(c("p7", 96 + h, 128 + h), k, x2))
            for h in (0, 1):
                red(c("p7", 48 * h + 31, 48 * h + 32), c("p7", 96 + 32 * h, 112 + 32 * h), Op.max)
                red(c("p7", 48 * h + 47, 48 * h + 48), c("p7", 112 + 32 * h, 128 + 32 * h), Op.max)
            tt(c("AB", XC, XC + 96), c("p7", 0, 96), c("FX"), Op.add)
            hash_tail(XC, 48)
            act(c("C", 240, 256), rp, Fn.Copy)
            act(c("nx", 0, 16), rp, Fn.Relu, bias=float(NEUTRAL), scale=-float(NEUTRAL))
            h2 = c("p7", 192, 240)
            tt(h2, c("SS", XC + 48, XC + 96), c("nx"), Op.max)
            tt(c("df", 240, 288), c("SS", XC, XC + 48), h2, Op.subtract)
            if above is not None:
                act(c("CU", 256 * r + 240, 256 * r + 256), par, Fn.Copy)
                tt(c("FU", 512, 768), ind(Ew, c("HU", hu + 32, hu + 48)), c("CU", 256 * r, 256 * r + 256), Op.not_equal)
            tt(c("YE"), ind(rp, c("EX")), c("D16"), Op.subtract)
            tt(c("FU", 0, 256), ind(Ew, c("HU", hu, hu + 16)), c("YE"), Op.not_equal)
            decode("p0", "FU", 0, 48, True)
            choose(c("p0", 0, 48), h2, 240, 48)
            if above is not None:
                sv = c("SV", 256 * r, 256 * r + 256)
                mm(c("p1", 256, 512), c("PK"), c("CU", 256 * r, 256 * r + 256), True, True)
                act(c("fu"), c("p1", 256, 512), Fn.Copy)
                tt(sv, ind(Vw, c("SU", 272, 288)), c("fu"), Op.subtract)
                rid, pid, _ = topo.addr(above)
                back = emit("G", [], [sv], lambda: g.remote_dma(T.RP[:, 256 * r:256 * r + 256], sv[0], T.sem["rp%d" % r], T.sem["lr%d" % r], pid, rid, topo.mask(core, above)),
                            (500, 0, 0, 0, 0), sem="lr%d" % r, inc=len(topo.engines(core, above)), chain=False, lat=(1, 1300))
            else:
                back = len(ops) - 1
            if below is not None:
                landed(c("RP", 256 * r, 256 * r + 256), "rp%d" % r, len(topo.engines(below, core)), back, (0 if above is not None else 1, 0))
            fetch(240, 256, ON_V[len(SC)])
            mms([(c("p3", 240, 256), c("PK"), c("N15", 0, 16)), (c("p3", 240, 256), c("PK"), c("C", 240, 256))])
            ts(c("zi"), c("MM", XC // 2 + 16, XC // 2 + 32), 7, Op.arith_shift_right, 2047, Op.bitwise_and)
            cp(c("zu"), c("zi"))
            for h in (0, 1):
                fd, z = c("FO", 256 * h, 256 * h + 256), c("p4", 256 * h, 256 * h + 256)
                act(fd, ind(Ew, c("HU", hu + 48 * h + 16, hu + 48 * h + 32)), Fn.Abs, bias=1.0)
                owns.append(len(ops) - 1)
                mms([(z, c("In1"), c("C", 0, 256)), (z, c("ID"), fd)])
            act(c("FO", 512, 1024), c("p4"), Fn.Square, bias=-1.0)
            owns.append(len(ops) - 1)
            decode("p4", "FO", 0, 64, True)
            sc(c("KO"), c("df", 256, 272), -1 / PEN)
            ts(c("fo", 0, 32), c("p4", 0, 32), 0.0, Op.is_equal, -PEN, Op.mult)
            ts(c("fo", 32, 64), c("p4", 32, 64), 0.0, Op.is_equal, -4 * PEN, Op.mult)
            tt(c("ta"), c("fo", 0, 16), c("KO"), Op.mult)
            tt(c("fm"), c("fo", 0, 48), c("fo", 16, 64), Op.min)
            tt(c("ta"), c("ta"), c("SS", XC + 64, XC + 80), Op.add)
            tt(c("fm", 0, 16), c("fm", 0, 16), c("fm", 32, 48), Op.add)
            tt(c("ta"), c("ta"), c("fm", 0, 16), Op.add)
            ts(c("tu"), c("ta"), PEN + PO, Op.add, float(NONE + PO), Op.min)
            act(c("t256", 0, 256), ind(c("PLC"), c("tu")), Fn.Copy)
            act(c("EVg"), ind(c("ENV"), c("zu")), Fn.Copy)
            return back

        def first(a, b):
            last, pack = c("MS", 16 * a + 15, 16 * b, 16), c("p3", a, b)
            tt(c("M", a, b), last, pack, Op.subtract)
            if a:
                tt(c("NG", a, b), last, pack, Op.is_lt)
            else:
                act(c("NG", a, b), c("M", a, b), Fn.Relu, scale=-1.0)
            if a == 240:
                ts(c("M", a, b), c("M", a, b), 255.0, Op.min)

        def count(a, b):
            z = c("p1" if a else "p6", a, b)
            mms([(z, c("TH", 256, 384), c("ONE", a, b)), (z, c("TH", 384, 512), c("ONE", a, b)), (z, c("BOn"), c("NG", a, b)), (z, c("BOz"), c("M", a, b))])
            tt(c("good", a, b), z, c("t256", a, b), Op.is_ge)
            scan(c("pre", a, b), c("good", a, b), c("good", a, b), c("pre", a - 1, a) if a else 0.0, Op.add, Op.max)

        def lower(a, b):
            m5, d = c("M" if below is None else "M5", a, b), c("p2" if a else "p4", a, b)
            if below is not None:
                z = c("p6" if a else "p7", a, b)
                tt(m5, c("RP", 256 * r + a, 256 * r + b), c("M", a, b), Op.min)
                mms([(z, c("TH", 0, 128), c("ONE", a, b)), (z, c("TH", 128, 256), c("ONE", a, b)), (z, c("BOp"), c("N5", a, b)), (z, c("BO8"), m5)])
                tt(c("tp", a, b), z, c("t256", a, b), Op.max)
            mms([(d, c("In1"), c("EVg", a, b)), (d, c("ID"), m5)])
            act(c("D", a, b), d, Fn.Abs)

        tests, fetches, owns = [], [], []
        piece(0)
        resolve(0)
        back = extras()
        for k in range(1, len(SC)):
            piece(k)
            resolve(k)
        ahead.extend((tests[-1], k) for k in fetches[LEAD:])
        ahead.extend(zip(tests, tests[1:]))
        ahead.extend((k, (tests + fetches)[at]) for k, at in zip(owns, OWN_AT[min(r, 1)]))
        cut = 16 * SC[-1][0]
        for a, b in ((240, 256), (0, cut), (cut, 240)):
            first(a, b)
        count(0, cut)
        count(cut, 256)
        if below is not None:
            act(c("N5"), c("RP", 256 * r, 256 * r + 256), Fn.Relu, scale=-1.0)
        lower(0, cut)
        lower(cut, 256)
        for k in range(4):
            junk = c("junk", 256 * k, 256 * k + 256)
            if k < 2:
                act(junk, c("pre"), Fn.Sign, bias=c("pc", 9 + k, 10 + k), accum=c("acc", k, k + 1))
            else:
                ts(junk, c("pre"), c("pc", 9 + k, 10 + k), Op.is_le)
                scan(junk, junk, junk, 0.0, Op.add, Op.max)
        ts(c("ix", 0, 2), c("acc", 0, 2), -0.5, Op.mult, 128.0, Op.add)
        cp(c("ix", 2, 4), c("junk", 767, 1024, 256))
        tp = c("tp" if below is not None else "t256")
        tt(c("tm"), ind(tp, c("ix")), c("mA"), Op.min)
        act(c("PS", 32, 96), ind(c("D"), c("ix")), Fn.Identity, bias=c("pc", 5, 6) if r < R - 1 else 0.0)
        if r == R - 1:
            tt(c("tB"), ind(tp, c("ix")), c("fr"), Op.add)
            scan(c("tA"), c("RZ", 0, 64), c("tm"), 0.0, Op.mult, Op.max)
            for k in range(4):
                z, own = c("zs", 64 * k, 64 * k + 64), c("tA", 16 * k + 15, 16 * k + 16)
                if k % 2:
                    act(z, c("tB"), Fn.Identity, bias=own, scale=-1.0)
                else:
                    ts(z, c("tB"), own, Op.subtract)
                red(c("acc", k, k + 1), z, Op.min, True)
                ts(c("pl", k, k + 1), c("acc", k, k + 1), c("sf", k, k + 1), Op.not_equal, c("sf", 4 + k, 5 + k), Op.mult)
                ts(c("so", k, k + 1), c("pl", k, k + 1), own, Op.max)
            cp(ind(Sw, c("so")), c("PS", 32, 96))
            cp(ind(c("ST"), c("so")), c("ONE", 0, 64))
            return
        tt(c("tB"), ind(tp, c("ix")), c("tr"), Op.min)
        act(c("Ce"), ind(c("C"), c("ix")), Fn.Copy)
        scan(c("tA"), c("RZ", 0, 64), c("tm"), 0.0, Op.mult, Op.max)
        act(c("iv"), c("tB"), Fn.Relu, bias=-4096 * 2.0 ** 56, scale=2.0 ** 56)
        mm(c("p7", 0, 64), c("ID"), c("nt"), True, False)
        mm(c("p7", 0, 64), c("ID"), c("iv"), False, False)
        for k in range(4):
            ts(c("eq", 64 * k, 64 * k + 64), c("tB"), c("tA", 16 * k + 15, 16 * k + 16), Op.is_equal, 2.0 ** (-1 - 32 * k), Op.mult)
            mm(c("p7", 0, 64), c("LD"), c("eq", 64 * k, 64 * k + 64), False, k == 3)
        dup, tb = c("p3", 0, 64), c("PB", 32, 96)
        ts(c("nb"), c("p7", 0, 64), 0.0, Op.is_ge)
        ts(dup, c("p7", 0, 64), 0.0, Op.is_ge, 4608.0, Op.mult)
        tt(tb, dup, c("tB"), Op.max)
        scan(c("qc"), c("ONE", 0, 64), c("nb"), 0.0, Op.add, Op.subtract)
        ts(c("ov"), c("qc"), c("rm", 0, 1), Op.is_gt)
        keys(r + 1, 16 * r, 96)
        tt(c("tm"), tb, c("mA"), Op.min)
        scan(c("tA"), c("RZ", 0, 64), c("tm"), 0.0, Op.mult, Op.max)
        cp(c("so"), c("tA", 15, 64, 16))
        cp(ind(Sw, c("so")), c("PS", 32, 96))
        cp(ind(Ew, c("so")), c("Ce"))
        if r == 0:
            tt(c("rm", 1, 2), c("rm", 0, 1), c("qc", 63, 64), Op.subtract)
            ts(c("rm", 1, 2), c("rm", 1, 2), 0.0, Op.max, 15.0, Op.add)
            ts(c("rm", 0, 1), c("rm", 1, 2), 256.0, Op.min)
        ranks(r + 1, 16 * r, 96, 2)

    cp(c("PS"), ind(Sw, c("qo")))
    dma("Y", c("S", 0, W, rows=row0), c("fx"), 1 << 16)
    for a, b in zip(CUTS[1:], CUTS[2:]):
        dma("Y", c("E", a, b), T.ex[:, a:b], 256 * (b - a))
    dma("Y", c("ENV"), T.env[:], 1 << 19)
    act(c("PB"), ind(Pw, c("qo")), Fn.Copy)
    keys(0, 0, 256)
    ranks(0, 0, 256, 7)
    build_vt(0)
    for r in range(R):
        round_(r)
    dma("Y", T.ys[:], c("S", 0, W), 1 << 20)
    dma("A", T.yst[:], c("ST", 0, W, rows=row0), 1 << 17)
    issue()
